import numpy as np
import ml_dtypes


def mxq(x, axis, fmt="e4m3"):
    dtype, down = {"e4m3": (ml_dtypes.float8_e4m3fn, 7), "e5m2": (ml_dtypes.float8_e5m2, 14)}[fmt]
    v = np.moveaxis(np.asarray(x, np.float32).astype(ml_dtypes.bfloat16).astype(np.float64), axis, -1)
    blocks = v.reshape(v.shape[:-1] + (-1, 32))
    amax = np.abs(blocks).max(-1, keepdims=True)
    byte = np.maximum(np.where(amax > 0, np.frexp(amax)[1] - 1 + 127, 0) - down, 1)
    scale = np.exp2(byte - 127.0)
    codes = (blocks / scale).astype(np.float32).astype(dtype).astype(np.float64)
    return np.moveaxis((codes * scale).reshape(v.shape), -1, axis)


WIDE = False


def mx_kscale(k):
    if not WIDE:
        return np.ones(k)
    levels = np.array([10, -10, 5, -5, 0])
    if k % 512:
        return np.exp2(np.random.permutation(np.resize(levels, k // 32))).repeat(32)
    a = np.empty((k // 512, 16))
    for p in range(k // 512):
        a[p, :8] = np.random.permutation(np.resize(levels, 8))
        for g in range(8):
            far = levels[np.abs(levels - a[p, g]) >= 10]
            a[p, g + 8] = far[np.random.randint(len(far))]
    return np.exp2(a.ravel()).repeat(32)


def f64(x):
    return np.asarray(x).astype(np.float64)


def striped(idx):
    return np.tile(idx.reshape(-1, 16).T, (8, 1)).astype(np.uint16)


def unstriped(offs):
    return offs[:16].T.reshape(-1).astype(np.int64)


E2M1 = np.array([0.0, 0.5, 1.0, 1.5, 2.0, 3.0, 4.0, 6.0, -0.0, -0.5, -1.0, -1.5, -2.0, -3.0, -4.0, -6.0])


def pack_weight(w, fmt):
    k, n = w.shape
    w = f64(np.asarray(w, np.float32).astype(ml_dtypes.bfloat16)).reshape(k // 32, 32, n)
    amax = np.abs(w).max(1)
    if fmt == "e4m3":
        byte = np.frexp(amax)[1] - 1 + 127 - 7
    else:
        mant, ex = np.frexp(amax / 6.0)
        byte = np.where(mant > 0.5, ex, ex - 1) + 127
    byte = np.clip(np.where(amax > 0, byte, 1), 1, 254)
    scaled = (w * np.exp2(127.0 - byte)[:, None, :]).reshape(k, n).astype(np.float32)
    by_word = np.ascontiguousarray(scaled.reshape(k // 512, 128, 4, n).transpose(0, 1, 3, 2))
    if fmt == "e4m3":
        words = by_word.astype(ml_dtypes.float8_e4m3fn).view(np.uint8)
    else:
        c = by_word.astype(ml_dtypes.float4_e2m1fn).view(np.uint8) & 0xF
        words = (c[..., 0::2] | (c[..., 1::2] << 4)).reshape(k // 512, 128, 2 * n)
    return np.ascontiguousarray(words), np.ascontiguousarray(byte.astype(np.uint8).reshape(k // 512, 16, n))


def unpack_weight(words, scales, fmt):
    g, _, n = scales.shape
    words = np.ascontiguousarray(words).reshape(g, 128, n, -1)
    if fmt == "e4m3":
        vals = words.view(ml_dtypes.float8_e4m3fn).astype(np.float64)
    else:
        nib = np.empty((g, 128, n, 4), np.uint8)
        nib[..., 0::2] = words & 0xF
        nib[..., 1::2] = words >> 4
        vals = E2M1[nib]
    vals = vals * np.repeat(np.exp2(scales.astype(np.float64) - 127.0), 8, axis=1)[..., None]
    return vals.transpose(0, 1, 3, 2).reshape(g * 512, n)


K, T, E1, C1, E2, C2, H = 256, 768, 6, 128, 6, 128, 512
N = 1024


def by_expert(wq, xq, E, C):
    return np.concatenate([wq[e].T @ xq[:, e * C:(e + 1) * C] for e in range(E)], axis=1)


def setup_inputs():
    n = np.random.standard_normal
    v = mx_kscale(N)
    u = mx_kscale(H)
    slots1, slots2 = np.random.permutation(T), np.random.permutation(T)
    dy = pack_weight(n((N, T)) * v[:, None], "e4m3")
    w1t = [pack_weight(m, "e2m1") for m in n((E1, H, K)) / np.sqrt(H) / u[None, :, None]]
    return {
        "dy_words": dy[0],
        "dy_scales": dy[1],
        "w2t": (n((E2, N, H)) / np.sqrt(N) / v[None, :, None] * u).astype(np.float32),
        "w1t_words": np.stack([m[0] for m in w1t]),
        "w1t_scales": np.stack([m[1] for m in w1t]),
        "gate1": (np.tile(np.random.uniform(0.2, 1.0, T), (128, 1))).astype(np.float32),
        "gate2": (np.tile(np.random.uniform(0.2, 1.0, T), (128, 1))).astype(np.float32),
        "offs": striped(slots1),
        "offs2": striped(slots2),
    }


def reference(dy_words, dy_scales, w2t, w1t_words, w1t_scales, gate1, gate2, offs, offs2):
    w2tq = mxq(f64(w2t), 1, "e4m3")
    w1t = np.stack([unpack_weight(w1t_words[e], w1t_scales[e], "e2m1") for e in range(E1)])
    idx, idx2 = unstriped(offs), unstriped(offs2)
    gq = unpack_weight(dy_words, dy_scales, "e4m3")[:, idx2]
    dc = np.zeros((H, T))
    dc[:, idx2] = f64(gate2[:1]) * by_expert(w2tq, gq, E2, C2)
    da = f64(gate1[:1]) * dc[:, idx]
    out = np.zeros((K, T))
    out[:, idx] = by_expert(w1t, mxq(da, 0, "e4m3"), E1, C1)
    return out

@@ -1,0 +1,219 @@
+from contextlib import ExitStack
+
+import concourse.mybir as mybir
+from concourse.masks import make_identity
+
+K, T, E, C, H, N = 256, 768, 6, 128, 512, 1024
+FLOPS = 2 * T * H * (N + K)
+
+F32 = mybir.dt.float32
+BF16 = mybir.dt.bfloat16
+I32 = mybir.dt.int32
+U32 = mybir.dt.uint32
+U16 = mybir.dt.uint16
+U8 = mybir.dt.uint8
+FP8X4 = mybir.dt.float8_e4m3fn_x4
+FP4X4 = mybir.dt.float4_e2m1fn_x4
+COPY = mybir.ActivationFunctionType.Copy
+MULT = mybir.AluOpType.mult
+
+P = 128
+PACK = 4
+PASSES = N // (P * PACK)
+BLOCKS = H // P
+K_BLOCKS = K // P
+PER_COLUMN = 16
+PIECE = 2 * C
+HALF = H // 2
+LAG1 = 1
+LAG2 = 3
+
+
+def entries(offsets, first, count):
+    return offsets[:, first // PER_COLUMN : (first + count) // PER_COLUMN]
+
+
+def tile_moe_seb_none_kernel(
+    tc, dy_words, dy_scales, w2t, w1t_words, w1t_scales, gate1, gate2, offs, offs2, out
+):
+    nc = tc.nc
+    with ExitStack() as ctx:
+        keep = ctx.enter_context(tc.tile_pool(name="keep", bufs=1))
+        ring = ctx.enter_context(tc.tile_pool(name="ring", bufs=6))
+        psum = ctx.enter_context(tc.psum_pool(name="psum", bufs=8))
+
+        list1 = keep.tile([P, T // PER_COLUMN], U16, name="list1")
+        list2 = keep.tile([P, T // PER_COLUMN], U16, name="list2")
+        dy_plane = keep.tile([P, T], U8, name="dy_plane", align_bytes=64)
+        w1_plane = keep.tile([P, E, K], U8, name="w1_plane", align_bytes=64)
+        w1_codes = keep.tile([P, E, 2 * K], U8, name="w1_codes", align_bytes=64)
+        gate1_rows = keep.tile([P, C], F32, name="gate1_rows")
+        gate1_cols = keep.tile([P, E], F32, name="gate1_cols")
+        gate2_sb = keep.tile([P, T], F32, name="gate2_sb")
+        identity = keep.tile([P, P], F32, name="identity")
+        dy_codes = [keep.tile([P, T], I32, name="dy_codes%d" % s, align_bytes=64) for s in range(PASSES)]
+        w2_raw = [[keep.tile([P, PACK, H], F32, name="w2_raw%d_%d" % (f, s)) for s in range(PASSES)] for f in range(E)]
+        dc = [keep.tile([P, T], F32, name="dc%d" % b) for b in range(BLOCKS)]
+        dx = [keep.tile([P, T], F32, name="dx%d" % b) for b in range(K_BLOCKS)]
+
+        nc.vector.memset(dy_plane[:].bitcast(I32), 0)
+        nc.gpsimd.memset(w1_plane[:].rearrange("p e k -> p (e k)").bitcast(I32), 0)
+        nc.gpsimd.memset(gate1_rows[:], 0.0)
+        make_identity(nc, identity[:])
+
+        def load_w2(f, s):
+            rows = w2t[f, s * P * PACK : (s + 1) * P * PACK, :]
+            nc.sync.dma_start(w2_raw[f][s][:], rows.rearrange("(p j) i -> p j i", j=PACK))
+
+        nc.sync.dma_start(list2[:], offs2)
+        for q in range(4):
+            nc.scalar.dma_start(
+                dy_plane[32 * q : 32 * q + 4 * PASSES, :].bitcast(I32),
+                dy_scales[:, 4 * q : 4 * q + 4, :].bitcast(I32),
+            )
+        for s in range(PASSES):
+            nc.sync.dma_start(dy_codes[s][:], dy_words[s].rearrange("p t d -> p (t d)").bitcast(I32))
+            load_w2(0, s)
+        nc.sync.dma_start(gate2_sb[:], gate2)
+        for f in range(1, E):
+            for s in range(PASSES):
+                load_w2(f, s)
+        nc.sync.dma_start(list1[:], offs)
+        nc.sync.dma_start(gate1_rows[0:E, :], gate1[0].rearrange("(e u) -> e u", u=C))
+        nc.sync.dma_start(w1_codes[:].bitcast(I32), w1t_words[:, 0].rearrange("e p b -> p e b").bitcast(I32))
+        for q in range(4):
+            nc.sync.dma_start(
+                w1_plane[32 * q : 32 * q + 4, :, :].bitcast(I32),
+                w1t_scales[:, 0, 4 * q : 4 * q + 4, :].rearrange("e r k -> r e k").bitcast(I32),
+            )
+
+        g_codes, g_plane = [], []
+        for a in range(T // PIECE):
+            picked = entries(list2, a * PIECE, PIECE)
+            words = [keep.tile([P, PIECE], U32, name="g_codes%d_%d" % (a, s), align_bytes=64) for s in range(PASSES)]
+            plane = keep.tile([P, PIECE], U8, name="g_plane%d" % a, align_bytes=64)
+            for s in range(PASSES):
+                nc.vector.tensor_copy(words[s][:], dy_codes[s][:].bitcast(U32).indirect(picked))
+            nc.vector.tensor_copy(plane[:], dy_plane[:].indirect(picked))
+            g_codes.append(words)
+            g_plane.append(plane)
+
+        def second_layer_products(f, half):
+            a, slots = f * C // PIECE, slice(f * C % PIECE, f * C % PIECE + C)
+            w2_codes, w2_planes = [], []
+            for s in range(PASSES):
+                codes = ring.tile([P, HALF], U32, name="w2_codes", align_bytes=64)
+                plane = ring.tile([P, HALF], U8, name="w2_plane", align_bytes=64)
+                if (s, half) == (0, 0):
+                    shares = ((nc.vector.tensor_copy, 0, P), (nc.scalar.copy, P, HALF))
+                else:
+                    shares = ((nc.scalar.copy, 0, HALF),)
+                for engine_copy, c0, c1 in shares:
+                    grouped = ring.tile([P, c1 - c0, PACK], BF16, name="grouped", align_bytes=64)
+                    engine_copy(
+                        grouped[:].rearrange("p (c i) j -> p c j i", i=4),
+                        w2_raw[f][s][:, :, half * HALF + c0 : half * HALF + c1].rearrange("p j (c i) -> p c j i", i=4),
+                    )
+                    nc.vector.quantize_mx(
+                        out=codes[:, c0:c1].bitcast(FP8X4),
+                        scales=plane[:, c0:c1],
+                        in_=grouped[:].rearrange("p i j -> p (i j)"),
+                    )
+                w2_codes.append(codes)
+                w2_planes.append(plane)
+            bank = psum.tile([P, BLOCKS, C], F32, name="bank")
+            for b in range(2):
+                cols = slice(b * P, (b + 1) * P)
+                for s in range(PASSES):
+                    nc.tensor.matmul_mx(
+                        out=bank[:, b, :],
+                        lhsT=w2_codes[s][:, cols].bitcast(FP8X4),
+                        lhsT_scale=w2_planes[s][:, cols],
+                        rhs=g_codes[a][s][:, slots].bitcast(FP8X4),
+                        rhs_scale=g_plane[a][4 * s : P, slots],
+                        start=(s == 0),
+                        stop=(s == PASSES - 1),
+                    )
+            return bank
+
+        def scatter_dc(f, half, bank):
+            sums = ring.tile([P, 2, C], F32, name="sums")
+            nc.scalar.copy(sums[:], bank[:, 0:2, :])
+            for b in range(2):
+                nc.vector.tensor_tensor(
+                    dc[2 * half + b][:].indirect(entries(list2, f * C, C)),
+                    sums[:, b, :],
+                    gate2_sb[:, f * C : (f + 1) * C],
+                    MULT,
+                )
+
+        units = [(f, half) for f in range(E) for half in range(2)]
+        banks = {}
+        for step in range(len(units) + LAG1):
+            if step < len(units):
+                banks[step] = second_layer_products(*units[step])
+            if step >= LAG1:
+                scatter_dc(*units[step - LAG1], banks[step - LAG1])
+
+        bank = psum.tile([P, BLOCKS, C], F32, name="bank")
+        nc.tensor.transpose(bank[:, 0, :], gate1_rows[:], identity[:])
+        nc.scalar.copy(gate1_cols[:], bank[:, 0, 0:E])
+
+        dc_slots = []
+        for a in range(T // PIECE):
+            picked = keep.tile([P, BLOCKS, PIECE], F32, name="dc_slots%d" % a)
+            for b in range(BLOCKS):
+                nc.vector.tensor_copy(picked[:, b, :], dc[b][:].indirect(entries(list1, a * PIECE, PIECE)))
+            dc_slots.append(picked)
+
+        def quantise_da(e):
+            a, slots = e * C // PIECE, slice(e * C % PIECE, e * C % PIECE + C)
+            by_slot = psum.tile([P, BLOCKS, C], F32, name="bank")
+            for b in range(BLOCKS):
+                nc.tensor.transpose(by_slot[:, b, :], dc_slots[a][:, b, slots], identity[:])
+            da_rows = ring.tile([P, 2, P, 2], BF16, name="da_rows")
+            nc.scalar.activation(
+                da_rows[:],
+                by_slot[:].rearrange("u b i -> u (b i)").rearrange("u (p h d) -> u h p d", h=2, d=2),
+                COPY,
+                scale=gate1_cols[:, e : e + 1],
+            )
+            pairs = da_rows[:].rearrange("u h p d -> u (h p d)").bitcast(F32)
+            by_row = psum.tile([P, BLOCKS, C], F32, name="bank")
+            for h in range(2):
+                nc.tensor.transpose(by_row[:, h, :], pairs[:, h * P : (h + 1) * P], identity[:])
+            da = ring.tile([P, C * PACK], BF16, name="da", align_bytes=64)
+            nc.scalar.copy(
+                da[:].bitcast(F32).rearrange("p (u h) -> p u h", h=2), by_row[:, 0:2, :].rearrange("p h u -> p u h")
+            )
+            da_codes = ring.tile([P, C], U32, name="da_codes", align_bytes=64)
+            da_plane = ring.tile([P, C], U8, name="da_plane", align_bytes=64)
+            nc.vector.quantize_mx(out=da_codes[:].bitcast(FP8X4), scales=da_plane[:], in_=da[:])
+            return da_codes, da_plane
+
+        def first_layer_products(e, da_codes, da_plane):
+            bank = psum.tile([P, BLOCKS, C], F32, name="bank")
+            for b in range(K_BLOCKS):
+                nc.tensor.matmul_mx(
+                    out=bank[:, b, :],
+                    lhsT=w1_codes[:, e, 2 * P * b : 2 * P * (b + 1)].bitcast(FP4X4),
+                    lhsT_scale=w1_plane[:, e, P * b : P * (b + 1)],
+                    rhs=da_codes[:].bitcast(FP8X4),
+                    rhs_scale=da_plane[:],
+                    start=True,
+                    stop=True,
+                )
+            results = ring.tile([P, K_BLOCKS, C], F32, name="results")
+            nc.scalar.copy(results[:], bank[:, 0:K_BLOCKS, :])
+            for b in range(K_BLOCKS):
+                nc.vector.tensor_copy(dx[b][:].indirect(entries(list1, e * C, C)), results[:, b, :])
+
+        da_mx = {}
+        for step in range(E + LAG2):
+            if step < E:
+                da_mx[step] = quantise_da(step)
+            if step >= LAG2:
+                first_layer_products(step - LAG2, *da_mx[step - LAG2])
+
+        for b in range(K_BLOCKS):
+            nc.sync.dma_start(out[b * P : (b + 1) * P, :], dx[b][:])

@@ -23,14 +23,27 @@ PASSES = N // (P * PACK)
 BLOCKS = H // P
 K_BLOCKS = K // P
 PER_COLUMN = 16
-PIECE = 2 * C
 HALF = H // 2
-LAG1 = 1
-LAG2 = 3
+GATE2_EARLY = 2 * C
+HALVED = 6
+LAG1 = 2
+LAG2 = 1
+DY_PIECES = (256, 512)
+DC_PIECES = (128, 128, 256, 256)
+DX_GROUP = 1
+VECTOR_CASTS = ((2, 1, 0), (4, 1, 0))
 
 
 def entries(offsets, first, count):
     return offsets[:, first // PER_COLUMN : (first + count) // PER_COLUMN]
+
+
+def piece_of(pieces, expert):
+    first = 0
+    for a, width in enumerate(pieces):
+        if expert * C < first + width:
+            return a, slice(expert * C - first, (expert + 1) * C - first)
+        first = first + width
 
 
 def tile_moe_seb_none_kernel(
@@ -49,35 +62,54 @@ def tile_moe_seb_none_kernel(
         w1_codes = keep.tile([P, E, 2 * K], U8, name="w1_codes", align_bytes=64)
         gate1_rows = keep.tile([P, C], F32, name="gate1_rows")
         gate1_cols = keep.tile([P, E], F32, name="gate1_cols")
-        gate2_sb = keep.tile([P, T], F32, name="gate2_sb")
+        gate2_sb = [
+            keep.tile([P, width], F32, name="gate2_sb%d" % a) for a, width in enumerate((GATE2_EARLY, T - GATE2_EARLY))
+        ]
         identity = keep.tile([P, P], F32, name="identity")
         dy_codes = [keep.tile([P, T], I32, name="dy_codes%d" % s, align_bytes=64) for s in range(PASSES)]
-        w2_raw = [[keep.tile([P, PACK, H], F32, name="w2_raw%d_%d" % (f, s)) for s in range(PASSES)] for f in range(E)]
         dc = [keep.tile([P, T], F32, name="dc%d" % b) for b in range(BLOCKS)]
         dx = [keep.tile([P, T], F32, name="dx%d" % b) for b in range(K_BLOCKS)]
 
-        nc.vector.memset(dy_plane[:].bitcast(I32), 0)
+        nc.gpsimd.memset(dy_plane[:].bitcast(I32), 0)
         nc.gpsimd.memset(w1_plane[:].rearrange("p e k -> p (e k)").bitcast(I32), 0)
         nc.gpsimd.memset(gate1_rows[:], 0.0)
         make_identity(nc, identity[:])
 
-        def load_w2(f, s):
-            rows = w2t[f, s * P * PACK : (s + 1) * P * PACK, :]
-            nc.sync.dma_start(w2_raw[f][s][:], rows.rearrange("(p j) i -> p j i", j=PACK))
+        w2_raw = {}
+
+        def load_w2(f, s, c0, c1):
+            raw = keep.tile([P, PACK, c1 - c0], F32, name="w2_raw%d_%d_%d" % (f, s, c0))
+            rows = w2t[f, s * P * PACK : (s + 1) * P * PACK, c0:c1]
+            nc.sync.dma_start(raw[:], rows.rearrange("(p j) i -> p j i", j=PACK))
+            for half in range(c0 // HALF, c1 // HALF):
+                w2_raw[f, s, half] = raw[:, :, half * HALF - c0 : (half + 1) * HALF - c0]
+
+        def load_dy(s):
+            nc.sync.dma_start(dy_codes[s][:], dy_words[s].rearrange("p t d -> p (t d)").bitcast(I32))
 
         nc.sync.dma_start(list2[:], offs2)
+        load_dy(0)
+        load_w2(0, 0, 0, HALF)
         for q in range(4):
-            nc.scalar.dma_start(
+            nc.sync.dma_start(
                 dy_plane[32 * q : 32 * q + 4 * PASSES, :].bitcast(I32),
                 dy_scales[:, 4 * q : 4 * q + 4, :].bitcast(I32),
             )
-        for s in range(PASSES):
-            nc.sync.dma_start(dy_codes[s][:], dy_words[s].rearrange("p t d -> p (t d)").bitcast(I32))
-            load_w2(0, s)
-        nc.sync.dma_start(gate2_sb[:], gate2)
+        load_w2(0, 1, 0, HALF)
+        load_dy(1)
+        load_w2(0, 0, HALF, H)
+        load_w2(0, 1, HALF, H)
+        nc.sync.dma_start(gate2_sb[0][:], gate2[:, :GATE2_EARLY])
         for f in range(1, E):
-            for s in range(PASSES):
-                load_w2(f, s)
+            if f < HALVED:
+                for half in range(2):
+                    for s in range(PASSES):
+                        load_w2(f, s, half * HALF, (half + 1) * HALF)
+            else:
+                for s in range(PASSES):
+                    load_w2(f, s, 0, H)
+            if f == 1:
+                nc.sync.dma_start(gate2_sb[1][:], gate2[:, GATE2_EARLY:])
         nc.sync.dma_start(list1[:], offs)
         nc.sync.dma_start(gate1_rows[0:E, :], gate1[0].rearrange("(e u) -> e u", u=C))
         nc.sync.dma_start(w1_codes[:].bitcast(I32), w1t_words[:, 0].rearrange("e p b -> p e b").bitcast(I32))
@@ -88,86 +120,94 @@ def tile_moe_seb_none_kernel(
             )
 
         g_codes, g_plane = [], []
-        for a in range(T // PIECE):
-            picked = entries(list2, a * PIECE, PIECE)
-            words = [keep.tile([P, PIECE], U32, name="g_codes%d_%d" % (a, s), align_bytes=64) for s in range(PASSES)]
-            plane = keep.tile([P, PIECE], U8, name="g_plane%d" % a, align_bytes=64)
-            for s in range(PASSES):
-                nc.vector.tensor_copy(words[s][:], dy_codes[s][:].bitcast(U32).indirect(picked))
+        for a, width in enumerate(DY_PIECES):
+            picked = entries(list2, sum(DY_PIECES[:a]), width)
+            words = [keep.tile([P, width], U32, name="g_codes%d_%d" % (a, s), align_bytes=64) for s in range(PASSES)]
+            plane = keep.tile([P, width], U8, name="g_plane%d" % a, align_bytes=64)
+            nc.vector.tensor_copy(words[0][:], dy_codes[0][:].bitcast(U32).indirect(picked))
             nc.vector.tensor_copy(plane[:], dy_plane[:].indirect(picked))
+            nc.vector.tensor_copy(words[1][:], dy_codes[1][:].bitcast(U32).indirect(picked))
             g_codes.append(words)
             g_plane.append(plane)
 
-        def second_layer_products(f, half):
-            a, slots = f * C // PIECE, slice(f * C % PIECE, f * C % PIECE + C)
-            w2_codes, w2_planes = [], []
+        def second_layer_products(f, half, sums_bank):
+            a, slots = piece_of(DY_PIECES, f)
+            grouped = ring.tile([P, PASSES, HALF * PACK], BF16, name="grouped", align_bytes=64)
             for s in range(PASSES):
-                codes = ring.tile([P, HALF], U32, name="w2_codes", align_bytes=64)
-                plane = ring.tile([P, HALF], U8, name="w2_plane", align_bytes=64)
-                if (s, half) == (0, 0):
-                    shares = ((nc.vector.tensor_copy, 0, P), (nc.scalar.copy, P, HALF))
-                else:
-                    shares = ((nc.scalar.copy, 0, HALF),)
-                for engine_copy, c0, c1 in shares:
-                    grouped = ring.tile([P, c1 - c0, PACK], BF16, name="grouped", align_bytes=64)
-                    engine_copy(
-                        grouped[:].rearrange("p (c i) j -> p c j i", i=4),
-                        w2_raw[f][s][:, :, half * HALF + c0 : half * HALF + c1].rearrange("p j (c i) -> p c j i", i=4),
-                    )
-                    nc.vector.quantize_mx(
-                        out=codes[:, c0:c1].bitcast(FP8X4),
-                        scales=plane[:, c0:c1],
-                        in_=grouped[:].rearrange("p i j -> p (i j)"),
-                    )
-                w2_codes.append(codes)
-                w2_planes.append(plane)
-            bank = psum.tile([P, BLOCKS, C], F32, name="bank")
+                engine_copy = nc.vector.tensor_copy if (f, s, half) in VECTOR_CASTS else nc.scalar.copy
+                engine_copy(
+                    grouped[:, s, :].rearrange("p (c i j) -> p c j i", i=4, j=PACK),
+                    w2_raw[f, s, half].rearrange("p j (c i) -> p c j i", i=4),
+                )
+            codes = ring.tile([P, PASSES, HALF], U32, name="w2_codes", align_bytes=64)
+            plane = ring.tile([P, PASSES, HALF], U8, name="w2_plane", align_bytes=64)
+            nc.vector.quantize_mx(
+                out=codes[:].rearrange("p s i -> p (s i)").bitcast(FP8X4),
+                scales=plane[:].rearrange("p s i -> p (s i)"),
+                in_=grouped[:].rearrange("p s x -> p (s x)"),
+            )
             for b in range(2):
                 cols = slice(b * P, (b + 1) * P)
                 for s in range(PASSES):
                     nc.tensor.matmul_mx(
-                        out=bank[:, b, :],
-                        lhsT=w2_codes[s][:, cols].bitcast(FP8X4),
-                        lhsT_scale=w2_planes[s][:, cols],
+                        out=sums_bank[:, b, :],
+                        lhsT=codes[:, s, cols].bitcast(FP8X4),
+                        lhsT_scale=plane[:, s, cols],
                         rhs=g_codes[a][s][:, slots].bitcast(FP8X4),
                         rhs_scale=g_plane[a][4 * s : P, slots],
                         start=(s == 0),
                         stop=(s == PASSES - 1),
                     )
-            return bank
 
-        def scatter_dc(f, half, bank):
-            sums = ring.tile([P, 2, C], F32, name="sums")
-            nc.scalar.copy(sums[:], bank[:, 0:2, :])
-            for b in range(2):
+        def scatter_dc(f, blocks, sums_bank):
+            later = min(2 * f + blocks[-1] // 2 + LAG1, 2 * E - 1)
+            if 2 * f + blocks[-1] // 2 + LAG1 < 2 * E and True:
+                sums = keep.tile([P, len(blocks), C], F32, name="w2_raw%d_0_%d" % (later // 2, later % 2 * HALF))
+            else:
+                sums = ring.tile([P, len(blocks), C], F32, name="sums")
+            nc.scalar.copy(sums[:], sums_bank)
+            a, slots = piece_of((GATE2_EARLY, T - GATE2_EARLY), f)
+            for n, b in enumerate(blocks):
                 nc.vector.tensor_tensor(
-                    dc[2 * half + b][:].indirect(entries(list2, f * C, C)),
-                    sums[:, b, :],
-                    gate2_sb[:, f * C : (f + 1) * C],
-                    MULT,
+                    dc[b][:].indirect(entries(list2, f * C, C)), sums[:, n, :], gate2_sb[a][:, slots], MULT
                 )
 
         units = [(f, half) for f in range(E) for half in range(2)]
         banks = {}
         for step in range(len(units) + LAG1):
             if step < len(units):
-                banks[step] = second_layer_products(*units[step])
+                f, half = units[step]
+                if (f, half) == (E - 1, 1):
+                    banks[step] = banks[step - 1]
+                    second_layer_products(f, half, banks[step][:, 2:4, :])
+                else:
+                    banks[step] = psum.tile([P, BLOCKS, C], F32, name="bank")
+                    second_layer_products(f, half, banks[step][:, 0:2, :])
             if step >= LAG1:
-                scatter_dc(*units[step - LAG1], banks[step - LAG1])
+                f, half = units[step - LAG1]
+                if f < E - 1:
+                    scatter_dc(f, (2 * half, 2 * half + 1), banks[step - LAG1][:, 0:2, :])
+                elif half == 1:
+                    scatter_dc(f, (0, 1, 2, 3), banks[step - LAG1][:])
 
         bank = psum.tile([P, BLOCKS, C], F32, name="bank")
         nc.tensor.transpose(bank[:, 0, :], gate1_rows[:], identity[:])
         nc.scalar.copy(gate1_cols[:], bank[:, 0, 0:E])
 
         dc_slots = []
-        for a in range(T // PIECE):
-            picked = keep.tile([P, BLOCKS, PIECE], F32, name="dc_slots%d" % a)
+
+        def gather_dc(a):
+            width = DC_PIECES[a]
+            picked = keep.tile([P, BLOCKS, width], F32, name="dc_slots%d" % a, align_bytes=64)
             for b in range(BLOCKS):
-                nc.vector.tensor_copy(picked[:, b, :], dc[b][:].indirect(entries(list1, a * PIECE, PIECE)))
+                nc.vector.tensor_copy(picked[:, b, :], dc[b][:].indirect(entries(list1, sum(DC_PIECES[:a]), width)))
             dc_slots.append(picked)
 
+        for a in range(len(DC_PIECES) - 1):
+            gather_dc(a)
+
         def quantise_da(e):
-            a, slots = e * C // PIECE, slice(e * C % PIECE, e * C % PIECE + C)
+            a, slots = piece_of(DC_PIECES, e)
             by_slot = psum.tile([P, BLOCKS, C], F32, name="bank")
             for b in range(BLOCKS):
                 nc.tensor.transpose(by_slot[:, b, :], dc_slots[a][:, b, slots], identity[:])
@@ -182,7 +222,10 @@ def tile_moe_seb_none_kernel(
             by_row = psum.tile([P, BLOCKS, C], F32, name="bank")
             for h in range(2):
                 nc.tensor.transpose(by_row[:, h, :], pairs[:, h * P : (h + 1) * P], identity[:])
-            da = ring.tile([P, C * PACK], BF16, name="da", align_bytes=64)
+            if e == 0:
+                da = keep.tile([P, C * PACK], BF16, name="dc_slots%d" % (len(DC_PIECES) - 1), align_bytes=64)
+            else:
+                da = ring.tile([P, C * PACK], BF16, name="da", align_bytes=64)
             nc.scalar.copy(
                 da[:].bitcast(F32).rearrange("p (u h) -> p u h", h=2), by_row[:, 0:2, :].rearrange("p h u -> p u h")
             )
@@ -190,6 +233,8 @@ def tile_moe_seb_none_kernel(
             da_plane = ring.tile([P, C], U8, name="da_plane", align_bytes=64)
             nc.vector.quantize_mx(out=da_codes[:].bitcast(FP8X4), scales=da_plane[:], in_=da[:])
             return da_codes, da_plane
+
+        results = [keep.tile([P, K_BLOCKS, DX_GROUP * C], F32, name="results%d" % a) for a in range(E // DX_GROUP)]
 
         def first_layer_products(e, da_codes, da_plane):
             bank = psum.tile([P, BLOCKS, C], F32, name="bank")
@@ -203,15 +248,20 @@ def tile_moe_seb_none_kernel(
                     start=True,
                     stop=True,
                 )
-            results = ring.tile([P, K_BLOCKS, C], F32, name="results")
-            nc.scalar.copy(results[:], bank[:, 0:K_BLOCKS, :])
-            for b in range(K_BLOCKS):
-                nc.vector.tensor_copy(dx[b][:].indirect(entries(list1, e * C, C)), results[:, b, :])
+            a, place = divmod(e, DX_GROUP)
+            nc.scalar.copy(results[a][:, :, place * C : (place + 1) * C], bank[:, 0:K_BLOCKS, :])
+            if place == DX_GROUP - 1:
+                for b in range(K_BLOCKS):
+                    nc.vector.tensor_copy(
+                        dx[b][:].indirect(entries(list1, a * DX_GROUP * C, DX_GROUP * C)), results[a][:, b, :]
+                    )
 
         da_mx = {}
         for step in range(E + LAG2):
             if step < E:
                 da_mx[step] = quantise_da(step)
+            if step == 0:
+                gather_dc(len(DC_PIECES) - 1)
             if step >= LAG2:
                 first_layer_products(step - LAG2, *da_mx[step - LAG2])
 

@@ -24,26 +24,19 @@ BLOCKS = H // P
 K_BLOCKS = K // P
 PER_COLUMN = 16
 HALF = H // 2
-GATE2_EARLY = 2 * C
-HALVED = 6
-LAG1 = 2
-LAG2 = 1
-DY_PIECES = (256, 512)
-DC_PIECES = (128, 128, 256, 256)
-DX_GROUP = 1
-VECTOR_CASTS = ((2, 1, 0), (4, 1, 0))
+UNITS = 2 * E
+PIECES = UNITS * PASSES
+PIECE_BYTES = PACK * HALF * 4
+KIB = 1024
+EARLY = 2 * C
+SUMS_LAG = 3
+VECTOR_CASTS = (4, 8)
+GATE_LOADS = (2, 6, 10)
+LOW_GATHERS = (15, 17, 19, 21)
 
 
 def entries(offsets, first, count):
     return offsets[:, first // PER_COLUMN : (first + count) // PER_COLUMN]
-
-
-def piece_of(pieces, expert):
-    first = 0
-    for a, width in enumerate(pieces):
-        if expert * C < first + width:
-            return a, slice(expert * C - first, (expert + 1) * C - first)
-        first = first + width
 
 
 def tile_moe_seb_none_kernel(
@@ -52,8 +45,13 @@ def tile_moe_seb_none_kernel(
     nc = tc.nc
     with ExitStack() as ctx:
         keep = ctx.enter_context(tc.tile_pool(name="keep", bufs=1))
-        ring = ctx.enter_context(tc.tile_pool(name="ring", bufs=6))
-        psum = ctx.enter_context(tc.psum_pool(name="psum", bufs=8))
+        raws = ctx.enter_context(tc.tile_pool(name="raws", bufs=1))
+        late = ctx.enter_context(tc.tile_pool(name="late", bufs=1))
+        ring = ctx.enter_context(tc.tile_pool(name="ring", bufs=4))
+        psum = ctx.enter_context(tc.psum_pool(name="psum", bufs=1))
+
+        def on_piece(piece, at, shape, dtype, name):
+            return raws.tile(shape, dtype, name=name, align_bytes=64, offset=piece * PIECE_BYTES + at)
 
         list1 = keep.tile([P, T // PER_COLUMN], U16, name="list1")
         list2 = keep.tile([P, T // PER_COLUMN], U16, name="list2")
@@ -62,9 +60,7 @@ def tile_moe_seb_none_kernel(
         w1_codes = keep.tile([P, E, 2 * K], U8, name="w1_codes", align_bytes=64)
         gate1_rows = keep.tile([P, C], F32, name="gate1_rows")
         gate1_cols = keep.tile([P, E], F32, name="gate1_cols")
-        gate2_sb = [
-            keep.tile([P, width], F32, name="gate2_sb%d" % a) for a, width in enumerate((GATE2_EARLY, T - GATE2_EARLY))
-        ]
+        gate2_sb = [keep.tile([P, EARLY], F32, name="gate2_sb%d" % a) for a in range(T // EARLY)]
         identity = keep.tile([P, P], F32, name="identity")
         dy_codes = [keep.tile([P, T], I32, name="dy_codes%d" % s, align_bytes=64) for s in range(PASSES)]
         dc = [keep.tile([P, T], F32, name="dc%d" % b) for b in range(BLOCKS)]
@@ -75,42 +71,36 @@ def tile_moe_seb_none_kernel(
         nc.gpsimd.memset(gate1_rows[:], 0.0)
         make_identity(nc, identity[:])
 
-        w2_raw = {}
+        w2_raw = []
 
-        def load_w2(f, s, c0, c1):
-            raw = keep.tile([P, PACK, c1 - c0], F32, name="w2_raw%d_%d_%d" % (f, s, c0))
-            rows = w2t[f, s * P * PACK : (s + 1) * P * PACK, c0:c1]
+        def load_w2(piece):
+            unit, s = divmod(piece, PASSES)
+            half, f = divmod(unit, E)
+            raw = on_piece(piece, 0, [P, PACK, HALF], F32, "w2_raw%d" % piece)
+            rows = w2t[f, s * P * PACK : (s + 1) * P * PACK, half * HALF : (half + 1) * HALF]
             nc.sync.dma_start(raw[:], rows.rearrange("(p j) i -> p j i", j=PACK))
-            for half in range(c0 // HALF, c1 // HALF):
-                w2_raw[f, s, half] = raw[:, :, half * HALF - c0 : (half + 1) * HALF - c0]
+            w2_raw.append(raw)
 
         def load_dy(s):
             nc.sync.dma_start(dy_codes[s][:], dy_words[s].rearrange("p t d -> p (t d)").bitcast(I32))
 
         nc.sync.dma_start(list2[:], offs2)
         load_dy(0)
-        load_w2(0, 0, 0, HALF)
         for q in range(4):
             nc.sync.dma_start(
                 dy_plane[32 * q : 32 * q + 4 * PASSES, :].bitcast(I32),
                 dy_scales[:, 4 * q : 4 * q + 4, :].bitcast(I32),
             )
-        load_w2(0, 1, 0, HALF)
+        load_w2(0)
+        load_w2(1)
         load_dy(1)
-        load_w2(0, 0, HALF, H)
-        load_w2(0, 1, HALF, H)
-        nc.sync.dma_start(gate2_sb[0][:], gate2[:, :GATE2_EARLY])
-        for f in range(1, E):
-            if f < HALVED:
-                for half in range(2):
-                    for s in range(PASSES):
-                        load_w2(f, s, half * HALF, (half + 1) * HALF)
-            else:
-                for s in range(PASSES):
-                    load_w2(f, s, 0, H)
-            if f == 1:
-                nc.sync.dma_start(gate2_sb[1][:], gate2[:, GATE2_EARLY:])
-        nc.sync.dma_start(list1[:], offs)
+        for piece in range(2, PIECES):
+            load_w2(piece)
+            if piece in GATE_LOADS:
+                a = GATE_LOADS.index(piece)
+                nc.sync.dma_start(gate2_sb[a][:], gate2[:, a * EARLY : (a + 1) * EARLY])
+            if piece == 10:
+                nc.sync.dma_start(list1[:], offs)
         nc.sync.dma_start(gate1_rows[0:E, :], gate1[0].rearrange("(e u) -> e u", u=C))
         nc.sync.dma_start(w1_codes[:].bitcast(I32), w1t_words[:, 0].rearrange("e p b -> p e b").bitcast(I32))
         for q in range(4):
@@ -119,38 +109,55 @@ def tile_moe_seb_none_kernel(
                 w1t_scales[:, 0, 4 * q : 4 * q + 4, :].rearrange("e r k -> r e k").bitcast(I32),
             )
 
-        g_codes, g_plane = [], []
-        for a, width in enumerate(DY_PIECES):
-            picked = entries(list2, sum(DY_PIECES[:a]), width)
-            words = [keep.tile([P, width], U32, name="g_codes%d_%d" % (a, s), align_bytes=64) for s in range(PASSES)]
-            plane = keep.tile([P, width], U8, name="g_plane%d" % a, align_bytes=64)
-            nc.vector.tensor_copy(words[0][:], dy_codes[0][:].bitcast(U32).indirect(picked))
-            nc.vector.tensor_copy(plane[:], dy_plane[:].indirect(picked))
-            nc.vector.tensor_copy(words[1][:], dy_codes[1][:].bitcast(U32).indirect(picked))
-            g_codes.append(words)
+        widths = (EARLY, T - EARLY)
+        picked = [entries(list2, 0, EARLY), entries(list2, EARLY, T - EARLY)]
+        g_codes = [[None, None], [None, None]]
+        g_plane = []
+        for a in range(2):
+            g_codes[a][0] = keep.tile([P, widths[a]], U32, name="g_codes%d_0" % a, align_bytes=64)
+            nc.vector.tensor_copy(g_codes[a][0][:], dy_codes[0][:].bitcast(U32).indirect(picked[a]))
+        for a in range(2):
+            plane = keep.tile([P, widths[a]], U8, name="g_plane%d" % a, align_bytes=64)
+            nc.vector.tensor_copy(plane[:], dy_plane[:].indirect(picked[a]))
             g_plane.append(plane)
+        g_codes[0][1] = keep.tile([P, EARLY], U32, name="g_codes0_1", align_bytes=64)
+        nc.vector.tensor_copy(g_codes[0][1][:], dy_codes[1][:].bitcast(U32).indirect(picked[0]))
 
-        def second_layer_products(f, half, sums_bank):
-            a, slots = piece_of(DY_PIECES, f)
-            grouped = ring.tile([P, PASSES, HALF * PACK], BF16, name="grouped", align_bytes=64)
-            for s in range(PASSES):
-                engine_copy = nc.vector.tensor_copy if (f, s, half) in VECTOR_CASTS else nc.scalar.copy
-                engine_copy(
-                    grouped[:, s, :].rearrange("p (c i j) -> p c j i", i=4, j=PACK),
-                    w2_raw[f, s, half].rearrange("p j (c i) -> p c j i", i=4),
-                )
+        def two_part(f):
+            if f * C < EARLY:
+                return 0, slice(f * C, (f + 1) * C)
+            return 1, slice(f * C - EARLY, (f + 1) * C - EARLY)
+
+        grouped, banks = {}, {}
+
+        def cast(piece):
+            unit, s = divmod(piece, PASSES)
+            if s == 0:
+                grouped[unit] = ring.tile([P, PASSES, HALF * PACK], BF16, name="grouped", align_bytes=64)
+            engine_copy = nc.vector.tensor_copy if piece in VECTOR_CASTS else nc.scalar.copy
+            engine_copy(
+                grouped[unit][:, s, :].rearrange("p (c i j) -> p c j i", i=4, j=PACK),
+                w2_raw[piece][:].rearrange("p j (c i) -> p c j i", i=4),
+            )
+
+        def products(unit):
+            a, slots = two_part(unit % E)
             codes = ring.tile([P, PASSES, HALF], U32, name="w2_codes", align_bytes=64)
             plane = ring.tile([P, PASSES, HALF], U8, name="w2_plane", align_bytes=64)
             nc.vector.quantize_mx(
                 out=codes[:].rearrange("p s i -> p (s i)").bitcast(FP8X4),
                 scales=plane[:].rearrange("p s i -> p (s i)"),
-                in_=grouped[:].rearrange("p s x -> p (s x)"),
+                in_=grouped[unit][:].rearrange("p s x -> p (s x)"),
             )
+            if unit == 0:
+                g_codes[1][1] = on_piece(1, 0, [P, T - EARLY], U32, "g_codes1_1")
+                nc.vector.tensor_copy(g_codes[1][1][:], dy_codes[1][:].bitcast(U32).indirect(picked[1]))
+            banks[unit] = psum.tile([P, BLOCKS, C], F32, name="sums_bank", bufs=3)
             for b in range(2):
                 cols = slice(b * P, (b + 1) * P)
                 for s in range(PASSES):
                     nc.tensor.matmul_mx(
-                        out=sums_bank[:, b, :],
+                        out=banks[unit][:, b, :],
                         lhsT=codes[:, s, cols].bitcast(FP8X4),
                         lhsT_scale=plane[:, s, cols],
                         rhs=g_codes[a][s][:, slots].bitcast(FP8X4),
@@ -159,59 +166,67 @@ def tile_moe_seb_none_kernel(
                         stop=(s == PASSES - 1),
                     )
 
-        def scatter_dc(f, blocks, sums_bank):
-            later = min(2 * f + blocks[-1] // 2 + LAG1, 2 * E - 1)
-            if 2 * f + blocks[-1] // 2 + LAG1 < 2 * E and True:
-                sums = keep.tile([P, len(blocks), C], F32, name="w2_raw%d_0_%d" % (later // 2, later % 2 * HALF))
+        LATE_AT = 0
+
+        def scatter_dc(unit, piece):
+            half, f = divmod(unit, E)
+            if unit == UNITS - 1:
+                sums = late.tile([P, 2, C], F32, name="last_sums", align_bytes=64, offset=LATE_AT)
+            elif unit == 0:
+                sums = keep.tile([P, 2, C], F32, name="first_sums")
             else:
-                sums = ring.tile([P, len(blocks), C], F32, name="sums")
-            nc.scalar.copy(sums[:], sums_bank)
-            a, slots = piece_of((GATE2_EARLY, T - GATE2_EARLY), f)
-            for n, b in enumerate(blocks):
+                sums = on_piece(piece, 0, [P, 2, C], F32, "sums%d" % unit)
+            nc.scalar.copy(sums[:], banks[unit][:, 0:2, :])
+            a, slots = f // 2, slice(f % 2 * C, (f % 2 + 1) * C)
+            for n in range(2):
                 nc.vector.tensor_tensor(
-                    dc[b][:].indirect(entries(list2, f * C, C)), sums[:, n, :], gate2_sb[a][:, slots], MULT
+                    dc[2 * half + n][:].indirect(entries(list2, f * C, C)), sums[:, n, :], gate2_sb[a][:, slots], MULT
                 )
 
-        units = [(f, half) for f in range(E) for half in range(2)]
-        banks = {}
-        for step in range(len(units) + LAG1):
-            if step < len(units):
-                f, half = units[step]
-                if (f, half) == (E - 1, 1):
-                    banks[step] = banks[step - 1]
-                    second_layer_products(f, half, banks[step][:, 2:4, :])
-                else:
-                    banks[step] = psum.tile([P, BLOCKS, C], F32, name="bank")
-                    second_layer_products(f, half, banks[step][:, 0:2, :])
-            if step >= LAG1:
-                f, half = units[step - LAG1]
-                if f < E - 1:
-                    scatter_dc(f, (2 * half, 2 * half + 1), banks[step - LAG1][:, 0:2, :])
-                elif half == 1:
-                    scatter_dc(f, (0, 1, 2, 3), banks[step - LAG1][:])
+        dc_slots = {}
 
-        bank = psum.tile([P, BLOCKS, C], F32, name="bank")
+        def gather_dc(target, b, first, count):
+            nc.vector.tensor_copy(target, dc[b][:].indirect(entries(list1, first * C, count * C)))
+            for n in range(count):
+                dc_slots[first + n, b] = target[:, n * C : (n + 1) * C]
+
+        copy_at = {}
+        for unit in range(UNITS):
+            copy_at[2 if unit == 0 else PASSES * unit + SUMS_LAG] = unit
+        for piece in range(PIECES + SUMS_LAG):
+            if piece < PIECES:
+                cast(piece)
+                if piece % PASSES == PASSES - 1:
+                    products(piece // PASSES)
+            if piece in copy_at:
+                scatter_dc(copy_at[piece], min(piece, PIECES - 1))
+            if piece in LOW_GATHERS:
+                pair, b = divmod(LOW_GATHERS.index(piece), 2)
+                target = on_piece(piece, KIB, [P, 2 * C], F32, "low_slots%d" % piece)
+                gather_dc(target[:], b, 2 * pair, 2)
+
+        bank = psum.tile([P, BLOCKS, C], F32, name="by_row", bufs=2)
         nc.tensor.transpose(bank[:, 0, :], gate1_rows[:], identity[:])
         nc.scalar.copy(gate1_cols[:], bank[:, 0, 0:E])
 
-        dc_slots = []
+        first_high = keep.tile([P, 2 * C], F32, name="first_high")
+        for n in range(2):
+            gather_dc(first_high[:, n * C : (n + 1) * C], 2 + n, 0, 1)
+        behind = late.tile([P, 10 * C], F32, name="behind", align_bytes=64, offset=LATE_AT)
+        for n in range(2):
+            gather_dc(behind[:, n * C : (n + 1) * C], 2 + n, 1, 1)
+        for n in range(2):
+            gather_dc(behind[:, (2 + 2 * n) * C : (4 + 2 * n) * C], 2 + n, 2, 2)
+        for n in range(2):
+            gather_dc(behind[:, (6 + 2 * n) * C : (8 + 2 * n) * C], n, 4, 2)
 
-        def gather_dc(a):
-            width = DC_PIECES[a]
-            picked = keep.tile([P, BLOCKS, width], F32, name="dc_slots%d" % a, align_bytes=64)
-            for b in range(BLOCKS):
-                nc.vector.tensor_copy(picked[:, b, :], dc[b][:].indirect(entries(list1, sum(DC_PIECES[:a]), width)))
-            dc_slots.append(picked)
-
-        for a in range(len(DC_PIECES) - 1):
-            gather_dc(a)
+        ROWS_STEP = 3 * KIB // 2
 
         def quantise_da(e):
-            a, slots = piece_of(DC_PIECES, e)
-            by_slot = psum.tile([P, BLOCKS, C], F32, name="bank")
+            by_slot = psum.tile([P, BLOCKS, C], F32, name="by_slot", bufs=2)
             for b in range(BLOCKS):
-                nc.tensor.transpose(by_slot[:, b, :], dc_slots[a][:, b, slots], identity[:])
-            da_rows = ring.tile([P, 2, P, 2], BF16, name="da_rows")
+                nc.tensor.transpose(by_slot[:, b, :], dc_slots[e, b], identity[:])
+            da_rows = late.tile([P, 2, P, 2], BF16, name="da_rows%d" % e, align_bytes=64, offset=5 * KIB + e * ROWS_STEP)
             nc.scalar.activation(
                 da_rows[:],
                 by_slot[:].rearrange("u b i -> u (b i)").rearrange("u (p h d) -> u h p d", h=2, d=2),
@@ -219,13 +234,10 @@ def tile_moe_seb_none_kernel(
                 scale=gate1_cols[:, e : e + 1],
             )
             pairs = da_rows[:].rearrange("u h p d -> u (h p d)").bitcast(F32)
-            by_row = psum.tile([P, BLOCKS, C], F32, name="bank")
+            by_row = psum.tile([P, BLOCKS, C], F32, name="by_row", bufs=2)
             for h in range(2):
                 nc.tensor.transpose(by_row[:, h, :], pairs[:, h * P : (h + 1) * P], identity[:])
-            if e == 0:
-                da = keep.tile([P, C * PACK], BF16, name="dc_slots%d" % (len(DC_PIECES) - 1), align_bytes=64)
-            else:
-                da = ring.tile([P, C * PACK], BF16, name="da", align_bytes=64)
+            da = ring.tile([P, C * PACK], BF16, name="da", align_bytes=64)
             nc.scalar.copy(
                 da[:].bitcast(F32).rearrange("p (u h) -> p u h", h=2), by_row[:, 0:2, :].rearrange("p h u -> p u h")
             )
@@ -234,10 +246,8 @@ def tile_moe_seb_none_kernel(
             nc.vector.quantize_mx(out=da_codes[:].bitcast(FP8X4), scales=da_plane[:], in_=da[:])
             return da_codes, da_plane
 
-        results = [keep.tile([P, K_BLOCKS, DX_GROUP * C], F32, name="results%d" % a) for a in range(E // DX_GROUP)]
-
         def first_layer_products(e, da_codes, da_plane):
-            bank = psum.tile([P, BLOCKS, C], F32, name="bank")
+            bank = psum.tile([P, BLOCKS, C], F32, name="sums_bank", bufs=3)
             for b in range(K_BLOCKS):
                 nc.tensor.matmul_mx(
                     out=bank[:, b, :],
@@ -248,22 +258,23 @@ def tile_moe_seb_none_kernel(
                     start=True,
                     stop=True,
                 )
-            a, place = divmod(e, DX_GROUP)
-            nc.scalar.copy(results[a][:, :, place * C : (place + 1) * C], bank[:, 0:K_BLOCKS, :])
-            if place == DX_GROUP - 1:
-                for b in range(K_BLOCKS):
-                    nc.vector.tensor_copy(
-                        dx[b][:].indirect(entries(list1, a * DX_GROUP * C, DX_GROUP * C)), results[a][:, b, :]
-                    )
+            results = late.tile(
+                [P, K_BLOCKS, C], F32, name="results%d" % e, align_bytes=64, offset=5 * KIB + (e + 1) * ROWS_STEP + KIB // 2
+            )
+            nc.scalar.copy(results[:], bank[:, 0:K_BLOCKS, :])
+            for b in range(K_BLOCKS):
+                nc.vector.tensor_copy(dx[b][:].indirect(entries(list1, e * C, C)), results[:, b, :])
 
         da_mx = {}
-        for step in range(E + LAG2):
+        for step in range(E + 1):
             if step < E:
                 da_mx[step] = quantise_da(step)
-            if step == 0:
-                gather_dc(len(DC_PIECES) - 1)
-            if step >= LAG2:
-                first_layer_products(step - LAG2, *da_mx[step - LAG2])
+            if step == 1:
+                last_high = late.tile([P, 4 * C], F32, name="last_high", align_bytes=64, offset=5 * KIB)
+                for n in range(2):
+                    gather_dc(last_high[:, 2 * n * C : (2 + 2 * n) * C], 2 + n, 4, 2)
+            if step >= 1:
+                first_layer_products(step - 1, *da_mx[step - 1])
 
         for b in range(K_BLOCKS):
             nc.sync.dma_start(out[b * P : (b + 1) * P, :], dx[b][:])

@@ -29,10 +29,35 @@ PIECES = UNITS * PASSES
 PIECE_BYTES = PACK * HALF * 4
 KIB = 1024
 EARLY = 2 * C
-SUMS_LAG = 3
-VECTOR_CASTS = (4, 8)
-GATE_LOADS = (2, 6, 10)
-LOW_GATHERS = (15, 17, 19, 21)
+SPLIT = (0, 4, 5)
+VECTOR_CASTS = (7, 11)
+GATE_LOADS = (2, 4, 6)
+LOW_GATHERS = (21, 21, 23, 23)
+WHOLE_LAG = 4
+SPLIT_LAG = 3
+
+
+def plan():
+    whole = [f for f in range(E) if f not in SPLIT]
+    units, loads, casts = [], [], []
+
+    def add_half(f, half):
+        units.append((f, half))
+        for s in range(PASSES):
+            loads.append((f, s, half * HALF, (half + 1) * HALF))
+            casts.append((f, s, half))
+
+    add_half(SPLIT[0], 0)
+    for f in whole:
+        units.extend([(f, 0), (f, 1)])
+        for s in range(PASSES):
+            loads.append((f, s, 0, H))
+            casts.extend([(f, s, 0), (f, s, 1)])
+    for f in SPLIT[1:]:
+        add_half(f, 0)
+    for f in SPLIT:
+        add_half(f, 1)
+    return units, loads, casts
 
 
 def entries(offsets, first, count):
@@ -71,15 +96,17 @@ def tile_moe_seb_none_kernel(
         nc.gpsimd.memset(gate1_rows[:], 0.0)
         make_identity(nc, identity[:])
 
-        w2_raw = []
+        units, loads, casts = plan()
+        w2_raw = {}
 
-        def load_w2(piece):
-            unit, s = divmod(piece, PASSES)
-            half, f = divmod(unit, E)
-            raw = on_piece(piece, 0, [P, PACK, HALF], F32, "w2_raw%d" % piece)
-            rows = w2t[f, s * P * PACK : (s + 1) * P * PACK, half * HALF : (half + 1) * HALF]
+        def load_w2(n):
+            f, s, c0, c1 = loads[n]
+            at = sum(PACK * 4 * (load[3] - load[2]) for load in loads[:n])
+            raw = raws.tile([P, PACK, c1 - c0], F32, name="w2_raw%d" % n, align_bytes=64, offset=at)
+            rows = w2t[f, s * P * PACK : (s + 1) * P * PACK, c0:c1]
             nc.sync.dma_start(raw[:], rows.rearrange("(p j) i -> p j i", j=PACK))
-            w2_raw.append(raw)
+            for half in range(c0 // HALF, c1 // HALF):
+                w2_raw[f, s, half] = raw[:, :, half * HALF - c0 : (half + 1) * HALF - c0]
 
         def load_dy(s):
             nc.sync.dma_start(dy_codes[s][:], dy_words[s].rearrange("p t d -> p (t d)").bitcast(I32))
@@ -94,12 +121,12 @@ def tile_moe_seb_none_kernel(
         load_w2(0)
         load_w2(1)
         load_dy(1)
-        for piece in range(2, PIECES):
+        for piece in range(2, len(loads)):
             load_w2(piece)
             if piece in GATE_LOADS:
                 a = GATE_LOADS.index(piece)
                 nc.sync.dma_start(gate2_sb[a][:], gate2[:, a * EARLY : (a + 1) * EARLY])
-            if piece == 10:
+            if piece == GATE_LOADS[-1]:
                 nc.sync.dma_start(list1[:], offs)
         nc.sync.dma_start(gate1_rows[0:E, :], gate1[0].rearrange("(e u) -> e u", u=C))
         nc.sync.dma_start(w1_codes[:].bitcast(I32), w1t_words[:, 0].rearrange("e p b -> p e b").bitcast(I32))
@@ -131,17 +158,18 @@ def tile_moe_seb_none_kernel(
         grouped, banks = {}, {}
 
         def cast(piece):
-            unit, s = divmod(piece, PASSES)
+            f, s, half = casts[piece]
+            unit = units.index((f, half))
             if s == 0:
                 grouped[unit] = ring.tile([P, PASSES, HALF * PACK], BF16, name="grouped", align_bytes=64)
             engine_copy = nc.vector.tensor_copy if piece in VECTOR_CASTS else nc.scalar.copy
             engine_copy(
                 grouped[unit][:, s, :].rearrange("p (c i j) -> p c j i", i=4, j=PACK),
-                w2_raw[piece][:].rearrange("p j (c i) -> p c j i", i=4),
+                w2_raw[casts[piece]].rearrange("p j (c i) -> p c j i", i=4),
             )
 
         def products(unit):
-            a, slots = two_part(unit % E)
+            a, slots = two_part(units[unit][0])
             codes = ring.tile([P, PASSES, HALF], U32, name="w2_codes", align_bytes=64)
             plane = ring.tile([P, PASSES, HALF], U8, name="w2_plane", align_bytes=64)
             nc.vector.quantize_mx(
@@ -169,14 +197,14 @@ def tile_moe_seb_none_kernel(
         LATE_AT = 0
 
         def scatter_dc(unit, piece):
-            half, f = divmod(unit, E)
+            f, half = units[unit]
             if unit == UNITS - 1:
-                sums = late.tile([P, 2, C], F32, name="last_sums", align_bytes=64, offset=LATE_AT)
+                sums = late.tile([P, 2, C], F32, name="last_sums", align_bytes=64, offset=LATE_AT)[:]
             elif unit == 0:
-                sums = keep.tile([P, 2, C], F32, name="first_sums")
+                sums = keep.tile([P, 2, C], F32, name="first_sums")[:]
             else:
-                sums = on_piece(piece, 0, [P, 2, C], F32, "sums%d" % unit)
-            nc.scalar.copy(sums[:], banks[unit][:, 0:2, :])
+                sums = w2_raw[casts[piece]][:, 0, :].rearrange("p (b u) -> p b u", b=2)
+            nc.scalar.copy(sums, banks[unit][:, 0:2, :])
             a, slots = f // 2, slice(f % 2 * C, (f % 2 + 1) * C)
             for n in range(2):
                 nc.vector.tensor_tensor(
@@ -191,19 +219,19 @@ def tile_moe_seb_none_kernel(
                 dc_slots[first + n, b] = target[:, n * C : (n + 1) * C]
 
         copy_at = {}
-        for unit in range(UNITS):
-            copy_at[2 if unit == 0 else PASSES * unit + SUMS_LAG] = unit
-        for piece in range(PIECES + SUMS_LAG):
+        for unit, (f, half) in enumerate(units):
+            copy_at[2 if unit == 0 else PASSES * unit + (SPLIT_LAG if f in SPLIT else WHOLE_LAG)] = unit
+        for piece in range(max(copy_at) + 1):
             if piece < PIECES:
                 cast(piece)
-                if piece % PASSES == PASSES - 1:
-                    products(piece // PASSES)
+                f, s, half = casts[piece]
+                if s == PASSES - 1:
+                    products(units.index((f, half)))
             if piece in copy_at:
                 scatter_dc(copy_at[piece], min(piece, PIECES - 1))
-            if piece in LOW_GATHERS:
-                pair, b = divmod(LOW_GATHERS.index(piece), 2)
-                target = on_piece(piece, KIB, [P, 2 * C], F32, "low_slots%d" % piece)
-                gather_dc(target[:], b, 2 * pair, 2)
+            for n, at in enumerate(LOW_GATHERS):
+                if at == piece:
+                    gather_dc(w2_raw[casts[piece]][:, 1 + n % 2, :], n % 2, 2 * (n // 2), 2)
 
         bank = psum.tile([P, BLOCKS, C], F32, name="by_row", bufs=2)
         nc.tensor.transpose(bank[:, 0, :], gate1_rows[:], identity[:])

@@ -29,35 +29,7 @@ PIECES = UNITS * PASSES
 PIECE_BYTES = PACK * HALF * 4
 KIB = 1024
 EARLY = 2 * C
-SPLIT = (0, 4, 5)
-VECTOR_CASTS = (7, 11)
-GATE_LOADS = (2, 4, 6)
-LOW_GATHERS = (21, 21, 23, 23)
-WHOLE_LAG = 4
-SPLIT_LAG = 3
-
-
-def plan():
-    whole = [f for f in range(E) if f not in SPLIT]
-    units, loads, casts = [], [], []
-
-    def add_half(f, half):
-        units.append((f, half))
-        for s in range(PASSES):
-            loads.append((f, s, half * HALF, (half + 1) * HALF))
-            casts.append((f, s, half))
-
-    add_half(SPLIT[0], 0)
-    for f in whole:
-        units.extend([(f, 0), (f, 1)])
-        for s in range(PASSES):
-            loads.append((f, s, 0, H))
-            casts.extend([(f, s, 0), (f, s, 1)])
-    for f in SPLIT[1:]:
-        add_half(f, 0)
-    for f in SPLIT:
-        add_half(f, 1)
-    return units, loads, casts
+VECTOR_COLUMNS = 96
 
 
 def entries(offsets, first, count):
@@ -75,66 +47,73 @@ def tile_moe_seb_none_kernel(
         ring = ctx.enter_context(tc.tile_pool(name="ring", bufs=4))
         psum = ctx.enter_context(tc.psum_pool(name="psum", bufs=1))
 
-        def on_piece(piece, at, shape, dtype, name):
-            return raws.tile(shape, dtype, name=name, align_bytes=64, offset=piece * PIECE_BYTES + at)
-
         list1 = keep.tile([P, T // PER_COLUMN], U16, name="list1")
         list2 = keep.tile([P, T // PER_COLUMN], U16, name="list2")
         dy_plane = keep.tile([P, T], U8, name="dy_plane", align_bytes=64)
         w1_plane = keep.tile([P, E, K], U8, name="w1_plane", align_bytes=64)
         w1_codes = keep.tile([P, E, 2 * K], U8, name="w1_codes", align_bytes=64)
-        gate1_rows = keep.tile([P, C], F32, name="gate1_rows")
-        gate1_cols = keep.tile([P, E], F32, name="gate1_cols")
-        gate2_sb = [keep.tile([P, EARLY], F32, name="gate2_sb%d" % a) for a in range(T // EARLY)]
+        gate_rows = [keep.tile([P, C], F32, name="gate_rows%d" % a) for a in range(2)]
+        gate_cols = [keep.tile([P, E], F32, name="gate_cols%d" % a) for a in range(2)]
         identity = keep.tile([P, P], F32, name="identity")
         dy_codes = [keep.tile([P, T], I32, name="dy_codes%d" % s, align_bytes=64) for s in range(PASSES)]
         dc = [keep.tile([P, T], F32, name="dc%d" % b) for b in range(BLOCKS)]
         dx = [keep.tile([P, T], F32, name="dx%d" % b) for b in range(K_BLOCKS)]
 
         nc.gpsimd.memset(dy_plane[:].bitcast(I32), 0)
-        nc.gpsimd.memset(w1_plane[:].rearrange("p e k -> p (e k)").bitcast(I32), 0)
-        nc.gpsimd.memset(gate1_rows[:], 0.0)
+        nc.gpsimd.memset(gate_rows[1][:], 0.0)
         make_identity(nc, identity[:])
+        nc.gpsimd.memset(gate_rows[0][:], 0.0)
+        nc.gpsimd.memset(w1_plane[:].rearrange("p e k -> p (e k)").bitcast(I32), 0)
 
-        units, loads, casts = plan()
         w2_raw = {}
 
-        def load_w2(n):
-            f, s, c0, c1 = loads[n]
-            at = sum(PACK * 4 * (load[3] - load[2]) for load in loads[:n])
-            raw = raws.tile([P, PACK, c1 - c0], F32, name="w2_raw%d" % n, align_bytes=64, offset=at)
-            rows = w2t[f, s * P * PACK : (s + 1) * P * PACK, c0:c1]
+        def load_w2(f, s):
+            at = (PASSES * f + s) * 2 * PIECE_BYTES
+            raw = raws.tile([P, PACK, H], F32, name="w2_raw%d_%d" % (f, s), align_bytes=64, offset=at)
+            rows = w2t[f, s * P * PACK : (s + 1) * P * PACK, :]
             nc.sync.dma_start(raw[:], rows.rearrange("(p j) i -> p j i", j=PACK))
-            for half in range(c0 // HALF, c1 // HALF):
-                w2_raw[f, s, half] = raw[:, :, half * HALF - c0 : (half + 1) * HALF - c0]
+            for half in range(2):
+                w2_raw[4 * f + 2 * s + half] = raw[:, :, half * HALF : (half + 1) * HALF]
 
         def load_dy(s):
             nc.sync.dma_start(dy_codes[s][:], dy_words[s].rearrange("p t d -> p (t d)").bitcast(I32))
 
         nc.sync.dma_start(list2[:], offs2)
         load_dy(0)
+        load_w2(0, 0)
         for q in range(4):
             nc.sync.dma_start(
                 dy_plane[32 * q : 32 * q + 4 * PASSES, :].bitcast(I32),
                 dy_scales[:, 4 * q : 4 * q + 4, :].bitcast(I32),
             )
-        load_w2(0)
-        load_w2(1)
+        nc.scalar.dma_start(gate_rows[1][0:E, :], gate2[0].rearrange("(e u) -> e u", u=C))
+        load_w2(0, 1)
         load_dy(1)
-        for piece in range(2, len(loads)):
-            load_w2(piece)
-            if piece in GATE_LOADS:
-                a = GATE_LOADS.index(piece)
-                nc.sync.dma_start(gate2_sb[a][:], gate2[:, a * EARLY : (a + 1) * EARLY])
-            if piece == GATE_LOADS[-1]:
-                nc.sync.dma_start(list1[:], offs)
-        nc.sync.dma_start(gate1_rows[0:E, :], gate1[0].rearrange("(e u) -> e u", u=C))
+        for f in range(1, E):
+            for s in range(PASSES):
+                load_w2(f, s)
+        nc.sync.dma_start(list1[:], offs)
+        nc.sync.dma_start(gate_rows[0][0:E, :], gate1[0].rearrange("(e u) -> e u", u=C))
         nc.sync.dma_start(w1_codes[:].bitcast(I32), w1t_words[:, 0].rearrange("e p b -> p e b").bitcast(I32))
         for q in range(4):
             nc.sync.dma_start(
                 w1_plane[32 * q : 32 * q + 4, :, :].bitcast(I32),
                 w1t_scales[:, 0, 4 * q : 4 * q + 4, :].rearrange("e r k -> r e k").bitcast(I32),
             )
+
+        def turn_gate(a):
+            bank = psum.tile([P, BLOCKS, C], F32, name="by_row", bufs=2)
+            nc.tensor.transpose(bank[:, 0, :], gate_rows[a][:], identity[:])
+            nc.scalar.copy(gate_cols[a][:], bank[:, 0, 0:E])
+
+        turn_gate(1)
+        gate2_banks = []
+        for first in range(0, E, E // 2):
+            bank = psum.tile([P, BLOCKS, C], F32, name="by_slot", bufs=2)
+            for n in range(E // 2):
+                column = gate_cols[1][:, first + n : first + n + 1]
+                nc.tensor.transpose(bank[:, n, :], column.to_broadcast([P, P]), identity[:])
+            gate2_banks.append(bank)
 
         widths = (EARLY, T - EARLY)
         picked = [entries(list2, 0, EARLY), entries(list2, EARLY, T - EARLY)]
@@ -158,18 +137,20 @@ def tile_moe_seb_none_kernel(
         grouped, banks = {}, {}
 
         def cast(piece):
-            f, s, half = casts[piece]
-            unit = units.index((f, half))
+            f, s, half = piece // 4, piece // 2 % 2, piece % 2
+            unit = 2 * f + half
             if s == 0:
                 grouped[unit] = ring.tile([P, PASSES, HALF * PACK], BF16, name="grouped", align_bytes=64)
-            engine_copy = nc.vector.tensor_copy if piece in VECTOR_CASTS else nc.scalar.copy
-            engine_copy(
-                grouped[unit][:, s, :].rearrange("p (c i j) -> p c j i", i=4, j=PACK),
-                w2_raw[casts[piece]].rearrange("p j (c i) -> p c j i", i=4),
-            )
+            cut = HALF - VECTOR_COLUMNS if piece % 4 == 1 and f > 0 else HALF
+            for engine_copy, c0, c1 in ((nc.scalar.copy, 0, cut), (nc.vector.tensor_copy, cut, HALF)):
+                if c0 < c1:
+                    engine_copy(
+                        grouped[unit][:, s, c0 * PACK : c1 * PACK].rearrange("p (c i j) -> p c j i", i=4, j=PACK),
+                        w2_raw[piece][:, :, c0:c1].rearrange("p j (c i) -> p c j i", i=4),
+                    )
 
         def products(unit):
-            a, slots = two_part(units[unit][0])
+            a, slots = two_part(unit // 2)
             codes = ring.tile([P, PASSES, HALF], U32, name="w2_codes", align_bytes=64)
             plane = ring.tile([P, PASSES, HALF], U8, name="w2_plane", align_bytes=64)
             nc.vector.quantize_mx(
@@ -177,9 +158,6 @@ def tile_moe_seb_none_kernel(
                 scales=plane[:].rearrange("p s i -> p (s i)"),
                 in_=grouped[unit][:].rearrange("p s x -> p (s x)"),
             )
-            if unit == 0:
-                g_codes[1][1] = on_piece(1, 0, [P, T - EARLY], U32, "g_codes1_1")
-                nc.vector.tensor_copy(g_codes[1][1][:], dy_codes[1][:].bitcast(U32).indirect(picked[1]))
             banks[unit] = psum.tile([P, BLOCKS, C], F32, name="sums_bank", bufs=3)
             for b in range(2):
                 cols = slice(b * P, (b + 1) * P)
@@ -197,18 +175,17 @@ def tile_moe_seb_none_kernel(
         LATE_AT = 0
 
         def scatter_dc(unit, piece):
-            f, half = units[unit]
+            f, half = divmod(unit, 2)
             if unit == UNITS - 1:
                 sums = late.tile([P, 2, C], F32, name="last_sums", align_bytes=64, offset=LATE_AT)[:]
-            elif unit == 0:
-                sums = keep.tile([P, 2, C], F32, name="first_sums")[:]
+            elif unit in (0, UNITS - 2):
+                sums = keep.tile([P, 2, C], F32, name="sums%d" % unit)[:]
             else:
-                sums = w2_raw[casts[piece]][:, 0, :].rearrange("p (b u) -> p b u", b=2)
+                sums = w2_raw[piece][:, 0, :].rearrange("p (b u) -> p b u", b=2)
             nc.scalar.copy(sums, banks[unit][:, 0:2, :])
-            a, slots = f // 2, slice(f % 2 * C, (f % 2 + 1) * C)
             for n in range(2):
                 nc.vector.tensor_tensor(
-                    dc[2 * half + n][:].indirect(entries(list2, f * C, C)), sums[:, n, :], gate2_sb[a][:, slots], MULT
+                    dc[2 * half + n][:].indirect(entries(list2, f * C, C)), sums[:, n, :], gate2_sb[:, f, :], MULT
                 )
 
         dc_slots = {}
@@ -218,35 +195,34 @@ def tile_moe_seb_none_kernel(
             for n in range(count):
                 dc_slots[first + n, b] = target[:, n * C : (n + 1) * C]
 
-        copy_at = {}
-        for unit, (f, half) in enumerate(units):
-            copy_at[2 if unit == 0 else PASSES * unit + (SPLIT_LAG if f in SPLIT else WHOLE_LAG)] = unit
-        for piece in range(max(copy_at) + 1):
+        for piece in range(PIECES + 4):
             if piece < PIECES:
                 cast(piece)
-                f, s, half = casts[piece]
-                if s == PASSES - 1:
-                    products(units.index((f, half)))
-            if piece in copy_at:
-                scatter_dc(copy_at[piece], min(piece, PIECES - 1))
-            for n, at in enumerate(LOW_GATHERS):
-                if at == piece:
-                    gather_dc(w2_raw[casts[piece]][:, 1 + n % 2, :], n % 2, 2 * (n // 2), 2)
+                if piece == 3:
+                    gate2_sb = raws.tile([P, E, C], F32, name="gate2_sb", align_bytes=64, offset=2 * PIECE_BYTES)
+                    g_codes[1][1] = raws.tile([P, T - EARLY], U32, name="g_codes1_1", align_bytes=64, offset=3 * PIECE_BYTES)
+                    nc.vector.tensor_copy(g_codes[1][1][:], dy_codes[1][:].bitcast(U32).indirect(picked[1]))
+                if piece % 4 >= 2:
+                    products(piece // 4 * 2 + piece % 2)
+            if piece == 3:
+                for a, bank in enumerate(gate2_banks):
+                    nc.scalar.copy(gate2_sb[:, a * E // 2 : (a + 1) * E // 2, :], bank[:, 0 : E // 2, :])
+                scatter_dc(0, piece)
+            if piece >= 7 and piece % 2 == 1:
+                scatter_dc(piece // 2 - 2, piece - 1)
+            if piece == PIECES + 1:
+                first_slots = keep.tile([P, BLOCKS * C], F32, name="first_slots")
+                for b in range(2):
+                    gather_dc(first_slots[:, b * C : (b + 1) * C], b, 0, 1)
 
-        bank = psum.tile([P, BLOCKS, C], F32, name="by_row", bufs=2)
-        nc.tensor.transpose(bank[:, 0, :], gate1_rows[:], identity[:])
-        nc.scalar.copy(gate1_cols[:], bank[:, 0, 0:E])
-
-        first_high = keep.tile([P, 2 * C], F32, name="first_high")
-        for n in range(2):
-            gather_dc(first_high[:, n * C : (n + 1) * C], 2 + n, 0, 1)
-        behind = late.tile([P, 10 * C], F32, name="behind", align_bytes=64, offset=LATE_AT)
-        for n in range(2):
-            gather_dc(behind[:, n * C : (n + 1) * C], 2 + n, 1, 1)
-        for n in range(2):
-            gather_dc(behind[:, (2 + 2 * n) * C : (4 + 2 * n) * C], 2 + n, 2, 2)
-        for n in range(2):
-            gather_dc(behind[:, (6 + 2 * n) * C : (8 + 2 * n) * C], n, 4, 2)
+        turn_gate(0)
+        for b in range(2, BLOCKS):
+            gather_dc(first_slots[:, b * C : (b + 1) * C], b, 0, 1)
+        behind = late.tile([P, 3 * BLOCKS * C], F32, name="behind", align_bytes=64, offset=LATE_AT)
+        for b in range(BLOCKS):
+            gather_dc(behind[:, b * C : (b + 1) * C], b, 1, 1)
+        for b in range(BLOCKS):
+            gather_dc(behind[:, (BLOCKS + 2 * b) * C : (BLOCKS + 2 * b + 2) * C], b, 2, 2)
 
         ROWS_STEP = 3 * KIB // 2
 
@@ -254,12 +230,12 @@ def tile_moe_seb_none_kernel(
             by_slot = psum.tile([P, BLOCKS, C], F32, name="by_slot", bufs=2)
             for b in range(BLOCKS):
                 nc.tensor.transpose(by_slot[:, b, :], dc_slots[e, b], identity[:])
-            da_rows = late.tile([P, 2, P, 2], BF16, name="da_rows%d" % e, align_bytes=64, offset=5 * KIB + e * ROWS_STEP)
+            da_rows = late.tile([P, 2, P, 2], BF16, name="da_rows%d" % e, align_bytes=64, offset=8 * KIB + e * ROWS_STEP)
             nc.scalar.activation(
                 da_rows[:],
                 by_slot[:].rearrange("u b i -> u (b i)").rearrange("u (p h d) -> u h p d", h=2, d=2),
                 COPY,
-                scale=gate1_cols[:, e : e + 1],
+                scale=gate_cols[0][:, e : e + 1],
             )
             pairs = da_rows[:].rearrange("u h p d -> u (h p d)").bitcast(F32)
             by_row = psum.tile([P, BLOCKS, C], F32, name="by_row", bufs=2)
@@ -287,7 +263,7 @@ def tile_moe_seb_none_kernel(
                     stop=True,
                 )
             results = late.tile(
-                [P, K_BLOCKS, C], F32, name="results%d" % e, align_bytes=64, offset=5 * KIB + (e + 1) * ROWS_STEP + KIB // 2
+                [P, K_BLOCKS, C], F32, name="results%d" % e, align_bytes=64, offset=8 * KIB + (e + 1) * ROWS_STEP + KIB // 2
             )
             nc.scalar.copy(results[:], bank[:, 0:K_BLOCKS, :])
             for b in range(K_BLOCKS):
@@ -298,9 +274,9 @@ def tile_moe_seb_none_kernel(
             if step < E:
                 da_mx[step] = quantise_da(step)
             if step == 1:
-                last_high = late.tile([P, 4 * C], F32, name="last_high", align_bytes=64, offset=5 * KIB)
-                for n in range(2):
-                    gather_dc(last_high[:, 2 * n * C : (2 + 2 * n) * C], 2 + n, 4, 2)
+                last_slots = late.tile([P, 2 * BLOCKS * C], F32, name="last_slots", align_bytes=64, offset=6 * KIB)
+                for b in range(BLOCKS):
+                    gather_dc(last_slots[:, 2 * b * C : (2 * b + 2) * C], b, 4, 2)
             if step >= 1:
                 first_layer_products(step - 1, *da_mx[step - 1])
 

@@ -30,6 +30,16 @@ PIECE_BYTES = PACK * HALF * 4
 KIB = 1024
 EARLY = 2 * C
 VECTOR_COLUMNS = 96
+WHOLE = 4
+EARLY_PAIRS = 1
+
+
+def plan():
+    loads = [(f, s, (0, 1)) for f in range(WHOLE) for s in range(PASSES)]
+    for half in range(2):
+        loads.extend([(f, s, (half,)) for f in range(WHOLE, E) for s in range(PASSES)])
+    units = [(f, half) for f, s, halves in loads for half in halves if s == PASSES - 1]
+    return loads, units
 
 
 def entries(offsets, first, count):
@@ -65,34 +75,36 @@ def tile_moe_seb_none_kernel(
         nc.gpsimd.memset(gate_rows[0][:], 0.0)
         nc.gpsimd.memset(w1_plane[:].rearrange("p e k -> p (e k)").bitcast(I32), 0)
 
+        loads, units = plan()
         w2_raw = {}
 
-        def load_w2(f, s):
-            at = (PASSES * f + s) * 2 * PIECE_BYTES
-            raw = raws.tile([P, PACK, H], F32, name="w2_raw%d_%d" % (f, s), align_bytes=64, offset=at)
-            rows = w2t[f, s * P * PACK : (s + 1) * P * PACK, :]
+        def load_w2(n):
+            f, s, halves = loads[n]
+            at = PIECE_BYTES * sum(len(load[2]) for load in loads[:n])
+            raw = raws.tile([P, PACK, len(halves) * HALF], F32, name="w2_raw%d" % n, align_bytes=64, offset=at)
+            rows = w2t[f, s * P * PACK : (s + 1) * P * PACK, halves[0] * HALF : (halves[-1] + 1) * HALF]
             nc.sync.dma_start(raw[:], rows.rearrange("(p j) i -> p j i", j=PACK))
-            for half in range(2):
-                w2_raw[4 * f + 2 * s + half] = raw[:, :, half * HALF : (half + 1) * HALF]
+            for a, half in enumerate(halves):
+                w2_raw[f, s, half] = raw[:, :, a * HALF : (a + 1) * HALF]
 
         def load_dy(s):
             nc.sync.dma_start(dy_codes[s][:], dy_words[s].rearrange("p t d -> p (t d)").bitcast(I32))
 
         nc.sync.dma_start(list2[:], offs2)
         load_dy(0)
-        load_w2(0, 0)
+        load_w2(0)
         for q in range(4):
             nc.sync.dma_start(
                 dy_plane[32 * q : 32 * q + 4 * PASSES, :].bitcast(I32),
                 dy_scales[:, 4 * q : 4 * q + 4, :].bitcast(I32),
             )
         nc.scalar.dma_start(gate_rows[1][0:E, :], gate2[0].rearrange("(e u) -> e u", u=C))
-        load_w2(0, 1)
+        load_w2(1)
         load_dy(1)
-        for f in range(1, E):
-            for s in range(PASSES):
-                load_w2(f, s)
-        nc.sync.dma_start(list1[:], offs)
+        for n in range(2, len(loads)):
+            load_w2(n)
+            if n == PASSES * WHOLE:
+                nc.sync.dma_start(list1[:], offs)
         nc.sync.dma_start(gate_rows[0][0:E, :], gate1[0].rearrange("(e u) -> e u", u=C))
         nc.sync.dma_start(w1_codes[:].bitcast(I32), w1t_words[:, 0].rearrange("e p b -> p e b").bitcast(I32))
         for q in range(4):
@@ -136,21 +148,20 @@ def tile_moe_seb_none_kernel(
 
         grouped, banks = {}, {}
 
-        def cast(piece):
-            f, s, half = piece // 4, piece // 2 % 2, piece % 2
-            unit = 2 * f + half
+        def cast(f, s, half):
+            unit = units.index((f, half))
             if s == 0:
                 grouped[unit] = ring.tile([P, PASSES, HALF * PACK], BF16, name="grouped", align_bytes=64)
-            cut = HALF - VECTOR_COLUMNS if piece % 4 == 1 and f > 0 else HALF
+            cut = HALF - VECTOR_COLUMNS if ((s, half) == (0, 1) and 0 < f < WHOLE) or (f, s, half) == (1, 1, 1) else HALF
             for engine_copy, c0, c1 in ((nc.scalar.copy, 0, cut), (nc.vector.tensor_copy, cut, HALF)):
                 if c0 < c1:
                     engine_copy(
                         grouped[unit][:, s, c0 * PACK : c1 * PACK].rearrange("p (c i j) -> p c j i", i=4, j=PACK),
-                        w2_raw[piece][:, :, c0:c1].rearrange("p j (c i) -> p c j i", i=4),
+                        w2_raw[f, s, half][:, :, c0:c1].rearrange("p j (c i) -> p c j i", i=4),
                     )
 
         def products(unit):
-            a, slots = two_part(unit // 2)
+            a, slots = two_part(units[unit][0])
             codes = ring.tile([P, PASSES, HALF], U32, name="w2_codes", align_bytes=64)
             plane = ring.tile([P, PASSES, HALF], U8, name="w2_plane", align_bytes=64)
             nc.vector.quantize_mx(
@@ -175,10 +186,10 @@ def tile_moe_seb_none_kernel(
         LATE_AT = 0
 
         def scatter_dc(unit, piece):
-            f, half = divmod(unit, 2)
+            f, half = units[unit]
             if unit == UNITS - 1:
                 sums = late.tile([P, 2, C], F32, name="last_sums", align_bytes=64, offset=LATE_AT)[:]
-            elif unit in (0, UNITS - 2):
+            elif unit == 0:
                 sums = keep.tile([P, 2, C], F32, name="sums%d" % unit)[:]
             else:
                 sums = w2_raw[piece][:, 0, :].rearrange("p (b u) -> p b u", b=2)
@@ -195,33 +206,43 @@ def tile_moe_seb_none_kernel(
             for n in range(count):
                 dc_slots[first + n, b] = target[:, n * C : (n + 1) * C]
 
-        for piece in range(PIECES + 4):
-            if piece < PIECES:
-                cast(piece)
-                if piece == 3:
-                    gate2_sb = raws.tile([P, E, C], F32, name="gate2_sb", align_bytes=64, offset=2 * PIECE_BYTES)
-                    g_codes[1][1] = raws.tile([P, T - EARLY], U32, name="g_codes1_1", align_bytes=64, offset=3 * PIECE_BYTES)
-                    nc.vector.tensor_copy(g_codes[1][1][:], dy_codes[1][:].bitcast(U32).indirect(picked[1]))
-                if piece % 4 >= 2:
-                    products(piece // 4 * 2 + piece % 2)
-            if piece == 3:
+        copy_at = {}
+        for n, (f, s, halves) in enumerate(loads):
+            if s == PASSES - 1:
+                for half in halves:
+                    copy_at[n + (1 if len(halves) - half == 2 else 2)] = units.index((f, half))
+        copy_at[1] = copy_at.pop(2)
+        for n in range(len(loads) + 2):
+            if n < len(loads):
+                f, s, halves = loads[n]
+                for half in halves:
+                    cast(f, s, half)
+                    if (n, half) == (1, 1):
+                        gate2_sb = raws.tile([P, E, C], F32, name="gate2_sb", align_bytes=64, offset=2 * PIECE_BYTES)
+                        g_codes[1][1] = raws.tile(
+                            [P, T - EARLY], U32, name="g_codes1_1", align_bytes=64, offset=3 * PIECE_BYTES
+                        )
+                        nc.vector.tensor_copy(g_codes[1][1][:], dy_codes[1][:].bitcast(U32).indirect(picked[1]))
+                    if s == PASSES - 1:
+                        products(units.index((f, half)))
+            if n == 1:
                 for a, bank in enumerate(gate2_banks):
                     nc.scalar.copy(gate2_sb[:, a * E // 2 : (a + 1) * E // 2, :], bank[:, 0 : E // 2, :])
-                scatter_dc(0, piece)
-            if piece >= 7 and piece % 2 == 1:
-                scatter_dc(piece // 2 - 2, piece - 1)
-            if piece == PIECES + 1:
-                first_slots = keep.tile([P, BLOCKS * C], F32, name="first_slots")
+            if n in copy_at:
+                scatter_dc(copy_at[n], (f, s, halves[0]))
+            pair = n - (len(loads) - 2 * EARLY_PAIRS)
+            if 0 <= pair < 2 * EARLY_PAIRS and pair % 2 == 0:
                 for b in range(2):
-                    gather_dc(first_slots[:, b * C : (b + 1) * C], b, 0, 1)
+                    gather_dc(w2_raw[f, s, 1][:, 1 + b, :], b, pair, 2)
 
         turn_gate(0)
+        first_slots = keep.tile([P, 2 * C], F32, name="first_slots")
         for b in range(2, BLOCKS):
-            gather_dc(first_slots[:, b * C : (b + 1) * C], b, 0, 1)
+            gather_dc(first_slots[:, (b - 2) * C : (b - 1) * C], b, 0, 1)
         behind = late.tile([P, 3 * BLOCKS * C], F32, name="behind", align_bytes=64, offset=LATE_AT)
-        for b in range(BLOCKS):
+        for b in range(2, BLOCKS):
             gather_dc(behind[:, b * C : (b + 1) * C], b, 1, 1)
-        for b in range(BLOCKS):
+        for b in range(0 if EARLY_PAIRS == 1 else 2, BLOCKS):
             gather_dc(behind[:, (BLOCKS + 2 * b) * C : (BLOCKS + 2 * b + 2) * C], b, 2, 2)
 
         ROWS_STEP = 3 * KIB // 2

@@ -22,16 +22,23 @@ PACK = 4
 PASSES = N // (P * PACK)
 BLOCKS = H // P
 K_BLOCKS = K // P
+QUADRANTS = 4
 PER_COLUMN = 16
 HALF = H // 2
 UNITS = 2 * E
-PIECES = UNITS * PASSES
-PIECE_BYTES = PACK * HALF * 4
-KIB = 1024
-EARLY = 2 * C
-VECTOR_COLUMNS = 96
+HALF_BYTES = PACK * HALF * 4
+RUN = 4
+BLOCK_PAIR_BYTES = 2 * C * 4
+
 WHOLE = 4
-EARLY_PAIRS = 1
+VECTOR_COLUMNS = 96
+EARLY = 2 * C
+TWO_BEHIND_FROM = 3
+RING_DEPTH = 4
+
+ROWS_STEP = 3 * BLOCK_PAIR_BYTES // 2
+MIDDLE_BYTES = 6 * BLOCK_PAIR_BYTES
+ROWS_AT = MIDDLE_BYTES + BLOCK_PAIR_BYTES
 
 
 def plan():
@@ -40,6 +47,12 @@ def plan():
         loads.extend([(f, s, (half,)) for f in range(WHOLE, E) for s in range(PASSES)])
     units = [(f, half) for f, s, halves in loads for half in halves if s == PASSES - 1]
     return loads, units
+
+
+def vector_share(f, s, half):
+    if half == 1 and (0 < f < WHOLE if s == 0 else f == 1):
+        return VECTOR_COLUMNS
+    return 0
 
 
 def entries(offsets, first, count):
@@ -54,34 +67,42 @@ def tile_moe_seb_none_kernel(
         keep = ctx.enter_context(tc.tile_pool(name="keep", bufs=1))
         raws = ctx.enter_context(tc.tile_pool(name="raws", bufs=1))
         late = ctx.enter_context(tc.tile_pool(name="late", bufs=1))
-        ring = ctx.enter_context(tc.tile_pool(name="ring", bufs=4))
+        ring = ctx.enter_context(tc.tile_pool(name="ring", bufs=RING_DEPTH))
         psum = ctx.enter_context(tc.psum_pool(name="psum", bufs=1))
+
+        def sums_bank():
+            return psum.tile([P, BLOCKS, C], F32, name="sums_bank", bufs=3)
+
+        def turn_bank(name):
+            return psum.tile([P, BLOCKS, C], F32, name=name, bufs=2)
 
         list1 = keep.tile([P, T // PER_COLUMN], U16, name="list1")
         list2 = keep.tile([P, T // PER_COLUMN], U16, name="list2")
         dy_plane = keep.tile([P, T], U8, name="dy_plane", align_bytes=64)
         w1_plane = keep.tile([P, E, K], U8, name="w1_plane", align_bytes=64)
         w1_codes = keep.tile([P, E, 2 * K], U8, name="w1_codes", align_bytes=64)
-        gate_rows = [keep.tile([P, C], F32, name="gate_rows%d" % a) for a in range(2)]
-        gate_cols = [keep.tile([P, E], F32, name="gate_cols%d" % a) for a in range(2)]
+        gate1_rows = keep.tile([P, C], F32, name="gate1_rows")
+        gate2_rows = keep.tile([P, C], F32, name="gate2_rows")
+        gate1_cols = keep.tile([P, E], F32, name="gate1_cols")
+        gate2_cols = keep.tile([P, E], F32, name="gate2_cols")
         identity = keep.tile([P, P], F32, name="identity")
         dy_codes = [keep.tile([P, T], I32, name="dy_codes%d" % s, align_bytes=64) for s in range(PASSES)]
         dc = [keep.tile([P, T], F32, name="dc%d" % b) for b in range(BLOCKS)]
         dx = [keep.tile([P, T], F32, name="dx%d" % b) for b in range(K_BLOCKS)]
 
         nc.gpsimd.memset(dy_plane[:].bitcast(I32), 0)
-        nc.gpsimd.memset(gate_rows[1][:], 0.0)
+        nc.gpsimd.memset(gate2_rows[:], 0.0)
         make_identity(nc, identity[:])
-        nc.gpsimd.memset(gate_rows[0][:], 0.0)
+        nc.gpsimd.memset(gate1_rows[:], 0.0)
         nc.gpsimd.memset(w1_plane[:].rearrange("p e k -> p (e k)").bitcast(I32), 0)
 
         loads, units = plan()
+        raw_at = [HALF_BYTES * sum(len(halves) for f, s, halves in loads[:n]) for n in range(len(loads))]
         w2_raw = {}
 
         def load_w2(n):
             f, s, halves = loads[n]
-            at = PIECE_BYTES * sum(len(load[2]) for load in loads[:n])
-            raw = raws.tile([P, PACK, len(halves) * HALF], F32, name="w2_raw%d" % n, align_bytes=64, offset=at)
+            raw = raws.tile([P, PACK, len(halves) * HALF], F32, name="w2_raw%d" % n, align_bytes=64, offset=raw_at[n])
             rows = w2t[f, s * P * PACK : (s + 1) * P * PACK, halves[0] * HALF : (halves[-1] + 1) * HALF]
             nc.sync.dma_start(raw[:], rows.rearrange("(p j) i -> p j i", j=PACK))
             for a, half in enumerate(halves):
@@ -93,110 +114,97 @@ def tile_moe_seb_none_kernel(
         nc.sync.dma_start(list2[:], offs2)
         load_dy(0)
         load_w2(0)
-        for q in range(4):
+        for q in range(QUADRANTS):
             nc.sync.dma_start(
                 dy_plane[32 * q : 32 * q + 4 * PASSES, :].bitcast(I32),
                 dy_scales[:, 4 * q : 4 * q + 4, :].bitcast(I32),
             )
-        nc.scalar.dma_start(gate_rows[1][0:E, :], gate2[0].rearrange("(e u) -> e u", u=C))
+        nc.scalar.dma_start(gate2_rows[0:E, :], gate2[0].rearrange("(e u) -> e u", u=C))
         load_w2(1)
         load_dy(1)
-        for n in range(2, len(loads)):
+        for n in range(PASSES, len(loads)):
             load_w2(n)
             if n == PASSES * WHOLE:
                 nc.sync.dma_start(list1[:], offs)
-        nc.sync.dma_start(gate_rows[0][0:E, :], gate1[0].rearrange("(e u) -> e u", u=C))
+        nc.sync.dma_start(gate1_rows[0:E, :], gate1[0].rearrange("(e u) -> e u", u=C))
         nc.sync.dma_start(w1_codes[:].bitcast(I32), w1t_words[:, 0].rearrange("e p b -> p e b").bitcast(I32))
-        for q in range(4):
+        for q in range(QUADRANTS):
             nc.sync.dma_start(
                 w1_plane[32 * q : 32 * q + 4, :, :].bitcast(I32),
                 w1t_scales[:, 0, 4 * q : 4 * q + 4, :].rearrange("e r k -> r e k").bitcast(I32),
             )
 
-        def turn_gate(a):
-            bank = psum.tile([P, BLOCKS, C], F32, name="by_row", bufs=2)
-            nc.tensor.transpose(bank[:, 0, :], gate_rows[a][:], identity[:])
-            nc.scalar.copy(gate_cols[a][:], bank[:, 0, 0:E])
+        def turn_gate(gate_rows, gate_cols):
+            bank = turn_bank("by_row")
+            nc.tensor.transpose(bank[:, 0, :], gate_rows[:], identity[:])
+            nc.scalar.copy(gate_cols[:], bank[:, 0, 0:E])
 
-        turn_gate(1)
+        turn_gate(gate2_rows, gate2_cols)
         gate2_banks = []
         for first in range(0, E, E // 2):
-            bank = psum.tile([P, BLOCKS, C], F32, name="by_slot", bufs=2)
+            bank = turn_bank("by_slot")
             for n in range(E // 2):
-                column = gate_cols[1][:, first + n : first + n + 1]
+                column = gate2_cols[:, first + n : first + n + 1]
                 nc.tensor.transpose(bank[:, n, :], column.to_broadcast([P, P]), identity[:])
             gate2_banks.append(bank)
 
         widths = (EARLY, T - EARLY)
-        picked = [entries(list2, 0, EARLY), entries(list2, EARLY, T - EARLY)]
-        g_codes = [[None, None], [None, None]]
-        g_plane = []
-        for a in range(2):
-            g_codes[a][0] = keep.tile([P, widths[a]], U32, name="g_codes%d_0" % a, align_bytes=64)
-            nc.vector.tensor_copy(g_codes[a][0][:], dy_codes[0][:].bitcast(U32).indirect(picked[a]))
-        for a in range(2):
-            plane = keep.tile([P, widths[a]], U8, name="g_plane%d" % a, align_bytes=64)
-            nc.vector.tensor_copy(plane[:], dy_plane[:].indirect(picked[a]))
-            g_plane.append(plane)
-        g_codes[0][1] = keep.tile([P, EARLY], U32, name="g_codes0_1", align_bytes=64)
-        nc.vector.tensor_copy(g_codes[0][1][:], dy_codes[1][:].bitcast(U32).indirect(picked[0]))
+        picked = (entries(list2, 0, EARLY), entries(list2, EARLY, T - EARLY))
+        g_codes, g_plane = {}, {}
 
-        def two_part(f):
-            if f * C < EARLY:
-                return 0, slice(f * C, (f + 1) * C)
-            return 1, slice(f * C - EARLY, (f + 1) * C - EARLY)
+        def gather_words(part, s, tile):
+            nc.vector.tensor_copy(tile[:], dy_codes[s][:].bitcast(U32).indirect(picked[part]))
+            g_codes[part, s] = tile
+
+        for part in range(2):
+            gather_words(part, 0, keep.tile([P, widths[part]], U32, name="g_codes%d_0" % part, align_bytes=64))
+        for part in range(2):
+            g_plane[part] = keep.tile([P, widths[part]], U8, name="g_plane%d" % part, align_bytes=64)
+            nc.vector.tensor_copy(g_plane[part][:], dy_plane[:].indirect(picked[part]))
+        gather_words(0, 1, keep.tile([P, EARLY], U32, name="g_codes0_1", align_bytes=64))
 
         grouped, banks = {}, {}
 
-        def cast(f, s, half):
-            unit = units.index((f, half))
+        def round_w2(f, s, half):
             if s == 0:
-                grouped[unit] = ring.tile([P, PASSES, HALF * PACK], BF16, name="grouped", align_bytes=64)
-            cut = HALF - VECTOR_COLUMNS if ((s, half) == (0, 1) and 0 < f < WHOLE) or (f, s, half) == (1, 1, 1) else HALF
+                grouped[f, half] = ring.tile([P, PASSES, HALF * PACK], BF16, name="grouped", align_bytes=64)
+            cut = HALF - vector_share(f, s, half)
             for engine_copy, c0, c1 in ((nc.scalar.copy, 0, cut), (nc.vector.tensor_copy, cut, HALF)):
                 if c0 < c1:
                     engine_copy(
-                        grouped[unit][:, s, c0 * PACK : c1 * PACK].rearrange("p (c i j) -> p c j i", i=4, j=PACK),
-                        w2_raw[f, s, half][:, :, c0:c1].rearrange("p j (c i) -> p c j i", i=4),
+                        grouped[f, half][:, s, c0 * PACK : c1 * PACK].rearrange("p (c i j) -> p c j i", i=RUN, j=PACK),
+                        w2_raw[f, s, half][:, :, c0:c1].rearrange("p j (c i) -> p c j i", i=RUN),
                     )
 
-        def products(unit):
-            a, slots = two_part(units[unit][0])
+        def second_layer_products(f, half):
+            part = 0 if f * C < EARLY else 1
+            slots = slice(f * C - part * EARLY, (f + 1) * C - part * EARLY)
             codes = ring.tile([P, PASSES, HALF], U32, name="w2_codes", align_bytes=64)
             plane = ring.tile([P, PASSES, HALF], U8, name="w2_plane", align_bytes=64)
             nc.vector.quantize_mx(
                 out=codes[:].rearrange("p s i -> p (s i)").bitcast(FP8X4),
                 scales=plane[:].rearrange("p s i -> p (s i)"),
-                in_=grouped[unit][:].rearrange("p s x -> p (s x)"),
+                in_=grouped[f, half][:].rearrange("p s x -> p (s x)"),
             )
-            banks[unit] = psum.tile([P, BLOCKS, C], F32, name="sums_bank", bufs=3)
+            banks[f, half] = sums_bank()
             for b in range(2):
                 cols = slice(b * P, (b + 1) * P)
                 for s in range(PASSES):
                     nc.tensor.matmul_mx(
-                        out=banks[unit][:, b, :],
+                        out=banks[f, half][:, b, :],
                         lhsT=codes[:, s, cols].bitcast(FP8X4),
                         lhsT_scale=plane[:, s, cols],
-                        rhs=g_codes[a][s][:, slots].bitcast(FP8X4),
-                        rhs_scale=g_plane[a][4 * s : P, slots],
+                        rhs=g_codes[part, s][:, slots].bitcast(FP8X4),
+                        rhs_scale=g_plane[part][4 * s : P, slots],
                         start=(s == 0),
                         stop=(s == PASSES - 1),
                     )
 
-        LATE_AT = 0
-
-        def scatter_dc(unit, piece):
-            f, half = units[unit]
-            if unit == UNITS - 1:
-                sums = late.tile([P, 2, C], F32, name="last_sums", align_bytes=64, offset=LATE_AT)[:]
-            elif unit == 0:
-                sums = keep.tile([P, 2, C], F32, name="sums%d" % unit)[:]
-            else:
-                sums = w2_raw[piece][:, 0, :].rearrange("p (b u) -> p b u", b=2)
-            nc.scalar.copy(sums, banks[unit][:, 0:2, :])
-            for n in range(2):
+        def scatter_dc(f, half, sums, gate2_all):
+            nc.scalar.copy(sums, banks[f, half][:, 0:2, :])
+            for b in range(2):
                 nc.vector.tensor_tensor(
-                    dc[2 * half + n][:].indirect(entries(list2, f * C, C)), sums[:, n, :], gate2_sb[:, f, :], MULT
+                    dc[2 * half + b][:].indirect(entries(list2, f * C, C)), sums[:, b, :], gate2_all[:, f, :], MULT
                 )
 
         dc_slots = {}
@@ -206,60 +214,60 @@ def tile_moe_seb_none_kernel(
             for n in range(count):
                 dc_slots[first + n, b] = target[:, n * C : (n + 1) * C]
 
-        copy_at = {}
+        leaves_after = {}
         for n, (f, s, halves) in enumerate(loads):
             if s == PASSES - 1:
                 for half in halves:
-                    copy_at[n + (1 if len(halves) - half == 2 else 2)] = units.index((f, half))
-        copy_at[1] = copy_at.pop(2)
-        for n in range(len(loads) + 2):
-            if n < len(loads):
-                f, s, halves = loads[n]
-                for half in halves:
-                    cast(f, s, half)
-                    if (n, half) == (1, 1):
-                        gate2_sb = raws.tile([P, E, C], F32, name="gate2_sb", align_bytes=64, offset=2 * PIECE_BYTES)
-                        g_codes[1][1] = raws.tile(
-                            [P, T - EARLY], U32, name="g_codes1_1", align_bytes=64, offset=3 * PIECE_BYTES
-                        )
-                        nc.vector.tensor_copy(g_codes[1][1][:], dy_codes[1][:].bitcast(U32).indirect(picked[1]))
-                    if s == PASSES - 1:
-                        products(units.index((f, half)))
-            if n == 1:
-                for a, bank in enumerate(gate2_banks):
-                    nc.scalar.copy(gate2_sb[:, a * E // 2 : (a + 1) * E // 2, :], bank[:, 0 : E // 2, :])
-            if n in copy_at:
-                scatter_dc(copy_at[n], (f, s, halves[0]))
-            pair = n - (len(loads) - 2 * EARLY_PAIRS)
-            if 0 <= pair < 2 * EARLY_PAIRS and pair % 2 == 0:
-                for b in range(2):
-                    gather_dc(w2_raw[f, s, 1][:, 1 + b, :], b, pair, 2)
+                    lag = 1 if (len(halves), half) == (2, 0) else 2
+                    leaves_after[n if (f, half) == units[0] else n + lag] = (f, half)
 
-        turn_gate(0)
+        for n, (f, s, halves) in enumerate(loads):
+            for half in halves:
+                round_w2(f, s, half)
+                if (f, s, half) == (0, 1, 1):
+                    gate2_all = raws.tile([P, E, C], F32, name="gate2_all", align_bytes=64, offset=raw_at[n])
+                    offset = raw_at[n] + HALF_BYTES
+                    gather_words(1, 1, raws.tile([P, widths[1]], U32, name="g_codes1_1", align_bytes=64, offset=offset))
+                if s == PASSES - 1:
+                    second_layer_products(f, half)
+            if leaves_after.get(n) == units[0]:
+                for a, bank in enumerate(gate2_banks):
+                    nc.scalar.copy(gate2_all[:, a * E // 2 : (a + 1) * E // 2, :], bank[:, 0 : E // 2, :])
+                first_sums = keep.tile([P, 2, C], F32, name="first_sums")
+                scatter_dc(*units[0], first_sums[:], gate2_all)
+            elif n in leaves_after:
+                sums = w2_raw[f, s, halves[0]][:, 0, :].rearrange("p (b u) -> p b u", b=2)
+                scatter_dc(*leaves_after[n], sums, gate2_all)
+            if (f, halves) == (E - 1, (1,)):
+                gather_dc(w2_raw[f, s, 1][:, 1, :], s, 0, 2)
+        last_sums = late.tile([P, 2, C], F32, name="last_sums", align_bytes=64, offset=0)
+        scatter_dc(*units[UNITS - 1], last_sums[:], gate2_all)
+
+        turn_gate(gate1_rows, gate1_cols)
         first_slots = keep.tile([P, 2 * C], F32, name="first_slots")
         for b in range(2, BLOCKS):
             gather_dc(first_slots[:, (b - 2) * C : (b - 1) * C], b, 0, 1)
-        behind = late.tile([P, 3 * BLOCKS * C], F32, name="behind", align_bytes=64, offset=LATE_AT)
+        middle = late.tile([P, MIDDLE_BYTES // 4], F32, name="middle", align_bytes=64, offset=0)
         for b in range(2, BLOCKS):
-            gather_dc(behind[:, b * C : (b + 1) * C], b, 1, 1)
-        for b in range(0 if EARLY_PAIRS == 1 else 2, BLOCKS):
-            gather_dc(behind[:, (BLOCKS + 2 * b) * C : (BLOCKS + 2 * b + 2) * C], b, 2, 2)
-
-        ROWS_STEP = 3 * KIB // 2
+            gather_dc(middle[:, b * C : (b + 1) * C], b, 1, 1)
+        for b in range(BLOCKS):
+            gather_dc(middle[:, (BLOCKS + 2 * b) * C : (BLOCKS + 2 * b + 2) * C], b, 2, 2)
+        gather_dc(middle[:, 0 : 2 * C], 0, 4, 2)
 
         def quantise_da(e):
-            by_slot = psum.tile([P, BLOCKS, C], F32, name="by_slot", bufs=2)
+            by_slot = turn_bank("by_slot")
             for b in range(BLOCKS):
                 nc.tensor.transpose(by_slot[:, b, :], dc_slots[e, b], identity[:])
-            da_rows = late.tile([P, 2, P, 2], BF16, name="da_rows%d" % e, align_bytes=64, offset=8 * KIB + e * ROWS_STEP)
+            offset = ROWS_AT + BLOCK_PAIR_BYTES + e * ROWS_STEP
+            da_rows = late.tile([P, 2, P, 2], BF16, name="da_rows%d" % e, align_bytes=64, offset=offset)
             nc.scalar.activation(
                 da_rows[:],
                 by_slot[:].rearrange("u b i -> u (b i)").rearrange("u (p h d) -> u h p d", h=2, d=2),
                 COPY,
-                scale=gate_cols[0][:, e : e + 1],
+                scale=gate1_cols[:, e : e + 1],
             )
             pairs = da_rows[:].rearrange("u h p d -> u (h p d)").bitcast(F32)
-            by_row = psum.tile([P, BLOCKS, C], F32, name="by_row", bufs=2)
+            by_row = turn_bank("by_row")
             for h in range(2):
                 nc.tensor.transpose(by_row[:, h, :], pairs[:, h * P : (h + 1) * P], identity[:])
             da = ring.tile([P, C * PACK], BF16, name="da", align_bytes=64)
@@ -271,8 +279,8 @@ def tile_moe_seb_none_kernel(
             nc.vector.quantize_mx(out=da_codes[:].bitcast(FP8X4), scales=da_plane[:], in_=da[:])
             return da_codes, da_plane
 
-        def first_layer_products(e, da_codes, da_plane):
-            bank = psum.tile([P, BLOCKS, C], F32, name="sums_bank", bufs=3)
+        def first_layer_products(e, behind, da_codes, da_plane):
+            bank = sums_bank()
             for b in range(K_BLOCKS):
                 nc.tensor.matmul_mx(
                     out=bank[:, b, :],
@@ -283,23 +291,23 @@ def tile_moe_seb_none_kernel(
                     start=True,
                     stop=True,
                 )
-            results = late.tile(
-                [P, K_BLOCKS, C], F32, name="results%d" % e, align_bytes=64, offset=8 * KIB + (e + 1) * ROWS_STEP + KIB // 2
-            )
+            offset = ROWS_AT + BLOCK_PAIR_BYTES + behind * ROWS_STEP + BLOCK_PAIR_BYTES // 2
+            results = late.tile([P, K_BLOCKS, C], F32, name="results%d" % e, align_bytes=64, offset=offset)
             nc.scalar.copy(results[:], bank[:, 0:K_BLOCKS, :])
             for b in range(K_BLOCKS):
                 nc.vector.tensor_copy(dx[b][:].indirect(entries(list1, e * C, C)), results[:, b, :])
 
+        follows = {e + (1 if e < TWO_BEHIND_FROM else 2): e for e in range(E)}
         da_mx = {}
-        for step in range(E + 1):
+        for step in range(max(follows) + 1):
             if step < E:
                 da_mx[step] = quantise_da(step)
             if step == 1:
-                last_slots = late.tile([P, 2 * BLOCKS * C], F32, name="last_slots", align_bytes=64, offset=6 * KIB)
-                for b in range(BLOCKS):
-                    gather_dc(last_slots[:, 2 * b * C : (2 * b + 2) * C], b, 4, 2)
-            if step >= 1:
-                first_layer_products(step - 1, *da_mx[step - 1])
+                last_slots = late.tile([P, BLOCKS - 1, 2 * C], F32, name="last_slots", align_bytes=64, offset=ROWS_AT)
+                for b in range(1, BLOCKS):
+                    gather_dc(last_slots[:, b - 1, :], b, 4, 2)
+            if step in follows:
+                first_layer_products(follows[step], step, *da_mx[follows[step]])
 
         for b in range(K_BLOCKS):
             nc.sync.dma_start(out[b * P : (b + 1) * P, :], dx[b][:])

@@ -31,10 +31,10 @@ RUN = 4
 BLOCK_PAIR_BYTES = 2 * C * 4
 
 WHOLE = 4
-VECTOR_COLUMNS = 96
+VECTOR_COLUMNS = 128
 EARLY = 2 * C
 TWO_BEHIND_FROM = 3
-RING_DEPTH = 4
+RING_DEPTH = 6
 
 ROWS_STEP = 3 * BLOCK_PAIR_BYTES // 2
 MIDDLE_BYTES = 6 * BLOCK_PAIR_BYTES
@@ -176,16 +176,25 @@ def tile_moe_seb_none_kernel(
                         w2_raw[f, s, half][:, :, c0:c1].rearrange("p j (c i) -> p c j i", i=RUN),
                     )
 
+        w2_mx = {}
+
+        def quantise_w2(f, half, first, end):
+            if first == 0:
+                w2_mx[f, half] = (
+                    ring.tile([P, PASSES, HALF], U32, name="w2_codes", align_bytes=64),
+                    ring.tile([P, PASSES, HALF], U8, name="w2_plane", align_bytes=64),
+                )
+            codes, plane = w2_mx[f, half]
+            nc.vector.quantize_mx(
+                out=codes[:, first:end, :].rearrange("p s i -> p (s i)").bitcast(FP8X4),
+                scales=plane[:, first:end, :].rearrange("p s i -> p (s i)"),
+                in_=grouped[f, half][:, first:end, :].rearrange("p s x -> p (s x)"),
+            )
+
         def second_layer_products(f, half):
             part = 0 if f * C < EARLY else 1
             slots = slice(f * C - part * EARLY, (f + 1) * C - part * EARLY)
-            codes = ring.tile([P, PASSES, HALF], U32, name="w2_codes", align_bytes=64)
-            plane = ring.tile([P, PASSES, HALF], U8, name="w2_plane", align_bytes=64)
-            nc.vector.quantize_mx(
-                out=codes[:].rearrange("p s i -> p (s i)").bitcast(FP8X4),
-                scales=plane[:].rearrange("p s i -> p (s i)"),
-                in_=grouped[f, half][:].rearrange("p s x -> p (s x)"),
-            )
+            codes, plane = w2_mx[f, half]
             banks[f, half] = sums_bank()
             for b in range(2):
                 cols = slice(b * P, (b + 1) * P)
@@ -228,6 +237,10 @@ def tile_moe_seb_none_kernel(
                     gate2_all = raws.tile([P, E, C], F32, name="gate2_all", align_bytes=64, offset=raw_at[n])
                     offset = raw_at[n] + HALF_BYTES
                     gather_words(1, 1, raws.tile([P, widths[1]], U32, name="g_codes1_1", align_bytes=64, offset=offset))
+                if f < WHOLE:
+                    quantise_w2(f, half, s, s + 1)
+                elif s == PASSES - 1:
+                    quantise_w2(f, half, 0, PASSES)
                 if s == PASSES - 1:
                     second_layer_products(f, half)
             if leaves_after.get(n) == units[0]:

@@ -24,35 +24,20 @@ BLOCKS = H // P
 K_BLOCKS = K // P
 QUADRANTS = 4
 PER_COLUMN = 16
-HALF = H // 2
-UNITS = 2 * E
-HALF_BYTES = PACK * HALF * 4
+PASS_BYTES = PACK * H * 4
 RUN = 4
 BLOCK_PAIR_BYTES = 2 * C * 4
 
-WHOLE = 4
-VECTOR_COLUMNS = 128
-EARLY = 2 * C
+SHARE = 64
+CUTS = (0, 2, E)
+HELD_FROM = 3
+GATE2_ROWS = 8
 TWO_BEHIND_FROM = 3
-RING_DEPTH = 6
+RING_DEPTH = 3
 
 ROWS_STEP = 3 * BLOCK_PAIR_BYTES // 2
 MIDDLE_BYTES = 6 * BLOCK_PAIR_BYTES
 ROWS_AT = MIDDLE_BYTES + BLOCK_PAIR_BYTES
-
-
-def plan():
-    loads = [(f, s, (0, 1)) for f in range(WHOLE) for s in range(PASSES)]
-    for half in range(2):
-        loads.extend([(f, s, (half,)) for f in range(WHOLE, E) for s in range(PASSES)])
-    units = [(f, half) for f, s, halves in loads for half in halves if s == PASSES - 1]
-    return loads, units
-
-
-def vector_share(f, s, half):
-    if half == 1 and (0 < f < WHOLE if s == 0 else f == 1):
-        return VECTOR_COLUMNS
-    return 0
 
 
 def entries(offsets, first, count):
@@ -66,6 +51,7 @@ def tile_moe_seb_none_kernel(
     with ExitStack() as ctx:
         keep = ctx.enter_context(tc.tile_pool(name="keep", bufs=1))
         raws = ctx.enter_context(tc.tile_pool(name="raws", bufs=1))
+        head = ctx.enter_context(tc.tile_pool(name="head", bufs=1))
         late = ctx.enter_context(tc.tile_pool(name="late", bufs=1))
         ring = ctx.enter_context(tc.tile_pool(name="ring", bufs=RING_DEPTH))
         psum = ctx.enter_context(tc.psum_pool(name="psum", bufs=1))
@@ -84,7 +70,7 @@ def tile_moe_seb_none_kernel(
         gate1_rows = keep.tile([P, C], F32, name="gate1_rows")
         gate2_rows = keep.tile([P, C], F32, name="gate2_rows")
         gate1_cols = keep.tile([P, E], F32, name="gate1_cols")
-        gate2_cols = keep.tile([P, E], F32, name="gate2_cols")
+        gate2_cols = keep.tile([P, GATE2_ROWS], F32, name="gate2_cols")
         identity = keep.tile([P, P], F32, name="identity")
         dy_codes = [keep.tile([P, T], I32, name="dy_codes%d" % s, align_bytes=64) for s in range(PASSES)]
         dc = [keep.tile([P, T], F32, name="dc%d" % b) for b in range(BLOCKS)]
@@ -96,35 +82,36 @@ def tile_moe_seb_none_kernel(
         nc.gpsimd.memset(gate1_rows[:], 0.0)
         nc.gpsimd.memset(w1_plane[:].rearrange("p e k -> p (e k)").bitcast(I32), 0)
 
-        loads, units = plan()
-        raw_at = [HALF_BYTES * sum(len(halves) for f, s, halves in loads[:n]) for n in range(len(loads))]
         w2_raw = {}
 
-        def load_w2(n):
-            f, s, halves = loads[n]
-            raw = raws.tile([P, PACK, len(halves) * HALF], F32, name="w2_raw%d" % n, align_bytes=64, offset=raw_at[n])
-            rows = w2t[f, s * P * PACK : (s + 1) * P * PACK, halves[0] * HALF : (halves[-1] + 1) * HALF]
+        def raw_at(f, s):
+            return PASS_BYTES * (PASSES * f + s)
+
+        def load_w2(f, s):
+            raw = raws.tile([P, PACK, H], F32, name="w2_raw%d_%d" % (f, s), align_bytes=64, offset=raw_at(f, s))
+            rows = w2t[f, s * P * PACK : (s + 1) * P * PACK, :]
             nc.sync.dma_start(raw[:], rows.rearrange("(p j) i -> p j i", j=PACK))
-            for a, half in enumerate(halves):
-                w2_raw[f, s, half] = raw[:, :, a * HALF : (a + 1) * HALF]
+            w2_raw[f, s] = raw
 
         def load_dy(s):
             nc.sync.dma_start(dy_codes[s][:], dy_words[s].rearrange("p t d -> p (t d)").bitcast(I32))
 
+        piece = T // GATE2_ROWS
         nc.sync.dma_start(list2[:], offs2)
         load_dy(0)
-        load_w2(0)
         for q in range(QUADRANTS):
             nc.sync.dma_start(
                 dy_plane[32 * q : 32 * q + 4 * PASSES, :].bitcast(I32),
                 dy_scales[:, 4 * q : 4 * q + 4, :].bitcast(I32),
             )
-        nc.scalar.dma_start(gate2_rows[0:E, :], gate2[0].rearrange("(e u) -> e u", u=C))
-        load_w2(1)
+        load_w2(0, 0)
+        nc.scalar.dma_start(gate2_rows[0:GATE2_ROWS, 0:piece], gate2[0].rearrange("(r u) -> r u", u=piece))
         load_dy(1)
-        for n in range(PASSES, len(loads)):
-            load_w2(n)
-            if n == PASSES * WHOLE:
+        load_w2(0, 1)
+        for f in range(1, E):
+            for s in range(PASSES):
+                load_w2(f, s)
+            if f == E - 2:
                 nc.sync.dma_start(list1[:], offs)
         nc.sync.dma_start(gate1_rows[0:E, :], gate1[0].rearrange("(e u) -> e u", u=C))
         nc.sync.dma_start(w1_codes[:].bitcast(I32), w1t_words[:, 0].rearrange("e p b -> p e b").bitcast(I32))
@@ -134,87 +121,80 @@ def tile_moe_seb_none_kernel(
                 w1t_scales[:, 0, 4 * q : 4 * q + 4, :].rearrange("e r k -> r e k").bitcast(I32),
             )
 
-        def turn_gate(gate_rows, gate_cols):
+        def turn_gate(gate_rows, gate_cols, count):
             bank = turn_bank("by_row")
             nc.tensor.transpose(bank[:, 0, :], gate_rows[:], identity[:])
-            nc.scalar.copy(gate_cols[:], bank[:, 0, 0:E])
+            nc.scalar.copy(gate_cols[:], bank[:, 0, 0:count])
 
-        turn_gate(gate2_rows, gate2_cols)
+        turn_gate(gate2_rows, gate2_cols, GATE2_ROWS)
         gate2_banks = []
-        for first in range(0, E, E // 2):
+        for first in range(0, GATE2_ROWS, BLOCKS):
             bank = turn_bank("by_slot")
-            for n in range(E // 2):
+            for n in range(BLOCKS):
                 column = gate2_cols[:, first + n : first + n + 1]
                 nc.tensor.transpose(bank[:, n, :], column.to_broadcast([P, P]), identity[:])
             gate2_banks.append(bank)
 
-        widths = (EARLY, T - EARLY)
-        picked = (entries(list2, 0, EARLY), entries(list2, EARLY, T - EARLY))
         g_codes, g_plane = {}, {}
 
-        def gather_words(part, s, tile):
-            nc.vector.tensor_copy(tile[:], dy_codes[s][:].bitcast(U32).indirect(picked[part]))
-            g_codes[part, s] = tile
+        def gather_dy(window, dtype, name, first, end, pool=keep, **place):
+            tile = pool.tile([P, (end - first) * C], dtype, name="%s_%d" % (name, first), align_bytes=64, **place)
+            nc.vector.tensor_copy(tile[:], window.indirect(entries(list2, first * C, (end - first) * C)))
+            return {f: tile[:, (f - first) * C : (f - first + 1) * C] for f in range(first, end)}
 
-        for part in range(2):
-            gather_words(part, 0, keep.tile([P, widths[part]], U32, name="g_codes%d_0" % part, align_bytes=64))
-        for part in range(2):
-            g_plane[part] = keep.tile([P, widths[part]], U8, name="g_plane%d" % part, align_bytes=64)
-            nc.vector.tensor_copy(g_plane[part][:], dy_plane[:].indirect(picked[part]))
-        gather_words(0, 1, keep.tile([P, EARLY], U32, name="g_codes0_1", align_bytes=64))
+        def gather_words(s, first, end, **place):
+            parts = gather_dy(dy_codes[s][:].bitcast(U32), U32, "g_codes%d" % s, first, end, **place)
+            g_codes.update({(f, s): part for f, part in parts.items()})
 
-        grouped, banks = {}, {}
+        for first, end in zip(CUTS, CUTS[1:]):
+            gather_words(0, first, end)
+        for first, end in zip(CUTS, CUTS[1:]):
+            g_plane.update(gather_dy(dy_plane[:], U8, "g_plane", first, end))
+        gather_words(1, 0, HELD_FROM)
 
-        def round_w2(f, s, half):
-            if s == 0:
-                grouped[f, half] = ring.tile([P, PASSES, HALF * PACK], BF16, name="grouped", align_bytes=64)
-            cut = HALF - vector_share(f, s, half)
-            for engine_copy, c0, c1 in ((nc.scalar.copy, 0, cut), (nc.vector.tensor_copy, cut, HALF)):
-                if c0 < c1:
-                    engine_copy(
-                        grouped[f, half][:, s, c0 * PACK : c1 * PACK].rearrange("p (c i j) -> p c j i", i=RUN, j=PACK),
-                        w2_raw[f, s, half][:, :, c0:c1].rearrange("p j (c i) -> p c j i", i=RUN),
-                    )
+        grouped, w2_codes, w2_plane, banks = {}, {}, {}, {}
 
-        w2_mx = {}
+        first_block = head.tile([P, P * PACK], BF16, name="first_block", align_bytes=64, offset=0)
 
-        def quantise_w2(f, half, first, end):
-            if first == 0:
-                w2_mx[f, half] = (
-                    ring.tile([P, PASSES, HALF], U32, name="w2_codes", align_bytes=64),
-                    ring.tile([P, PASSES, HALF], U8, name="w2_plane", align_bytes=64),
-                )
-            codes, plane = w2_mx[f, half]
-            nc.vector.quantize_mx(
-                out=codes[:, first:end, :].rearrange("p s i -> p (s i)").bitcast(FP8X4),
-                scales=plane[:, first:end, :].rearrange("p s i -> p (s i)"),
-                in_=grouped[f, half][:, first:end, :].rearrange("p s x -> p (s x)"),
+        def rounded_columns(f, s, c0, c1):
+            tile = first_block if (f, s, c0) == (0, 1, 0) else grouped[f, s]
+            return tile[:, c0 * PACK : c1 * PACK]
+
+        def round_w2(engine_copy, f, s, c0, c1):
+            engine_copy(
+                rounded_columns(f, s, c0, c1).rearrange("p (c i j) -> p c j i", i=RUN, j=PACK),
+                w2_raw[f, s][:, :, c0:c1].rearrange("p j (c i) -> p c j i", i=RUN),
             )
 
-        def second_layer_products(f, half):
-            part = 0 if f * C < EARLY else 1
-            slots = slice(f * C - part * EARLY, (f + 1) * C - part * EARLY)
-            codes, plane = w2_mx[f, half]
-            banks[f, half] = sums_bank()
-            for b in range(2):
-                cols = slice(b * P, (b + 1) * P)
-                for s in range(PASSES):
-                    nc.tensor.matmul_mx(
-                        out=banks[f, half][:, b, :],
-                        lhsT=codes[:, s, cols].bitcast(FP8X4),
-                        lhsT_scale=plane[:, s, cols],
-                        rhs=g_codes[part, s][:, slots].bitcast(FP8X4),
-                        rhs_scale=g_plane[part][4 * s : P, slots],
-                        start=(s == 0),
-                        stop=(s == PASSES - 1),
-                    )
+        def quantise_w2(f, s, first, end):
+            nc.vector.quantize_mx(
+                out=w2_codes[f, s][:, first * P : end * P].bitcast(FP8X4),
+                scales=w2_plane[f, s][:, first * P : end * P],
+                in_=rounded_columns(f, s, first * P, end * P),
+            )
 
-        def scatter_dc(f, half, sums, gate2_all):
-            nc.scalar.copy(sums, banks[f, half][:, 0:2, :])
-            for b in range(2):
-                nc.vector.tensor_tensor(
-                    dc[2 * half + b][:].indirect(entries(list2, f * C, C)), sums[:, b, :], gate2_all[:, f, :], MULT
+        def second_layer_products(f, b, bank, place):
+            cols = slice(b * P, (b + 1) * P)
+            for s in range(PASSES):
+                nc.tensor.matmul_mx(
+                    out=bank[:, place, :],
+                    lhsT=w2_codes[f, s][:, cols].bitcast(FP8X4),
+                    lhsT_scale=w2_plane[f, s][:, cols],
+                    rhs=g_codes[f, s].bitcast(FP8X4),
+                    rhs_scale=g_plane[f][4 * s : P, :],
+                    start=(s == 0),
+                    stop=(s == PASSES - 1),
                 )
+            banks[f, b] = bank
+
+        def scatter_dc(f, first, count, sums):
+            nc.scalar.copy(sums, banks[f, first][:, 0:count, :])
+            for n in range(count):
+                window = dc[first + n][:].indirect(entries(list2, f * C, C))
+                nc.vector.tensor_tensor(window, sums[:, n, :], gate2_all[:, f // 3, (f % 3) * C : (f % 3 + 1) * C], MULT)
+
+        def parked(f, s, count):
+            return w2_raw[f, s][:, 0:count, 0:C]
 
         dc_slots = {}
 
@@ -223,40 +203,61 @@ def tile_moe_seb_none_kernel(
             for n in range(count):
                 dc_slots[first + n, b] = target[:, n * C : (n + 1) * C]
 
-        leaves_after = {}
-        for n, (f, s, halves) in enumerate(loads):
-            if s == PASSES - 1:
-                for half in halves:
-                    lag = 1 if (len(halves), half) == (2, 0) else 2
-                    leaves_after[n if (f, half) == units[0] else n + lag] = (f, half)
+        for f in range(E):
+            for s in range(PASSES):
+                grouped[f, s] = ring.tile([P, H * PACK], BF16, name="grouped%d" % s, align_bytes=64)
+                w2_codes[f, s] = ring.tile([P, H], U32, name="w2_codes%d" % s, align_bytes=64)
+                w2_plane[f, s] = ring.tile([P, H], U8, name="w2_plane%d" % s, align_bytes=64)
+            end = H - P if f == 1 else H
+            if end < H:
+                round_w2(nc.vector.tensor_copy, f, 0, end, H)
+            round_w2(nc.scalar.copy, f, 0, 0, P)
+            round_w2(nc.scalar.copy, f, 0, P, 2 * P)
+            quantise_w2(f, 0, 0, 2)
+            if f > 0:
+                scatter_dc(f - 1, 1, 1, parked(f, 0, 1))
+            if f == 0:
+                round_w2(nc.scalar.copy, f, 0, 2 * P, 3 * P)
+                round_w2(nc.scalar.copy, f, 0, 3 * P, H)
+            else:
+                round_w2(nc.scalar.copy, f, 0, 2 * P, end)
+            quantise_w2(f, 0, 2, BLOCKS)
+            if f == 0:
+                gate2_all = w2_raw[0, 0][:, 0:2, 0 : T // 2]
+                for n, gate2_bank in enumerate(gate2_banks):
+                    spread = gate2_all[:, n, :].rearrange("p (r u) -> p r u", u=piece)
+                    nc.scalar.copy(spread, gate2_bank[:, :, 0:piece])
 
-        for n, (f, s, halves) in enumerate(loads):
-            for half in halves:
-                round_w2(f, s, half)
-                if (f, s, half) == (0, 1, 1):
-                    gate2_all = raws.tile([P, E, C], F32, name="gate2_all", align_bytes=64, offset=raw_at[n])
-                    offset = raw_at[n] + HALF_BYTES
-                    gather_words(1, 1, raws.tile([P, widths[1]], U32, name="g_codes1_1", align_bytes=64, offset=offset))
-                if f < WHOLE:
-                    quantise_w2(f, half, s, s + 1)
-                elif s == PASSES - 1:
-                    quantise_w2(f, half, 0, PASSES)
-                if s == PASSES - 1:
-                    second_layer_products(f, half)
-            if leaves_after.get(n) == units[0]:
-                for a, bank in enumerate(gate2_banks):
-                    nc.scalar.copy(gate2_all[:, a * E // 2 : (a + 1) * E // 2, :], bank[:, 0 : E // 2, :])
-                first_sums = keep.tile([P, 2, C], F32, name="first_sums")
-                scatter_dc(*units[0], first_sums[:], gate2_all)
-            elif n in leaves_after:
-                sums = w2_raw[f, s, halves[0]][:, 0, :].rearrange("p (b u) -> p b u", b=2)
-                scatter_dc(*leaves_after[n], sums, gate2_all)
-            if (f, halves) == (E - 1, (1,)):
-                gather_dc(w2_raw[f, s, 1][:, 1, :], s, 0, 2)
+            if f == 0:
+                round_w2(nc.vector.tensor_copy, f, 1, 0, P)
+                quantise_w2(f, 1, 0, 1)
+                gather_words(1, HELD_FROM, E, pool=head, offset=0)
+                round_w2(nc.scalar.copy, f, 1, P, 2 * P)
+            else:
+                round_w2(nc.vector.tensor_copy, f, 1, 2 * P - SHARE, 2 * P)
+                round_w2(nc.scalar.copy, f, 1, 0, P)
+                quantise_w2(f, 1, 0, 1)
+                round_w2(nc.scalar.copy, f, 1, P, 2 * P - SHARE)
+            second_layer_products(f, 0, sums_bank(), 0)
+            quantise_w2(f, 1, 1, 2)
+            second_layer_products(f, 1, sums_bank(), 0)
+            if f > 0:
+                scatter_dc(f - 1, 2, 2, parked(f, 1, 2))
+            round_w2(nc.scalar.copy, f, 1, 2 * P, H)
+            quantise_w2(f, 1, 2, BLOCKS)
+            high_bank = sums_bank()
+            for b in range(2, BLOCKS):
+                second_layer_products(f, b, high_bank, b - 2)
+            low_sums = ring.tile([P, 1, C], F32, name="low_sums")
+            scatter_dc(f, 0, 1, low_sums[:])
+        scatter_dc(E - 1, 1, 1, keep.tile([P, 1, C], F32, name="second_sums")[:])
+        early_slots = keep.tile([P, 2, 2 * C], F32, name="early_slots")
+        for b in range(2):
+            gather_dc(early_slots[:, b, :], b, 0, 2)
         last_sums = late.tile([P, 2, C], F32, name="last_sums", align_bytes=64, offset=0)
-        scatter_dc(*units[UNITS - 1], last_sums[:], gate2_all)
+        scatter_dc(E - 1, 2, 2, last_sums[:])
 
-        turn_gate(gate1_rows, gate1_cols)
+        turn_gate(gate1_rows, gate1_cols, E)
         first_slots = keep.tile([P, 2 * C], F32, name="first_slots")
         for b in range(2, BLOCKS):
             gather_dc(first_slots[:, (b - 2) * C : (b - 1) * C], b, 0, 1)

@@ -64,19 +64,19 @@ def tile_moe_seb_none_kernel(
 
         list1 = keep.tile([P, T // PER_COLUMN], U16, name="list1")
         list2 = keep.tile([P, T // PER_COLUMN], U16, name="list2")
-        dy_plane = keep.tile([P, T], U8, name="dy_plane", align_bytes=64)
-        w1_plane = keep.tile([P, E, K], U8, name="w1_plane", align_bytes=64)
-        w1_codes = keep.tile([P, E, 2 * K], U8, name="w1_codes", align_bytes=64)
+        dy_plane = keep.tile([P, T], U8, name="dy_plane", align_bytes=256)
+        w1_plane = keep.tile([P, E, K], U8, name="w1_plane", align_bytes=256)
+        w1_codes = keep.tile([P, E, 2 * K], U8, name="w1_codes", align_bytes=256)
         gate1_rows = keep.tile([P, C], F32, name="gate1_rows")
         gate2_rows = keep.tile([P, C], F32, name="gate2_rows")
         gate1_cols = keep.tile([P, E], F32, name="gate1_cols")
         gate2_cols = keep.tile([P, GATE2_ROWS], F32, name="gate2_cols")
         identity = keep.tile([P, P], F32, name="identity")
-        dy_codes = [keep.tile([P, T], I32, name="dy_codes%d" % s, align_bytes=64) for s in range(PASSES)]
+        dy_codes = [keep.tile([P, T], I32, name="dy_codes%d" % s, align_bytes=256) for s in range(PASSES)]
         dc = [keep.tile([P, T], F32, name="dc%d" % b) for b in range(BLOCKS)]
-        dx = [keep.tile([P, T], F32, name="dx%d" % b) for b in range(K_BLOCKS)]
+        dx = [keep.tile([P, T], F32, name="dx%d" % b, align_bytes=256) for b in range(K_BLOCKS)]
 
-        nc.gpsimd.memset(dy_plane[:].bitcast(I32), 0)
+        nc.vector.memset(dy_plane[:].bitcast(I32), 0)
         nc.gpsimd.memset(gate2_rows[:], 0.0)
         make_identity(nc, identity[:])
         nc.gpsimd.memset(gate1_rows[:], 0.0)
@@ -88,7 +88,7 @@ def tile_moe_seb_none_kernel(
             return PASS_BYTES * (PASSES * f + s)
 
         def load_w2(f, s):
-            raw = raws.tile([P, PACK, H], F32, name="w2_raw%d_%d" % (f, s), align_bytes=64, offset=raw_at(f, s))
+            raw = raws.tile([P, PACK, H], F32, name="w2_raw%d_%d" % (f, s), align_bytes=256, offset=raw_at(f, s))
             rows = w2t[f, s * P * PACK : (s + 1) * P * PACK, :]
             nc.sync.dma_start(raw[:], rows.rearrange("(p j) i -> p j i", j=PACK))
             w2_raw[f, s] = raw

@@ -29,11 +29,13 @@ RUN = 4
 BLOCK_PAIR_BYTES = 2 * C * 4
 
 SHARE = 64
+WHOLE = 3
+HALF = H // 2
 CUTS = (0, 2, E)
 HELD_FROM = 3
 GATE2_ROWS = 8
 TWO_BEHIND_FROM = 3
-RING_DEPTH = 3
+RING_DEPTH = 8
 
 ROWS_STEP = 3 * BLOCK_PAIR_BYTES // 2
 MIDDLE_BYTES = 6 * BLOCK_PAIR_BYTES
@@ -50,7 +52,6 @@ def tile_moe_seb_none_kernel(
     nc = tc.nc
     with ExitStack() as ctx:
         keep = ctx.enter_context(tc.tile_pool(name="keep", bufs=1))
-        raws = ctx.enter_context(tc.tile_pool(name="raws", bufs=1))
         head = ctx.enter_context(tc.tile_pool(name="head", bufs=1))
         late = ctx.enter_context(tc.tile_pool(name="late", bufs=1))
         ring = ctx.enter_context(tc.tile_pool(name="ring", bufs=RING_DEPTH))
@@ -84,14 +85,14 @@ def tile_moe_seb_none_kernel(
 
         w2_raw = {}
 
-        def raw_at(f, s):
-            return PASS_BYTES * (PASSES * f + s)
-
-        def load_w2(f, s):
-            raw = raws.tile([P, PACK, H], F32, name="w2_raw%d_%d" % (f, s), align_bytes=256, offset=raw_at(f, s))
-            rows = w2t[f, s * P * PACK : (s + 1) * P * PACK, :]
+        def load_w2(f, s, c0, c1):
+            raw = keep.tile([P, PACK, c1 - c0], F32, name="w2_raw%d_%d_%d" % (f, s, c0), align_bytes=256)
+            rows = w2t[f, s * P * PACK : (s + 1) * P * PACK, c0:c1]
             nc.sync.dma_start(raw[:], rows.rearrange("(p j) i -> p j i", j=PACK))
-            w2_raw[f, s] = raw
+            for start in range(c0, c1, HALF):
+                w2_raw[f, s, start // HALF] = raw[:, :, start - c0 : start - c0 + HALF]
+            if c1 - c0 == H:
+                w2_raw[f, s] = raw
 
         def load_dy(s):
             nc.sync.dma_start(dy_codes[s][:], dy_words[s].rearrange("p t d -> p (t d)").bitcast(I32))
@@ -104,15 +105,18 @@ def tile_moe_seb_none_kernel(
                 dy_plane[32 * q : 32 * q + 4 * PASSES, :].bitcast(I32),
                 dy_scales[:, 4 * q : 4 * q + 4, :].bitcast(I32),
             )
-        load_w2(0, 0)
+        load_w2(0, 0, 0, H)
         nc.scalar.dma_start(gate2_rows[0:GATE2_ROWS, 0:piece], gate2[0].rearrange("(r u) -> r u", u=piece))
         load_dy(1)
-        load_w2(0, 1)
-        for f in range(1, E):
+        load_w2(0, 1, 0, H)
+        for f in range(1, WHOLE):
             for s in range(PASSES):
-                load_w2(f, s)
-            if f == E - 2:
-                nc.sync.dma_start(list1[:], offs)
+                load_w2(f, s, 0, H)
+        nc.sync.dma_start(list1[:], offs)
+        units = [(f, half) for half in range(2) for f in range(WHOLE, E)]
+        for f, half in units:
+            for s in range(PASSES):
+                load_w2(f, s, half * HALF, (half + 1) * HALF)
         nc.sync.dma_start(gate1_rows[0:E, :], gate1[0].rearrange("(e u) -> e u", u=C))
         nc.sync.dma_start(w1_codes[:].bitcast(I32), w1t_words[:, 0].rearrange("e p b -> p e b").bitcast(I32))
         for q in range(QUADRANTS):
@@ -156,30 +160,36 @@ def tile_moe_seb_none_kernel(
 
         first_block = head.tile([P, P * PACK], BF16, name="first_block", align_bytes=64, offset=0)
 
+        def open_unit(f, half):
+            for s in range(PASSES):
+                grouped[f, s, half] = ring.tile([P, HALF * PACK], BF16, name="grouped", align_bytes=64)
+                w2_codes[f, s, half] = ring.tile([P, HALF], U32, name="w2_codes", align_bytes=64)
+                w2_plane[f, s, half] = ring.tile([P, HALF], U8, name="w2_plane", align_bytes=64)
+
         def rounded_columns(f, s, c0, c1):
-            tile = first_block if (f, s, c0) == (0, 1, 0) else grouped[f, s]
-            return tile[:, c0 * PACK : c1 * PACK]
+            tile = first_block if (f, s, c0) == (0, 1, 0) else grouped[f, s, c0 // HALF]
+            return tile[:, c0 % HALF * PACK : (c0 % HALF + c1 - c0) * PACK]
 
         def round_w2(engine_copy, f, s, c0, c1):
             engine_copy(
                 rounded_columns(f, s, c0, c1).rearrange("p (c i j) -> p c j i", i=RUN, j=PACK),
-                w2_raw[f, s][:, :, c0:c1].rearrange("p j (c i) -> p c j i", i=RUN),
+                w2_raw[f, s, c0 // HALF][:, :, c0 % HALF : c0 % HALF + c1 - c0].rearrange("p j (c i) -> p c j i", i=RUN),
             )
 
         def quantise_w2(f, s, first, end):
             nc.vector.quantize_mx(
-                out=w2_codes[f, s][:, first * P : end * P].bitcast(FP8X4),
-                scales=w2_plane[f, s][:, first * P : end * P],
+                out=w2_codes[f, s, first // 2][:, first % 2 * P : (first % 2 + end - first) * P].bitcast(FP8X4),
+                scales=w2_plane[f, s, first // 2][:, first % 2 * P : (first % 2 + end - first) * P],
                 in_=rounded_columns(f, s, first * P, end * P),
             )
 
         def second_layer_products(f, b, bank, place):
-            cols = slice(b * P, (b + 1) * P)
+            cols = slice(b % 2 * P, (b % 2 + 1) * P)
             for s in range(PASSES):
                 nc.tensor.matmul_mx(
                     out=bank[:, place, :],
-                    lhsT=w2_codes[f, s][:, cols].bitcast(FP8X4),
-                    lhsT_scale=w2_plane[f, s][:, cols],
+                    lhsT=w2_codes[f, s, b // 2][:, cols].bitcast(FP8X4),
+                    lhsT_scale=w2_plane[f, s, b // 2][:, cols],
                     rhs=g_codes[f, s].bitcast(FP8X4),
                     rhs_scale=g_plane[f][4 * s : P, :],
                     start=(s == 0),
@@ -193,8 +203,8 @@ def tile_moe_seb_none_kernel(
                 window = dc[first + n][:].indirect(entries(list2, f * C, C))
                 nc.vector.tensor_tensor(window, sums[:, n, :], gate2_all[:, f // 3, (f % 3) * C : (f % 3 + 1) * C], MULT)
 
-        def parked(f, s, count):
-            return w2_raw[f, s][:, 0:count, 0:C]
+        def parked(f, s, count, half=0):
+            return w2_raw[f, s, half][:, 0:count, 0:C]
 
         dc_slots = {}
 
@@ -203,11 +213,9 @@ def tile_moe_seb_none_kernel(
             for n in range(count):
                 dc_slots[first + n, b] = target[:, n * C : (n + 1) * C]
 
-        for f in range(E):
-            for s in range(PASSES):
-                grouped[f, s] = ring.tile([P, H * PACK], BF16, name="grouped%d" % s, align_bytes=64)
-                w2_codes[f, s] = ring.tile([P, H], U32, name="w2_codes%d" % s, align_bytes=64)
-                w2_plane[f, s] = ring.tile([P, H], U8, name="w2_plane%d" % s, align_bytes=64)
+        for f in range(WHOLE):
+            for half in range(2):
+                open_unit(f, half)
             end = H - P if f == 1 else H
             if end < H:
                 round_w2(nc.vector.tensor_copy, f, 0, end, H)
@@ -250,10 +258,23 @@ def tile_moe_seb_none_kernel(
                 second_layer_products(f, b, high_bank, b - 2)
             low_sums = ring.tile([P, 1, C], F32, name="low_sums")
             scatter_dc(f, 0, 1, low_sums[:])
-        scatter_dc(E - 1, 1, 1, keep.tile([P, 1, C], F32, name="second_sums")[:])
         early_slots = keep.tile([P, 2, 2 * C], F32, name="early_slots")
-        for b in range(2):
-            gather_dc(early_slots[:, b, :], b, 0, 2)
+        for n, (f, half) in enumerate(units):
+            open_unit(f, half)
+            for s in range(PASSES):
+                for b in range(2 * half, 2 * half + 2):
+                    round_w2(nc.scalar.copy, f, s, b * P, (b + 1) * P)
+                quantise_w2(f, s, 2 * half, 2 * half + 2)
+                if n == 0:
+                    scatter_dc(WHOLE - 1, 1 + s, 1 + s, parked(f, s, 1 + s, half))
+                elif s == 1:
+                    scatter_dc(units[n - 1][0], 2 * units[n - 1][1], 2, parked(f, s, 2, half))
+            if n > 0 and units[n - 1] == (E - 1, 0):
+                for b in range(2):
+                    gather_dc(early_slots[:, b, :], b, 0, 2)
+            bank = sums_bank()
+            for b in range(2):
+                second_layer_products(f, 2 * half + b, bank, b)
         last_sums = late.tile([P, 2, C], F32, name="last_sums", align_bytes=64, offset=0)
         scatter_dc(E - 1, 2, 2, last_sums[:])
 

@@ -113,11 +113,11 @@ def tile_moe_seb_none_kernel(
             for s in range(PASSES):
                 load_w2(f, s, 0, H)
         nc.sync.dma_start(list1[:], offs)
+        nc.sync.dma_start(gate1_rows[0:E, :], gate1[0].rearrange("(e u) -> e u", u=C))
         units = [(f, half) for half in range(2) for f in range(WHOLE, E)]
         for f, half in units:
             for s in range(PASSES):
                 load_w2(f, s, half * HALF, (half + 1) * HALF)
-        nc.sync.dma_start(gate1_rows[0:E, :], gate1[0].rearrange("(e u) -> e u", u=C))
         nc.sync.dma_start(w1_codes[:].bitcast(I32), w1t_words[:, 0].rearrange("e p b -> p e b").bitcast(I32))
         for q in range(QUADRANTS):
             nc.sync.dma_start(
@@ -258,13 +258,16 @@ def tile_moe_seb_none_kernel(
                 second_layer_products(f, b, high_bank, b - 2)
             low_sums = ring.tile([P, 1, C], F32, name="low_sums")
             scatter_dc(f, 0, 1, low_sums[:])
-        early_slots = keep.tile([P, 2, 2 * C], F32, name="early_slots")
+        early_slots = keep.tile([P, 3, 2 * C], F32, name="early_slots")
         for n, (f, half) in enumerate(units):
             open_unit(f, half)
             for s in range(PASSES):
                 for b in range(2 * half, 2 * half + 2):
                     round_w2(nc.scalar.copy, f, s, b * P, (b + 1) * P)
-                quantise_w2(f, s, 2 * half, 2 * half + 2)
+                    if (n, s) == (len(units) - 1, 1):
+                        quantise_w2(f, s, b, b + 1)
+                if (n, s) != (len(units) - 1, 1):
+                    quantise_w2(f, s, 2 * half, 2 * half + 2)
                 if n == 0:
                     scatter_dc(WHOLE - 1, 1 + s, 1 + s, parked(f, s, 1 + s, half))
                 elif s == 1:
@@ -272,11 +275,16 @@ def tile_moe_seb_none_kernel(
             if n > 0 and units[n - 1] == (E - 1, 0):
                 for b in range(2):
                     gather_dc(early_slots[:, b, :], b, 0, 2)
+                gather_dc(early_slots[:, 2, :], 0, 2, 2)
             bank = sums_bank()
-            for b in range(2):
-                second_layer_products(f, 2 * half + b, bank, b)
-        last_sums = late.tile([P, 2, C], F32, name="last_sums", align_bytes=64, offset=0)
-        scatter_dc(E - 1, 2, 2, last_sums[:])
+            if n < len(units) - 1:
+                for b in range(2):
+                    second_layer_products(f, 2 * half + b, bank, b)
+        second_layer_products(E - 1, 2, bank, 0)
+        second_layer_products(E - 1, 3, sums_bank(), 0)
+        scatter_dc(E - 1, 2, 1, keep.tile([P, 1, C], F32, name="third_sums")[:])
+        last_sums = late.tile([P, 1, C], F32, name="last_sums", align_bytes=64, offset=0)
+        scatter_dc(E - 1, 3, 1, last_sums[:])
 
         turn_gate(gate1_rows, gate1_cols, E)
         first_slots = keep.tile([P, 2 * C], F32, name="first_slots")
@@ -285,22 +293,24 @@ def tile_moe_seb_none_kernel(
         middle = late.tile([P, MIDDLE_BYTES // 4], F32, name="middle", align_bytes=64, offset=0)
         for b in range(2, BLOCKS):
             gather_dc(middle[:, b * C : (b + 1) * C], b, 1, 1)
-        for b in range(BLOCKS):
+        for b in range(1, BLOCKS):
             gather_dc(middle[:, (BLOCKS + 2 * b) * C : (BLOCKS + 2 * b + 2) * C], b, 2, 2)
         gather_dc(middle[:, 0 : 2 * C], 0, 4, 2)
 
         def quantise_da(e):
-            by_slot = turn_bank("by_slot")
-            for b in range(BLOCKS):
-                nc.tensor.transpose(by_slot[:, b, :], dc_slots[e, b], identity[:])
             offset = ROWS_AT + BLOCK_PAIR_BYTES + e * ROWS_STEP
             da_rows = late.tile([P, 2, P, 2], BF16, name="da_rows%d" % e, align_bytes=64, offset=offset)
-            nc.scalar.activation(
-                da_rows[:],
-                by_slot[:].rearrange("u b i -> u (b i)").rearrange("u (p h d) -> u h p d", h=2, d=2),
-                COPY,
-                scale=gate1_cols[:, e : e + 1],
-            )
+            parts = ((0, 2), (2, BLOCKS)) if e == 0 else ((0, BLOCKS),)
+            for first, end in parts:
+                by_slot = sums_bank() if end < BLOCKS else turn_bank("by_slot")
+                for b in range(first, end):
+                    nc.tensor.transpose(by_slot[:, b, :], dc_slots[e, b], identity[:])
+                nc.scalar.activation(
+                    da_rows[:, :, first * P // PACK : end * P // PACK, :],
+                    by_slot[:, first:end, :].rearrange("u b i -> u (b i)").rearrange("u (p h d) -> u h p d", h=2, d=2),
+                    COPY,
+                    scale=gate1_cols[:, e : e + 1],
+                )
             pairs = da_rows[:].rearrange("u h p d -> u (h p d)").bitcast(F32)
             by_row = turn_bank("by_row")
             for h in range(2):

@@ -24,18 +24,19 @@ BLOCKS = H // P
 K_BLOCKS = K // P
 QUADRANTS = 4
 PER_COLUMN = 16
-PASS_BYTES = PACK * H * 4
+HALF = H // 2
 RUN = 4
 BLOCK_PAIR_BYTES = 2 * C * 4
 
-SHARE = 64
+DMA_ALIGN = 256
+
 WHOLE = 3
-HALF = H // 2
-CUTS = (0, 2, E)
+SHARE = 64
+EARLY = 2
 HELD_FROM = 3
 GATE2_ROWS = 8
 TWO_BEHIND_FROM = 3
-RING_DEPTH = 8
+RING_DEPTH = 2 * 2 * PASSES
 
 ROWS_STEP = 3 * BLOCK_PAIR_BYTES // 2
 MIDDLE_BYTES = 6 * BLOCK_PAIR_BYTES
@@ -65,17 +66,17 @@ def tile_moe_seb_none_kernel(
 
         list1 = keep.tile([P, T // PER_COLUMN], U16, name="list1")
         list2 = keep.tile([P, T // PER_COLUMN], U16, name="list2")
-        dy_plane = keep.tile([P, T], U8, name="dy_plane", align_bytes=256)
-        w1_plane = keep.tile([P, E, K], U8, name="w1_plane", align_bytes=256)
-        w1_codes = keep.tile([P, E, 2 * K], U8, name="w1_codes", align_bytes=256)
+        dy_plane = keep.tile([P, T], U8, name="dy_plane", align_bytes=DMA_ALIGN)
+        w1_plane = keep.tile([P, E, K], U8, name="w1_plane", align_bytes=DMA_ALIGN)
+        w1_codes = keep.tile([P, E, 2 * K], U8, name="w1_codes", align_bytes=DMA_ALIGN)
         gate1_rows = keep.tile([P, C], F32, name="gate1_rows")
         gate2_rows = keep.tile([P, C], F32, name="gate2_rows")
         gate1_cols = keep.tile([P, E], F32, name="gate1_cols")
         gate2_cols = keep.tile([P, GATE2_ROWS], F32, name="gate2_cols")
         identity = keep.tile([P, P], F32, name="identity")
-        dy_codes = [keep.tile([P, T], I32, name="dy_codes%d" % s, align_bytes=256) for s in range(PASSES)]
+        dy_codes = [keep.tile([P, T], I32, name="dy_codes%d" % s, align_bytes=DMA_ALIGN) for s in range(PASSES)]
         dc = [keep.tile([P, T], F32, name="dc%d" % b) for b in range(BLOCKS)]
-        dx = [keep.tile([P, T], F32, name="dx%d" % b, align_bytes=256) for b in range(K_BLOCKS)]
+        dx = [keep.tile([P, T], F32, name="dx%d" % b, align_bytes=DMA_ALIGN) for b in range(K_BLOCKS)]
 
         nc.vector.memset(dy_plane[:].bitcast(I32), 0)
         nc.gpsimd.memset(gate2_rows[:], 0.0)
@@ -86,13 +87,12 @@ def tile_moe_seb_none_kernel(
         w2_raw = {}
 
         def load_w2(f, s, c0, c1):
-            raw = keep.tile([P, PACK, c1 - c0], F32, name="w2_raw%d_%d_%d" % (f, s, c0), align_bytes=256)
+            raw = keep.tile([P, PACK, c1 - c0], F32, name="w2_raw%d_%d_%d" % (f, s, c0), align_bytes=DMA_ALIGN)
             rows = w2t[f, s * P * PACK : (s + 1) * P * PACK, c0:c1]
             nc.sync.dma_start(raw[:], rows.rearrange("(p j) i -> p j i", j=PACK))
             for start in range(c0, c1, HALF):
                 w2_raw[f, s, start // HALF] = raw[:, :, start - c0 : start - c0 + HALF]
-            if c1 - c0 == H:
-                w2_raw[f, s] = raw
+            return raw
 
         def load_dy(s):
             nc.sync.dma_start(dy_codes[s][:], dy_words[s].rearrange("p t d -> p (t d)").bitcast(I32))
@@ -105,7 +105,7 @@ def tile_moe_seb_none_kernel(
                 dy_plane[32 * q : 32 * q + 4 * PASSES, :].bitcast(I32),
                 dy_scales[:, 4 * q : 4 * q + 4, :].bitcast(I32),
             )
-        load_w2(0, 0, 0, H)
+        first_load = load_w2(0, 0, 0, H)
         nc.scalar.dma_start(gate2_rows[0:GATE2_ROWS, 0:piece], gate2[0].rearrange("(r u) -> r u", u=piece))
         load_dy(1)
         load_w2(0, 1, 0, H)
@@ -150,9 +150,9 @@ def tile_moe_seb_none_kernel(
             parts = gather_dy(dy_codes[s][:].bitcast(U32), U32, "g_codes%d" % s, first, end, **place)
             g_codes.update({(f, s): part for f, part in parts.items()})
 
-        for first, end in zip(CUTS, CUTS[1:]):
+        for first, end in ((0, EARLY), (EARLY, E)):
             gather_words(0, first, end)
-        for first, end in zip(CUTS, CUTS[1:]):
+        for first, end in ((0, EARLY), (EARLY, E)):
             g_plane.update(gather_dy(dy_plane[:], U8, "g_plane", first, end))
         gather_words(1, 0, HELD_FROM)
 
@@ -171,15 +171,17 @@ def tile_moe_seb_none_kernel(
             return tile[:, c0 % HALF * PACK : (c0 % HALF + c1 - c0) * PACK]
 
         def round_w2(engine_copy, f, s, c0, c1):
+            raw = w2_raw[f, s, c0 // HALF][:, :, c0 % HALF : c0 % HALF + c1 - c0]
             engine_copy(
                 rounded_columns(f, s, c0, c1).rearrange("p (c i j) -> p c j i", i=RUN, j=PACK),
-                w2_raw[f, s, c0 // HALF][:, :, c0 % HALF : c0 % HALF + c1 - c0].rearrange("p j (c i) -> p c j i", i=RUN),
+                raw.rearrange("p j (c i) -> p c j i", i=RUN),
             )
 
         def quantise_w2(f, s, first, end):
+            cols = slice(first % 2 * P, (first % 2 + end - first) * P)
             nc.vector.quantize_mx(
-                out=w2_codes[f, s, first // 2][:, first % 2 * P : (first % 2 + end - first) * P].bitcast(FP8X4),
-                scales=w2_plane[f, s, first // 2][:, first % 2 * P : (first % 2 + end - first) * P],
+                out=w2_codes[f, s, first // 2][:, cols].bitcast(FP8X4),
+                scales=w2_plane[f, s, first // 2][:, cols],
                 in_=rounded_columns(f, s, first * P, end * P),
             )
 
@@ -199,9 +201,10 @@ def tile_moe_seb_none_kernel(
 
         def scatter_dc(f, first, count, sums):
             nc.scalar.copy(sums, banks[f, first][:, 0:count, :])
+            row, place = divmod(f, E // 2)
             for n in range(count):
                 window = dc[first + n][:].indirect(entries(list2, f * C, C))
-                nc.vector.tensor_tensor(window, sums[:, n, :], gate2_all[:, f // 3, (f % 3) * C : (f % 3 + 1) * C], MULT)
+                nc.vector.tensor_tensor(window, sums[:, n, :], gate2_all[:, row, place * C : (place + 1) * C], MULT)
 
         def parked(f, s, count, half=0):
             return w2_raw[f, s, half][:, 0:count, 0:C]
@@ -216,57 +219,62 @@ def tile_moe_seb_none_kernel(
         for f in range(WHOLE):
             for half in range(2):
                 open_unit(f, half)
-            end = H - P if f == 1 else H
-            if end < H:
-                round_w2(nc.vector.tensor_copy, f, 0, end, H)
+            scalar_end = H - P if f == 1 else H
+            if scalar_end < H:
+                round_w2(nc.vector.tensor_copy, f, 0, scalar_end, H)
             round_w2(nc.scalar.copy, f, 0, 0, P)
             round_w2(nc.scalar.copy, f, 0, P, 2 * P)
             quantise_w2(f, 0, 0, 2)
-            if f > 0:
-                scatter_dc(f - 1, 1, 1, parked(f, 0, 1))
             if f == 0:
                 round_w2(nc.scalar.copy, f, 0, 2 * P, 3 * P)
                 round_w2(nc.scalar.copy, f, 0, 3 * P, H)
-            else:
-                round_w2(nc.scalar.copy, f, 0, 2 * P, end)
-            quantise_w2(f, 0, 2, BLOCKS)
-            if f == 0:
-                gate2_all = w2_raw[0, 0][:, 0:2, 0 : T // 2]
+                quantise_w2(f, 0, 2, BLOCKS)
+                gate2_all = first_load[:, 0:2, 0 : T // 2]
                 for n, gate2_bank in enumerate(gate2_banks):
                     spread = gate2_all[:, n, :].rearrange("p (r u) -> p r u", u=piece)
                     nc.scalar.copy(spread, gate2_bank[:, :, 0:piece])
-
-            if f == 0:
                 round_w2(nc.vector.tensor_copy, f, 1, 0, P)
                 quantise_w2(f, 1, 0, 1)
                 gather_words(1, HELD_FROM, E, pool=head, offset=0)
                 round_w2(nc.scalar.copy, f, 1, P, 2 * P)
             else:
-                round_w2(nc.vector.tensor_copy, f, 1, 2 * P - SHARE, 2 * P)
+                scatter_dc(f - 1, 1, 1, parked(f, 0, 1))
+                round_w2(nc.scalar.copy, f, 0, 2 * P, scalar_end)
+                quantise_w2(f, 0, 2, BLOCKS)
+                round_w2(nc.vector.tensor_copy, f, 1, HALF - SHARE, HALF)
+                if scalar_end < H:
+                    round_w2(nc.vector.tensor_copy, f, 1, scalar_end, H)
                 round_w2(nc.scalar.copy, f, 1, 0, P)
                 quantise_w2(f, 1, 0, 1)
-                round_w2(nc.scalar.copy, f, 1, P, 2 * P - SHARE)
+                round_w2(nc.scalar.copy, f, 1, P, HALF - SHARE)
             second_layer_products(f, 0, sums_bank(), 0)
             quantise_w2(f, 1, 1, 2)
             second_layer_products(f, 1, sums_bank(), 0)
             if f > 0:
                 scatter_dc(f - 1, 2, 2, parked(f, 1, 2))
-            round_w2(nc.scalar.copy, f, 1, 2 * P, H)
+            round_w2(nc.scalar.copy, f, 1, 2 * P, scalar_end)
             quantise_w2(f, 1, 2, BLOCKS)
             high_bank = sums_bank()
             for b in range(2, BLOCKS):
                 second_layer_products(f, b, high_bank, b - 2)
             low_sums = ring.tile([P, 1, C], F32, name="low_sums")
             scatter_dc(f, 0, 1, low_sums[:])
+
         early_slots = keep.tile([P, 3, 2 * C], F32, name="early_slots")
         for n, (f, half) in enumerate(units):
             open_unit(f, half)
             for s in range(PASSES):
-                for b in range(2 * half, 2 * half + 2):
-                    round_w2(nc.scalar.copy, f, s, b * P, (b + 1) * P)
-                    if (n, s) == (len(units) - 1, 1):
+                helped = s == 1 and half == 0 and n > 0
+                by_block = helped or (n, s) == (len(units) - 1, 1)
+                if helped:
+                    round_w2(nc.vector.tensor_copy, f, s, HALF - SHARE, HALF)
+                blocks_a_copy = 1 if n == 0 or s == 1 else 2
+                for b in range(2 * half, 2 * half + 2, blocks_a_copy):
+                    cut = SHARE if helped and b == 1 else 0
+                    round_w2(nc.scalar.copy, f, s, b * P, (b + blocks_a_copy) * P - cut)
+                    if by_block:
                         quantise_w2(f, s, b, b + 1)
-                if (n, s) != (len(units) - 1, 1):
+                if not by_block:
                     quantise_w2(f, s, 2 * half, 2 * half + 2)
                 if n == 0:
                     scatter_dc(WHOLE - 1, 1 + s, 1 + s, parked(f, s, 1 + s, half))

@@ -26,21 +26,10 @@ QUADRANTS = 4
 PER_COLUMN = 16
 HALF = H // 2
 RUN = 4
-BLOCK_PAIR_BYTES = 2 * C * 4
-
 DMA_ALIGN = 256
-
-WHOLE = 3
-SHARE = 64
-EARLY = 2
-HELD_FROM = 3
 GATE2_ROWS = 8
-TWO_BEHIND_FROM = 3
-RING_DEPTH = 2 * 2 * PASSES
-
-ROWS_STEP = 3 * BLOCK_PAIR_BYTES // 2
-MIDDLE_BYTES = 6 * BLOCK_PAIR_BYTES
-ROWS_AT = MIDDLE_BYTES + BLOCK_PAIR_BYTES
+SHARE = 128
+EARLY = 2
 
 
 def entries(offsets, first, count):
@@ -53,16 +42,14 @@ def tile_moe_seb_none_kernel(
     nc = tc.nc
     with ExitStack() as ctx:
         keep = ctx.enter_context(tc.tile_pool(name="keep", bufs=1))
-        head = ctx.enter_context(tc.tile_pool(name="head", bufs=1))
-        late = ctx.enter_context(tc.tile_pool(name="late", bufs=1))
-        ring = ctx.enter_context(tc.tile_pool(name="ring", bufs=RING_DEPTH))
+        ring = ctx.enter_context(tc.tile_pool(name="ring", bufs=4))
         psum = ctx.enter_context(tc.psum_pool(name="psum", bufs=1))
 
-        def sums_bank():
-            return psum.tile([P, BLOCKS, C], F32, name="sums_bank", bufs=3)
+        def wide_bank():
+            return psum.tile([P, BLOCKS, C], F32, name="wide_bank", bufs=6)
 
-        def turn_bank(name):
-            return psum.tile([P, BLOCKS, C], F32, name=name, bufs=2)
+        def row_bank():
+            return psum.tile([P, BLOCKS, C], F32, name="row_bank", bufs=2)
 
         list1 = keep.tile([P, T // PER_COLUMN], U16, name="list1")
         list2 = keep.tile([P, T // PER_COLUMN], U16, name="list2")
@@ -73,6 +60,7 @@ def tile_moe_seb_none_kernel(
         gate2_rows = keep.tile([P, C], F32, name="gate2_rows")
         gate1_cols = keep.tile([P, E], F32, name="gate1_cols")
         gate2_cols = keep.tile([P, GATE2_ROWS], F32, name="gate2_cols")
+        gate2_all = keep.tile([P, T], F32, name="gate2_all")
         identity = keep.tile([P, P], F32, name="identity")
         dy_codes = [keep.tile([P, T], I32, name="dy_codes%d" % s, align_bytes=DMA_ALIGN) for s in range(PASSES)]
         dc = [keep.tile([P, T], F32, name="dc%d" % b) for b in range(BLOCKS)]
@@ -86,38 +74,28 @@ def tile_moe_seb_none_kernel(
 
         w2_raw = {}
 
-        def load_w2(f, s, c0, c1):
-            raw = keep.tile([P, PACK, c1 - c0], F32, name="w2_raw%d_%d_%d" % (f, s, c0), align_bytes=DMA_ALIGN)
-            rows = w2t[f, s * P * PACK : (s + 1) * P * PACK, c0:c1]
+        def load_w2(f, s):
+            raw = keep.tile([P, PACK, H], F32, name="w2_raw%d_%d" % (f, s), align_bytes=DMA_ALIGN)
+            rows = w2t[f, s * P * PACK : (s + 1) * P * PACK, :]
             nc.sync.dma_start(raw[:], rows.rearrange("(p j) i -> p j i", j=PACK))
-            for start in range(c0, c1, HALF):
-                w2_raw[f, s, start // HALF] = raw[:, :, start - c0 : start - c0 + HALF]
-            return raw
-
-        def load_dy(s):
-            nc.sync.dma_start(dy_codes[s][:], dy_words[s].rearrange("p t d -> p (t d)").bitcast(I32))
+            w2_raw[f, s] = raw
 
         piece = T // GATE2_ROWS
         nc.sync.dma_start(list2[:], offs2)
-        load_dy(0)
+        nc.sync.dma_start(dy_codes[0][:], dy_words[0].rearrange("p t d -> p (t d)").bitcast(I32))
         for q in range(QUADRANTS):
             nc.sync.dma_start(
                 dy_plane[32 * q : 32 * q + 4 * PASSES, :].bitcast(I32),
                 dy_scales[:, 4 * q : 4 * q + 4, :].bitcast(I32),
             )
-        first_load = load_w2(0, 0, 0, H)
+        nc.sync.dma_start(dy_codes[1][:], dy_words[1].rearrange("p t d -> p (t d)").bitcast(I32))
         nc.scalar.dma_start(gate2_rows[0:GATE2_ROWS, 0:piece], gate2[0].rearrange("(r u) -> r u", u=piece))
-        load_dy(1)
-        load_w2(0, 1, 0, H)
-        for f in range(1, WHOLE):
+        for f in range(E):
+            if f == E - 1:
+                nc.sync.dma_start(list1[:], offs)
+                nc.sync.dma_start(gate1_rows[0:E, :], gate1[0].rearrange("(e u) -> e u", u=C))
             for s in range(PASSES):
-                load_w2(f, s, 0, H)
-        nc.sync.dma_start(list1[:], offs)
-        nc.sync.dma_start(gate1_rows[0:E, :], gate1[0].rearrange("(e u) -> e u", u=C))
-        units = [(f, half) for half in range(2) for f in range(WHOLE, E)]
-        for f, half in units:
-            for s in range(PASSES):
-                load_w2(f, s, half * HALF, (half + 1) * HALF)
+                load_w2(f, s)
         nc.sync.dma_start(w1_codes[:].bitcast(I32), w1t_words[:, 0].rearrange("e p b -> p e b").bitcast(I32))
         for q in range(QUADRANTS):
             nc.sync.dma_start(
@@ -126,241 +104,189 @@ def tile_moe_seb_none_kernel(
             )
 
         def turn_gate(gate_rows, gate_cols, count):
-            bank = turn_bank("by_row")
+            bank = row_bank()
             nc.tensor.transpose(bank[:, 0, :], gate_rows[:], identity[:])
             nc.scalar.copy(gate_cols[:], bank[:, 0, 0:count])
 
         turn_gate(gate2_rows, gate2_cols, GATE2_ROWS)
-        gate2_banks = []
         for first in range(0, GATE2_ROWS, BLOCKS):
-            bank = turn_bank("by_slot")
+            bank = wide_bank()
             for n in range(BLOCKS):
                 column = gate2_cols[:, first + n : first + n + 1]
                 nc.tensor.transpose(bank[:, n, :], column.to_broadcast([P, P]), identity[:])
-            gate2_banks.append(bank)
+            spread = gate2_all[:, first * piece : (first + BLOCKS) * piece].rearrange("p (r u) -> p r u", u=piece)
+            nc.scalar.copy(spread, bank[:, :, 0:piece])
 
         g_codes, g_plane = {}, {}
 
-        def gather_dy(window, dtype, name, first, end, pool=keep, **place):
-            tile = pool.tile([P, (end - first) * C], dtype, name="%s_%d" % (name, first), align_bytes=64, **place)
+        def gather_dy(window, dtype, name, first, end):
+            tile = keep.tile([P, (end - first) * C], dtype, name="%s_%d" % (name, first), align_bytes=64)
             nc.vector.tensor_copy(tile[:], window.indirect(entries(list2, first * C, (end - first) * C)))
             return {f: tile[:, (f - first) * C : (f - first + 1) * C] for f in range(first, end)}
 
-        def gather_words(s, first, end, **place):
-            parts = gather_dy(dy_codes[s][:].bitcast(U32), U32, "g_codes%d" % s, first, end, **place)
-            g_codes.update({(f, s): part for f, part in parts.items()})
+        def gather_words(s):
+            for first, end in ((0, EARLY), (EARLY, E)):
+                parts = gather_dy(dy_codes[s][:].bitcast(U32), U32, "g_codes%d" % s, first, end)
+                g_codes.update({(f, s): part for f, part in parts.items()})
 
-        for first, end in ((0, EARLY), (EARLY, E)):
-            gather_words(0, first, end)
+        gather_words(0)
         for first, end in ((0, EARLY), (EARLY, E)):
             g_plane.update(gather_dy(dy_plane[:], U8, "g_plane", first, end))
-        gather_words(1, 0, HELD_FROM)
+        gather_words(1)
 
         grouped, w2_codes, w2_plane, banks = {}, {}, {}, {}
 
-        first_block = head.tile([P, P * PACK], BF16, name="first_block", align_bytes=64, offset=0)
-
-        def open_unit(f, half):
-            for s in range(PASSES):
-                grouped[f, s, half] = ring.tile([P, HALF * PACK], BF16, name="grouped", align_bytes=64)
-                w2_codes[f, s, half] = ring.tile([P, HALF], U32, name="w2_codes", align_bytes=64)
-                w2_plane[f, s, half] = ring.tile([P, HALF], U8, name="w2_plane", align_bytes=64)
-
-        def rounded_columns(f, s, c0, c1):
-            tile = first_block if (f, s, c0) == (0, 1, 0) else grouped[f, s, c0 // HALF]
-            return tile[:, c0 % HALF * PACK : (c0 % HALF + c1 - c0) * PACK]
+        def open_pass(f, s):
+            grouped[f, s] = ring.tile([P, H * PACK], BF16, name="grouped", align_bytes=64)
+            w2_codes[f, s] = ring.tile([P, H], U32, name="w2_codes", align_bytes=64)
+            w2_plane[f, s] = ring.tile([P, H], U8, name="w2_plane", align_bytes=64)
 
         def round_w2(engine_copy, f, s, c0, c1):
-            raw = w2_raw[f, s, c0 // HALF][:, :, c0 % HALF : c0 % HALF + c1 - c0]
             engine_copy(
-                rounded_columns(f, s, c0, c1).rearrange("p (c i j) -> p c j i", i=RUN, j=PACK),
-                raw.rearrange("p j (c i) -> p c j i", i=RUN),
+                grouped[f, s][:, c0 * PACK : c1 * PACK].rearrange("p (c i j) -> p c j i", i=RUN, j=PACK),
+                w2_raw[f, s][:, :, c0:c1].rearrange("p j (c i) -> p c j i", i=RUN),
             )
 
-        def quantise_w2(f, s, first, end):
-            cols = slice(first % 2 * P, (first % 2 + end - first) * P)
+        def quantise_w2(f, s, c0, c1):
             nc.vector.quantize_mx(
-                out=w2_codes[f, s, first // 2][:, cols].bitcast(FP8X4),
-                scales=w2_plane[f, s, first // 2][:, cols],
-                in_=rounded_columns(f, s, first * P, end * P),
+                out=w2_codes[f, s][:, c0:c1].bitcast(FP8X4),
+                scales=w2_plane[f, s][:, c0:c1],
+                in_=grouped[f, s][:, c0 * PACK : c1 * PACK],
             )
 
-        def second_layer_products(f, b, bank, place):
-            cols = slice(b % 2 * P, (b % 2 + 1) * P)
+        def second_layer_products(f, first, end):
+            bank = wide_bank()
+            for b in range(first, end):
+                cols = slice(b * P, (b + 1) * P)
+                for s in range(PASSES):
+                    nc.tensor.matmul_mx(
+                        out=bank[:, b, :],
+                        lhsT=w2_codes[f, s][:, cols].bitcast(FP8X4),
+                        lhsT_scale=w2_plane[f, s][:, cols],
+                        rhs=g_codes[f, s].bitcast(FP8X4),
+                        rhs_scale=g_plane[f][4 * s : P, :],
+                        start=(s == 0),
+                        stop=(s == PASSES - 1),
+                    )
+            return bank
+
+        def gate_sums(f, bank, sums, first, end):
+            gate = gate2_all[:, f * C : (f + 1) * C].unsqueeze(1).to_broadcast([P, end - first, C])
+            nc.vector.tensor_tensor(sums[:, first:end, :], bank[:, first:end, :], gate, MULT)
+
+        def scalar_move(target, source):
+            nc.scalar.activation(target, source, COPY)
+
+        def scatter_dc(move, f, b, sums):
+            move(dc[b][:].indirect(entries(list2, f * C, C)), sums[:, b, :])
+
+        for f in range(E):
             for s in range(PASSES):
-                nc.tensor.matmul_mx(
-                    out=bank[:, place, :],
-                    lhsT=w2_codes[f, s, b // 2][:, cols].bitcast(FP8X4),
-                    lhsT_scale=w2_plane[f, s, b // 2][:, cols],
-                    rhs=g_codes[f, s].bitcast(FP8X4),
-                    rhs_scale=g_plane[f][4 * s : P, :],
-                    start=(s == 0),
-                    stop=(s == PASSES - 1),
-                )
-            banks[f, b] = bank
-
-        def scatter_dc(f, first, count, sums):
-            nc.scalar.copy(sums, banks[f, first][:, 0:count, :])
-            row, place = divmod(f, E // 2)
-            for n in range(count):
-                window = dc[first + n][:].indirect(entries(list2, f * C, C))
-                nc.vector.tensor_tensor(window, sums[:, n, :], gate2_all[:, row, place * C : (place + 1) * C], MULT)
-
-        def parked(f, s, count, half=0):
-            return w2_raw[f, s, half][:, 0:count, 0:C]
-
-        dc_slots = {}
-
-        def gather_dc(target, b, first, count):
-            nc.vector.tensor_copy(target, dc[b][:].indirect(entries(list1, first * C, count * C)))
-            for n in range(count):
-                dc_slots[first + n, b] = target[:, n * C : (n + 1) * C]
-
-        for f in range(WHOLE):
-            for half in range(2):
-                open_unit(f, half)
-            scalar_end = H - P if f == 1 else H
-            if scalar_end < H:
-                round_w2(nc.vector.tensor_copy, f, 0, scalar_end, H)
-            round_w2(nc.scalar.copy, f, 0, 0, P)
-            round_w2(nc.scalar.copy, f, 0, P, 2 * P)
-            quantise_w2(f, 0, 0, 2)
+                open_pass(f, s)
             if f == 0:
-                round_w2(nc.scalar.copy, f, 0, 2 * P, 3 * P)
-                round_w2(nc.scalar.copy, f, 0, 3 * P, H)
-                quantise_w2(f, 0, 2, BLOCKS)
-                gate2_all = first_load[:, 0:2, 0 : T // 2]
-                for n, gate2_bank in enumerate(gate2_banks):
-                    spread = gate2_all[:, n, :].rearrange("p (r u) -> p r u", u=piece)
-                    nc.scalar.copy(spread, gate2_bank[:, :, 0:piece])
-                round_w2(nc.vector.tensor_copy, f, 1, 0, P)
-                quantise_w2(f, 1, 0, 1)
-                gather_words(1, HELD_FROM, E, pool=head, offset=0)
-                round_w2(nc.scalar.copy, f, 1, P, 2 * P)
+                round_w2(nc.scalar.copy, f, 0, 0, HALF)
+                round_w2(nc.scalar.copy, f, 0, HALF, H)
+                quantise_w2(f, 0, 0, HALF)
+                quantise_w2(f, 0, HALF, H)
+                round_w2(nc.vector.tensor_copy, f, 1, 0, HALF)
+                round_w2(nc.scalar.copy, f, 1, HALF, H)
             else:
-                scatter_dc(f - 1, 1, 1, parked(f, 0, 1))
-                round_w2(nc.scalar.copy, f, 0, 2 * P, scalar_end)
-                quantise_w2(f, 0, 2, BLOCKS)
-                round_w2(nc.vector.tensor_copy, f, 1, HALF - SHARE, HALF)
-                if scalar_end < H:
-                    round_w2(nc.vector.tensor_copy, f, 1, scalar_end, H)
-                round_w2(nc.scalar.copy, f, 1, 0, P)
-                quantise_w2(f, 1, 0, 1)
-                round_w2(nc.scalar.copy, f, 1, P, HALF - SHARE)
-            second_layer_products(f, 0, sums_bank(), 0)
-            quantise_w2(f, 1, 1, 2)
-            second_layer_products(f, 1, sums_bank(), 0)
-            if f > 0:
-                scatter_dc(f - 1, 2, 2, parked(f, 1, 2))
-            round_w2(nc.scalar.copy, f, 1, 2 * P, scalar_end)
-            quantise_w2(f, 1, 2, BLOCKS)
-            high_bank = sums_bank()
-            for b in range(2, BLOCKS):
-                second_layer_products(f, b, high_bank, b - 2)
-            low_sums = ring.tile([P, 1, C], F32, name="low_sums")
-            scatter_dc(f, 0, 1, low_sums[:])
-
-        early_slots = keep.tile([P, 3, 2 * C], F32, name="early_slots")
-        for n, (f, half) in enumerate(units):
-            open_unit(f, half)
-            for s in range(PASSES):
-                helped = s == 1 and half == 0 and n > 0
-                by_block = helped or (n, s) == (len(units) - 1, 1)
-                if helped:
-                    round_w2(nc.vector.tensor_copy, f, s, HALF - SHARE, HALF)
-                blocks_a_copy = 1 if n == 0 or s == 1 else 2
-                for b in range(2 * half, 2 * half + 2, blocks_a_copy):
-                    cut = SHARE if helped and b == 1 else 0
-                    round_w2(nc.scalar.copy, f, s, b * P, (b + blocks_a_copy) * P - cut)
-                    if by_block:
-                        quantise_w2(f, s, b, b + 1)
-                if not by_block:
-                    quantise_w2(f, s, 2 * half, 2 * half + 2)
-                if n == 0:
-                    scatter_dc(WHOLE - 1, 1 + s, 1 + s, parked(f, s, 1 + s, half))
-                elif s == 1:
-                    scatter_dc(units[n - 1][0], 2 * units[n - 1][1], 2, parked(f, s, 2, half))
-            if n > 0 and units[n - 1] == (E - 1, 0):
-                for b in range(2):
-                    gather_dc(early_slots[:, b, :], b, 0, 2)
-                gather_dc(early_slots[:, 2, :], 0, 2, 2)
-            bank = sums_bank()
-            if n < len(units) - 1:
-                for b in range(2):
-                    second_layer_products(f, 2 * half + b, bank, b)
-        second_layer_products(E - 1, 2, bank, 0)
-        second_layer_products(E - 1, 3, sums_bank(), 0)
-        scatter_dc(E - 1, 2, 1, keep.tile([P, 1, C], F32, name="third_sums")[:])
-        last_sums = late.tile([P, 1, C], F32, name="last_sums", align_bytes=64, offset=0)
-        scatter_dc(E - 1, 3, 1, last_sums[:])
+                round_w2(nc.scalar.copy, f, 0, H - SHARE, H)
+                round_w2(nc.vector.tensor_copy, f, 0, 0, P)
+                round_w2(nc.vector.tensor_copy, f, 0, P, H - SHARE)
+                sums = w2_raw[f, 0][:, :, 0:C]
+                gate_sums(f - 1, banks[f - 1], sums, 0, BLOCKS)
+                for b in range(BLOCKS):
+                    scatter_dc(scalar_move, f - 1, b, sums)
+                quantise_w2(f, 0, 0, H)
+                round_w2(nc.vector.tensor_copy, f, 1, 0, HALF)
+                round_w2(nc.vector.tensor_copy, f, 1, HALF, H)
+            quantise_w2(f, 1, 0, HALF)
+            quantise_w2(f, 1, HALF, H)
+            if f < E - 1:
+                banks[f] = second_layer_products(f, 0, BLOCKS)
+        last_sums = keep.tile([P, BLOCKS, C], F32, name="last_sums")
+        for first, move in ((0, scalar_move), (2, nc.vector.tensor_copy)):
+            gate_sums(E - 1, second_layer_products(E - 1, first, first + 2), last_sums, first, first + 2)
+            for b in range(first, first + 2):
+                scatter_dc(move, E - 1, b, last_sums)
 
         turn_gate(gate1_rows, gate1_cols, E)
-        first_slots = keep.tile([P, 2 * C], F32, name="first_slots")
-        for b in range(2, BLOCKS):
-            gather_dc(first_slots[:, (b - 2) * C : (b - 1) * C], b, 0, 1)
-        middle = late.tile([P, MIDDLE_BYTES // 4], F32, name="middle", align_bytes=64, offset=0)
-        for b in range(2, BLOCKS):
-            gather_dc(middle[:, b * C : (b + 1) * C], b, 1, 1)
-        for b in range(1, BLOCKS):
-            gather_dc(middle[:, (BLOCKS + 2 * b) * C : (BLOCKS + 2 * b + 2) * C], b, 2, 2)
-        gather_dc(middle[:, 0 : 2 * C], 0, 4, 2)
 
-        def quantise_da(e):
-            offset = ROWS_AT + BLOCK_PAIR_BYTES + e * ROWS_STEP
-            da_rows = late.tile([P, 2, P, 2], BF16, name="da_rows%d" % e, align_bytes=64, offset=offset)
-            parts = ((0, 2), (2, BLOCKS)) if e == 0 else ((0, BLOCKS),)
-            for first, end in parts:
-                by_slot = sums_bank() if end < BLOCKS else turn_bank("by_slot")
-                for b in range(first, end):
+        def vector_scale(target, source, factor):
+            nc.vector.tensor_scalar(target, source, factor, None, MULT)
+
+        def scalar_scale(target, source, factor):
+            nc.scalar.activation(target, source, COPY, scale=factor)
+
+        lanes = (
+            (nc.vector.tensor_copy, nc.vector.tensor_copy, vector_scale, (0, 1, 2), (2, 3, 0, 1)),
+            (scalar_move, nc.scalar.copy, scalar_scale, (5, 4, 3), (0, 1, 2, 3)),
+        )
+        dc_slots = {}
+        for move, copy, scale, experts, blocks in lanes:
+            first = min(experts)
+            for b in blocks:
+                slots = keep.tile([P, len(experts) * C], F32, name="slots%d_%d" % (first, b))
+                for e in experts:
+                    dc_slots[e, b] = slots[:, (e - first) * C : (e - first + 1) * C]
+                if b == blocks[-1]:
+                    for e in experts:
+                        move(dc_slots[e, b], dc[b][:].indirect(entries(list1, e * C, C)))
+                else:
+                    move(slots[:], dc[b][:].indirect(entries(list1, first * C, len(experts) * C)))
+
+        da_rows, da, da_mx = {}, {}, {}
+        for n in range(E // 2):
+            for move, copy, scale, experts, blocks in lanes:
+                e = experts[n]
+                by_slot = wide_bank()
+                for b in blocks:
                     nc.tensor.transpose(by_slot[:, b, :], dc_slots[e, b], identity[:])
-                nc.scalar.activation(
-                    da_rows[:, :, first * P // PACK : end * P // PACK, :],
-                    by_slot[:, first:end, :].rearrange("u b i -> u (b i)").rearrange("u (p h d) -> u h p d", h=2, d=2),
-                    COPY,
-                    scale=gate1_cols[:, e : e + 1],
+                da_rows[e] = keep.tile([P, 2, P, 2], BF16, name="da_rows%d" % e, align_bytes=64)
+                scale(
+                    da_rows[e][:],
+                    by_slot[:].rearrange("u b i -> u (b i)").rearrange("u (p h d) -> u h p d", h=2, d=2),
+                    gate1_cols[:, e : e + 1],
                 )
-            pairs = da_rows[:].rearrange("u h p d -> u (h p d)").bitcast(F32)
-            by_row = turn_bank("by_row")
-            for h in range(2):
-                nc.tensor.transpose(by_row[:, h, :], pairs[:, h * P : (h + 1) * P], identity[:])
-            da = ring.tile([P, C * PACK], BF16, name="da", align_bytes=64)
-            nc.scalar.copy(
-                da[:].bitcast(F32).rearrange("p (u h) -> p u h", h=2), by_row[:, 0:2, :].rearrange("p h u -> p u h")
-            )
-            da_codes = ring.tile([P, C], U32, name="da_codes", align_bytes=64)
-            da_plane = ring.tile([P, C], U8, name="da_plane", align_bytes=64)
-            nc.vector.quantize_mx(out=da_codes[:].bitcast(FP8X4), scales=da_plane[:], in_=da[:])
-            return da_codes, da_plane
-
-        def first_layer_products(e, behind, da_codes, da_plane):
-            bank = sums_bank()
-            for b in range(K_BLOCKS):
-                nc.tensor.matmul_mx(
-                    out=bank[:, b, :],
-                    lhsT=w1_codes[:, e, 2 * P * b : 2 * P * (b + 1)].bitcast(FP4X4),
-                    lhsT_scale=w1_plane[:, e, P * b : P * (b + 1)],
-                    rhs=da_codes[:].bitcast(FP8X4),
-                    rhs_scale=da_plane[:],
-                    start=True,
-                    stop=True,
+        for n in range(E // 2):
+            for move, copy, scale, experts, blocks in lanes:
+                e = experts[n]
+                pairs = da_rows[e][:].rearrange("u h p d -> u (h p d)").bitcast(F32)
+                by_row = row_bank()
+                for h in range(2):
+                    nc.tensor.transpose(by_row[:, h, :], pairs[:, h * P : (h + 1) * P], identity[:])
+                da[e] = keep.tile([P, C * PACK], BF16, name="da%d" % e, align_bytes=64)
+                copy(
+                    da[e][:].bitcast(F32).rearrange("p (u h) -> p u h", h=2),
+                    by_row[:, 0:2, :].rearrange("p h u -> p u h"),
                 )
-            offset = ROWS_AT + BLOCK_PAIR_BYTES + behind * ROWS_STEP + BLOCK_PAIR_BYTES // 2
-            results = late.tile([P, K_BLOCKS, C], F32, name="results%d" % e, align_bytes=64, offset=offset)
-            nc.scalar.copy(results[:], bank[:, 0:K_BLOCKS, :])
-            for b in range(K_BLOCKS):
-                nc.vector.tensor_copy(dx[b][:].indirect(entries(list1, e * C, C)), results[:, b, :])
+        for n in range(E // 2):
+            for move, copy, scale, experts, blocks in lanes:
+                e = experts[n]
+                da_codes = keep.tile([P, C], U32, name="da_codes%d" % e, align_bytes=64)
+                da_plane = keep.tile([P, C], U8, name="da_plane%d" % e, align_bytes=64)
+                nc.vector.quantize_mx(out=da_codes[:].bitcast(FP8X4), scales=da_plane[:], in_=da[e][:])
+                da_mx[e] = da_codes, da_plane
 
-        follows = {e + (1 if e < TWO_BEHIND_FROM else 2): e for e in range(E)}
-        da_mx = {}
-        for step in range(max(follows) + 1):
-            if step < E:
-                da_mx[step] = quantise_da(step)
-            if step == 1:
-                last_slots = late.tile([P, BLOCKS - 1, 2 * C], F32, name="last_slots", align_bytes=64, offset=ROWS_AT)
-                for b in range(1, BLOCKS):
-                    gather_dc(last_slots[:, b - 1, :], b, 4, 2)
-            if step in follows:
-                first_layer_products(follows[step], step, *da_mx[follows[step]])
+        for first in (0, 4, 2):
+            for b in range(K_BLOCKS):
+                move, copy = lanes[b][0:2]
+                bank = wide_bank()
+                for n in range(2):
+                    e = first + n
+                    nc.tensor.matmul_mx(
+                        out=bank[:, n, :],
+                        lhsT=w1_codes[:, e, 2 * P * b : 2 * P * (b + 1)].bitcast(FP4X4),
+                        lhsT_scale=w1_plane[:, e, P * b : P * (b + 1)],
+                        rhs=da_mx[e][0][:].bitcast(FP8X4),
+                        rhs_scale=da_mx[e][1][:],
+                        start=True,
+                        stop=True,
+                    )
+                results = keep.tile([P, 2 * C], F32, name="results%d_%d" % (first, b))
+                copy(results[:], bank[:, 0:2, :].rearrange("p n u -> p (n u)"))
+                move(dx[b][:].indirect(entries(list1, first * C, 2 * C)), results[:])
 
         for b in range(K_BLOCKS):
             nc.sync.dma_start(out[b * P : (b + 1) * P, :], dx[b][:])

@@ -28,7 +28,7 @@ HALF = H // 2
 RUN = 4
 DMA_ALIGN = 256
 GATE2_ROWS = 8
-SHARE = 128
+SPLIT = 64
 EARLY = 2
 
 
@@ -56,9 +56,8 @@ def tile_moe_seb_none_kernel(
         dy_plane = keep.tile([P, T], U8, name="dy_plane", align_bytes=DMA_ALIGN)
         w1_plane = keep.tile([P, E, K], U8, name="w1_plane", align_bytes=DMA_ALIGN)
         w1_codes = keep.tile([P, E, 2 * K], U8, name="w1_codes", align_bytes=DMA_ALIGN)
-        gate1_rows = keep.tile([P, C], F32, name="gate1_rows")
+        gate1_all = keep.tile([P, T], F32, name="gate1_all", align_bytes=DMA_ALIGN)
         gate2_rows = keep.tile([P, C], F32, name="gate2_rows")
-        gate1_cols = keep.tile([P, E], F32, name="gate1_cols")
         gate2_cols = keep.tile([P, GATE2_ROWS], F32, name="gate2_cols")
         gate2_all = keep.tile([P, T], F32, name="gate2_all")
         identity = keep.tile([P, P], F32, name="identity")
@@ -69,7 +68,6 @@ def tile_moe_seb_none_kernel(
         nc.vector.memset(dy_plane[:].bitcast(I32), 0)
         nc.gpsimd.memset(gate2_rows[:], 0.0)
         make_identity(nc, identity[:])
-        nc.gpsimd.memset(gate1_rows[:], 0.0)
         nc.gpsimd.memset(w1_plane[:].rearrange("p e k -> p (e k)").bitcast(I32), 0)
 
         w2_raw = {}
@@ -91,11 +89,10 @@ def tile_moe_seb_none_kernel(
         nc.sync.dma_start(dy_codes[1][:], dy_words[1].rearrange("p t d -> p (t d)").bitcast(I32))
         nc.scalar.dma_start(gate2_rows[0:GATE2_ROWS, 0:piece], gate2[0].rearrange("(r u) -> r u", u=piece))
         for f in range(E):
-            if f == E - 1:
-                nc.sync.dma_start(list1[:], offs)
-                nc.sync.dma_start(gate1_rows[0:E, :], gate1[0].rearrange("(e u) -> e u", u=C))
             for s in range(PASSES):
                 load_w2(f, s)
+        nc.sync.dma_start(list1[:], offs)
+        nc.sync.dma_start(gate1_all[:], gate1)
         nc.sync.dma_start(w1_codes[:].bitcast(I32), w1t_words[:, 0].rearrange("e p b -> p e b").bitcast(I32))
         for q in range(QUADRANTS):
             nc.sync.dma_start(
@@ -141,10 +138,10 @@ def tile_moe_seb_none_kernel(
             w2_codes[f, s] = ring.tile([P, H], U32, name="w2_codes", align_bytes=64)
             w2_plane[f, s] = ring.tile([P, H], U8, name="w2_plane", align_bytes=64)
 
-        def round_w2(engine_copy, f, s, c0, c1):
+        def round_w2(engine_copy, f, s, blocks, places):
             engine_copy(
-                grouped[f, s][:, c0 * PACK : c1 * PACK].rearrange("p (c i j) -> p c j i", i=RUN, j=PACK),
-                w2_raw[f, s][:, :, c0:c1].rearrange("p j (c i) -> p c j i", i=RUN),
+                grouped[f, s][:].rearrange("p (t m j) -> p m j t", t=BLOCKS, j=PACK)[:, places, :, blocks],
+                w2_raw[f, s][:].rearrange("p j (m t) -> p m j t", t=BLOCKS)[:, places, :, blocks],
             )
 
         def quantise_w2(f, s, c0, c1):
@@ -180,27 +177,28 @@ def tile_moe_seb_none_kernel(
         def scatter_dc(move, f, b, sums):
             move(dc[b][:].indirect(entries(list2, f * C, C)), sums[:, b, :])
 
+        low, high, whole = slice(0, 2), slice(2, BLOCKS), slice(0, P)
         for f in range(E):
             for s in range(PASSES):
                 open_pass(f, s)
             if f == 0:
-                round_w2(nc.scalar.copy, f, 0, 0, HALF)
-                round_w2(nc.scalar.copy, f, 0, HALF, H)
+                round_w2(nc.scalar.copy, f, 0, low, whole)
+                round_w2(nc.scalar.copy, f, 0, high, whole)
                 quantise_w2(f, 0, 0, HALF)
                 quantise_w2(f, 0, HALF, H)
-                round_w2(nc.vector.tensor_copy, f, 1, 0, HALF)
-                round_w2(nc.scalar.copy, f, 1, HALF, H)
+                round_w2(nc.vector.tensor_copy, f, 1, low, whole)
+                round_w2(nc.scalar.copy, f, 1, high, whole)
             else:
-                round_w2(nc.scalar.copy, f, 0, H - SHARE, H)
-                round_w2(nc.vector.tensor_copy, f, 0, 0, P)
-                round_w2(nc.vector.tensor_copy, f, 0, P, H - SHARE)
+                round_w2(nc.scalar.copy, f, 0, high, slice(SPLIT, P))
+                round_w2(nc.vector.tensor_copy, f, 0, slice(0, BLOCKS), slice(0, SPLIT))
+                round_w2(nc.vector.tensor_copy, f, 0, low, slice(SPLIT, P))
                 sums = w2_raw[f, 0][:, :, 0:C]
                 gate_sums(f - 1, banks[f - 1], sums, 0, BLOCKS)
                 for b in range(BLOCKS):
                     scatter_dc(scalar_move, f - 1, b, sums)
                 quantise_w2(f, 0, 0, H)
-                round_w2(nc.vector.tensor_copy, f, 1, 0, HALF)
-                round_w2(nc.vector.tensor_copy, f, 1, HALF, H)
+                round_w2(nc.vector.tensor_copy, f, 1, low, whole)
+                round_w2(nc.vector.tensor_copy, f, 1, high, whole)
             quantise_w2(f, 1, 0, HALF)
             quantise_w2(f, 1, HALF, H)
             if f < E - 1:
@@ -211,82 +209,68 @@ def tile_moe_seb_none_kernel(
             for b in range(first, first + 2):
                 scatter_dc(move, E - 1, b, last_sums)
 
-        turn_gate(gate1_rows, gate1_cols, E)
+        PAIR = 2 * C
+        slots = [keep.tile([P, BLOCKS, PAIR], F32, name="slots%d" % n) for n in range(E // 2)]
 
-        def vector_scale(target, source, factor):
-            nc.vector.tensor_scalar(target, source, factor, None, MULT)
+        def gather_dc(move, n, b):
+            move(slots[n][:, b, :], dc[b][:].indirect(entries(list1, n * PAIR, PAIR)))
 
-        def scalar_scale(target, source, factor):
-            nc.scalar.activation(target, source, COPY, scale=factor)
+        for n, b in ((0, 2), (0, 3), (1, 2)):
+            gather_dc(nc.vector.tensor_copy, n, b)
+        for n, b in ((0, 0), (0, 1), (1, 0), (1, 1), (1, 3), (2, 0), (2, 1), (2, 2), (2, 3)):
+            gather_dc(scalar_move, n, b)
 
-        lanes = (
-            (nc.vector.tensor_copy, nc.vector.tensor_copy, vector_scale, (0, 1, 2), (2, 3, 0, 1)),
-            (scalar_move, nc.scalar.copy, scalar_scale, (5, 4, 3), (0, 1, 2, 3)),
-        )
-        dc_slots = {}
-        for move, copy, scale, experts, blocks in lanes:
-            first = min(experts)
-            for b in blocks:
-                slots = keep.tile([P, len(experts) * C], F32, name="slots%d_%d" % (first, b))
-                for e in experts:
-                    dc_slots[e, b] = slots[:, (e - first) * C : (e - first + 1) * C]
-                if b == blocks[-1]:
-                    for e in experts:
-                        move(dc_slots[e, b], dc[b][:].indirect(entries(list1, e * C, C)))
-                else:
-                    move(slots[:], dc[b][:].indirect(entries(list1, first * C, len(experts) * C)))
+        def round_da(n):
+            da = keep.tile([P, PAIR * PACK], BF16, name="da", align_bytes=64)
+            gate = gate1_all[:, n * PAIR : (n + 1) * PAIR].rearrange("p (c i) -> p c i", i=RUN)
+            nc.vector.tensor_tensor(
+                da[:].rearrange("p (c i t) -> p c t i", i=RUN, t=PACK),
+                slots[n][:].rearrange("p t (c i) -> p c t i", i=RUN),
+                gate.unsqueeze(2).to_broadcast([P, PAIR // RUN, PACK, RUN]),
+                MULT,
+            )
+            return da
 
-        da_rows, da, da_mx = {}, {}, {}
-        for n in range(E // 2):
-            for move, copy, scale, experts, blocks in lanes:
-                e = experts[n]
-                by_slot = wide_bank()
-                for b in blocks:
-                    nc.tensor.transpose(by_slot[:, b, :], dc_slots[e, b], identity[:])
-                da_rows[e] = keep.tile([P, 2, P, 2], BF16, name="da_rows%d" % e, align_bytes=64)
-                scale(
-                    da_rows[e][:],
-                    by_slot[:].rearrange("u b i -> u (b i)").rearrange("u (p h d) -> u h p d", h=2, d=2),
-                    gate1_cols[:, e : e + 1],
-                )
-        for n in range(E // 2):
-            for move, copy, scale, experts, blocks in lanes:
-                e = experts[n]
-                pairs = da_rows[e][:].rearrange("u h p d -> u (h p d)").bitcast(F32)
-                by_row = row_bank()
-                for h in range(2):
-                    nc.tensor.transpose(by_row[:, h, :], pairs[:, h * P : (h + 1) * P], identity[:])
-                da[e] = keep.tile([P, C * PACK], BF16, name="da%d" % e, align_bytes=64)
-                copy(
-                    da[e][:].bitcast(F32).rearrange("p (u h) -> p u h", h=2),
-                    by_row[:, 0:2, :].rearrange("p h u -> p u h"),
-                )
-        for n in range(E // 2):
-            for move, copy, scale, experts, blocks in lanes:
-                e = experts[n]
-                da_codes = keep.tile([P, C], U32, name="da_codes%d" % e, align_bytes=64)
-                da_plane = keep.tile([P, C], U8, name="da_plane%d" % e, align_bytes=64)
-                nc.vector.quantize_mx(out=da_codes[:].bitcast(FP8X4), scales=da_plane[:], in_=da[e][:])
-                da_mx[e] = da_codes, da_plane
-
-        for first in (0, 4, 2):
+        def first_layer_products(n, da):
+            da_codes = keep.tile([P, PAIR], U32, name="da_codes%d" % n, align_bytes=64)
+            da_plane = keep.tile([P, PAIR], U8, name="da_plane%d" % n, align_bytes=64)
+            nc.vector.quantize_mx(out=da_codes[:].bitcast(FP8X4), scales=da_plane[:], in_=da[:])
+            pair_banks = []
             for b in range(K_BLOCKS):
-                move, copy = lanes[b][0:2]
                 bank = wide_bank()
-                for n in range(2):
-                    e = first + n
+                for m in range(2):
+                    e = 2 * n + m
                     nc.tensor.matmul_mx(
-                        out=bank[:, n, :],
+                        out=bank[:, m, :],
                         lhsT=w1_codes[:, e, 2 * P * b : 2 * P * (b + 1)].bitcast(FP4X4),
                         lhsT_scale=w1_plane[:, e, P * b : P * (b + 1)],
-                        rhs=da_mx[e][0][:].bitcast(FP8X4),
-                        rhs_scale=da_mx[e][1][:],
+                        rhs=da_codes[:, m * C : (m + 1) * C].bitcast(FP8X4),
+                        rhs_scale=da_plane[:, m * C : (m + 1) * C],
                         start=True,
                         stop=True,
                     )
-                results = keep.tile([P, 2 * C], F32, name="results%d_%d" % (first, b))
-                copy(results[:], bank[:, 0:2, :].rearrange("p n u -> p (n u)"))
-                move(dx[b][:].indirect(entries(list1, first * C, 2 * C)), results[:])
+                pair_banks.append(bank)
+            return pair_banks
 
-        for b in range(K_BLOCKS):
-            nc.sync.dma_start(out[b * P : (b + 1) * P, :], dx[b][:])
+        def empty(copy, n, b, bank):
+            results = keep.tile([P, PAIR], F32, name="results%d_%d" % (n, b))
+            copy(results[:], bank[:, 0:2, :].rearrange("p m u -> p (m u)"))
+            return results
+
+        def scatter_dx(move, n, b, results):
+            move(dx[b][:].indirect(entries(list1, n * PAIR, PAIR)), results[:])
+
+        made = {}
+        for n in range(E // 2 + 1):
+            if n < E // 2:
+                da = round_da(n)
+            if n > 0:
+                results = empty(nc.vector.tensor_copy, n - 1, 0, made[n - 1][0])
+            if n < E // 2:
+                made[n] = first_layer_products(n, da)
+            if n > 0:
+                scatter_dx(nc.vector.tensor_copy, n - 1, 0, results)
+                scatter_dx(scalar_move, n - 1, 1, empty(nc.scalar.copy, n - 1, 1, made[n - 1][1]))
+
+        nc.sync.dma_start(out[0:P, :], dx[0][:])
+        nc.scalar.dma_start(out[P : 2 * P, :], dx[1][:])

@@ -59,14 +59,13 @@ def tile_moe_seb_none_kernel(
         gate1_all = keep.tile([P, T], F32, name="gate1_all", align_bytes=DMA_ALIGN)
         gate2_rows = keep.tile([P, C], F32, name="gate2_rows")
         gate2_cols = keep.tile([P, GATE2_ROWS], F32, name="gate2_cols")
-        gate2_all = keep.tile([P, T], F32, name="gate2_all")
         identity = keep.tile([P, P], F32, name="identity")
         dy_codes = [keep.tile([P, T], I32, name="dy_codes%d" % s, align_bytes=DMA_ALIGN) for s in range(PASSES)]
         dc = [keep.tile([P, T], F32, name="dc%d" % b) for b in range(BLOCKS)]
         dx = [keep.tile([P, T], F32, name="dx%d" % b, align_bytes=DMA_ALIGN) for b in range(K_BLOCKS)]
 
+        nc.vector.memset(gate2_rows[:], 0.0)
         nc.vector.memset(dy_plane[:].bitcast(I32), 0)
-        nc.gpsimd.memset(gate2_rows[:], 0.0)
         make_identity(nc, identity[:])
         nc.gpsimd.memset(w1_plane[:].rearrange("p e k -> p (e k)").bitcast(I32), 0)
 
@@ -81,13 +80,13 @@ def tile_moe_seb_none_kernel(
         piece = T // GATE2_ROWS
         nc.sync.dma_start(list2[:], offs2)
         nc.sync.dma_start(dy_codes[0][:], dy_words[0].rearrange("p t d -> p (t d)").bitcast(I32))
+        nc.sync.dma_start(gate2_rows[0:GATE2_ROWS, 0:piece], gate2[0].rearrange("(r u) -> r u", u=piece))
         for q in range(QUADRANTS):
             nc.sync.dma_start(
                 dy_plane[32 * q : 32 * q + 4 * PASSES, :].bitcast(I32),
                 dy_scales[:, 4 * q : 4 * q + 4, :].bitcast(I32),
             )
         nc.sync.dma_start(dy_codes[1][:], dy_words[1].rearrange("p t d -> p (t d)").bitcast(I32))
-        nc.scalar.dma_start(gate2_rows[0:GATE2_ROWS, 0:piece], gate2[0].rearrange("(r u) -> r u", u=piece))
         for f in range(E):
             for s in range(PASSES):
                 load_w2(f, s)
@@ -106,13 +105,14 @@ def tile_moe_seb_none_kernel(
             nc.scalar.copy(gate_cols[:], bank[:, 0, 0:count])
 
         turn_gate(gate2_rows, gate2_cols, GATE2_ROWS)
+        gate2_banks = []
+        gate2_all = w2_raw[0, 1][:, 0:2, H - T // 2 : H]
         for first in range(0, GATE2_ROWS, BLOCKS):
             bank = wide_bank()
             for n in range(BLOCKS):
                 column = gate2_cols[:, first + n : first + n + 1]
                 nc.tensor.transpose(bank[:, n, :], column.to_broadcast([P, P]), identity[:])
-            spread = gate2_all[:, first * piece : (first + BLOCKS) * piece].rearrange("p (r u) -> p r u", u=piece)
-            nc.scalar.copy(spread, bank[:, :, 0:piece])
+            gate2_banks.append(bank)
 
         g_codes, g_plane = {}, {}
 
@@ -153,22 +153,23 @@ def tile_moe_seb_none_kernel(
 
         def second_layer_products(f, first, end):
             bank = wide_bank()
-            for b in range(first, end):
-                cols = slice(b * P, (b + 1) * P)
-                for s in range(PASSES):
+            for s in range(PASSES):
+                for b in range(first, end):
+                    cols = slice(b * P, (b + 1) * P)
                     nc.tensor.matmul_mx(
                         out=bank[:, b, :],
                         lhsT=w2_codes[f, s][:, cols].bitcast(FP8X4),
                         lhsT_scale=w2_plane[f, s][:, cols],
                         rhs=g_codes[f, s].bitcast(FP8X4),
                         rhs_scale=g_plane[f][4 * s : P, :],
-                        start=(s == 0),
-                        stop=(s == PASSES - 1),
+                        start=(s, b) == (0, first),
+                        stop=(s, b) == (PASSES - 1, end - 1),
                     )
             return bank
 
         def gate_sums(f, bank, sums, first, end):
-            gate = gate2_all[:, f * C : (f + 1) * C].unsqueeze(1).to_broadcast([P, end - first, C])
+            row, place = divmod(f, E // 2)
+            gate = gate2_all[:, row, place * C : (place + 1) * C].unsqueeze(1).to_broadcast([P, end - first, C])
             nc.vector.tensor_tensor(sums[:, first:end, :], bank[:, first:end, :], gate, MULT)
 
         def scalar_move(target, source):
@@ -186,8 +187,12 @@ def tile_moe_seb_none_kernel(
                 round_w2(nc.scalar.copy, f, 0, high, whole)
                 quantise_w2(f, 0, 0, HALF)
                 quantise_w2(f, 0, HALF, H)
-                round_w2(nc.vector.tensor_copy, f, 1, low, whole)
-                round_w2(nc.scalar.copy, f, 1, high, whole)
+                round_w2(nc.scalar.copy, f, 1, low, whole)
+                round_w2(nc.scalar.copy, f, 1, high, slice(SPLIT, P))
+                round_w2(nc.vector.tensor_copy, f, 1, high, slice(0, SPLIT))
+                for n, gate2_bank in enumerate(gate2_banks):
+                    spread = gate2_all[:, n, :].rearrange("p (r u) -> p r u", u=piece)
+                    nc.scalar.copy(spread, gate2_bank[:, :, 0:piece])
             else:
                 round_w2(nc.scalar.copy, f, 0, high, slice(SPLIT, P))
                 round_w2(nc.vector.tensor_copy, f, 0, slice(0, BLOCKS), slice(0, SPLIT))
@@ -204,10 +209,10 @@ def tile_moe_seb_none_kernel(
             if f < E - 1:
                 banks[f] = second_layer_products(f, 0, BLOCKS)
         last_sums = keep.tile([P, BLOCKS, C], F32, name="last_sums")
-        for first, move in ((0, scalar_move), (2, nc.vector.tensor_copy)):
+        for first in (0, 2):
             gate_sums(E - 1, second_layer_products(E - 1, first, first + 2), last_sums, first, first + 2)
-            for b in range(first, first + 2):
-                scatter_dc(move, E - 1, b, last_sums)
+        for b in range(BLOCKS):
+            scatter_dc(nc.vector.tensor_copy if b % 2 else scalar_move, E - 1, b, last_sums)
 
         PAIR = 2 * C
         slots = [keep.tile([P, BLOCKS, PAIR], F32, name="slots%d" % n) for n in range(E // 2)]
@@ -215,26 +220,26 @@ def tile_moe_seb_none_kernel(
         def gather_dc(move, n, b):
             move(slots[n][:, b, :], dc[b][:].indirect(entries(list1, n * PAIR, PAIR)))
 
-        for n, b in ((0, 2), (0, 3), (1, 2)):
+        for n, b in ((0, 1), (0, 3), (1, 1), (1, 3)):
             gather_dc(nc.vector.tensor_copy, n, b)
-        for n, b in ((0, 0), (0, 1), (1, 0), (1, 1), (1, 3), (2, 0), (2, 1), (2, 2), (2, 3)):
+        for n, b in ((0, 0), (0, 2), (1, 0), (1, 2), (2, 0), (2, 1), (2, 2), (2, 3)):
             gather_dc(scalar_move, n, b)
 
-        def round_da(n):
-            da = keep.tile([P, PAIR * PACK], BF16, name="da", align_bytes=64)
-            gate = gate1_all[:, n * PAIR : (n + 1) * PAIR].rearrange("p (c i) -> p c i", i=RUN)
+        da = [keep.tile([P, PAIR * PACK], BF16, name="da%d" % n, align_bytes=64) for n in range(E // 2)]
+
+        def round_da(n, c0, c1):
+            gate = gate1_all[:, n * PAIR + c0 : n * PAIR + c1].rearrange("p (c i) -> p c i", i=RUN)
             nc.vector.tensor_tensor(
-                da[:].rearrange("p (c i t) -> p c t i", i=RUN, t=PACK),
-                slots[n][:].rearrange("p t (c i) -> p c t i", i=RUN),
-                gate.unsqueeze(2).to_broadcast([P, PAIR // RUN, PACK, RUN]),
+                da[n][:, c0 * PACK : c1 * PACK].rearrange("p (c i t) -> p c t i", i=RUN, t=PACK),
+                slots[n][:, :, c0:c1].rearrange("p t (c i) -> p c t i", i=RUN),
+                gate.unsqueeze(2).to_broadcast([P, (c1 - c0) // RUN, PACK, RUN]),
                 MULT,
             )
-            return da
 
-        def first_layer_products(n, da):
+        def first_layer_products(n):
             da_codes = keep.tile([P, PAIR], U32, name="da_codes%d" % n, align_bytes=64)
             da_plane = keep.tile([P, PAIR], U8, name="da_plane%d" % n, align_bytes=64)
-            nc.vector.quantize_mx(out=da_codes[:].bitcast(FP8X4), scales=da_plane[:], in_=da[:])
+            nc.vector.quantize_mx(out=da_codes[:].bitcast(FP8X4), scales=da_plane[:], in_=da[n][:])
             pair_banks = []
             for b in range(K_BLOCKS):
                 bank = wide_bank()
@@ -260,17 +265,16 @@ def tile_moe_seb_none_kernel(
         def scatter_dx(move, n, b, results):
             move(dx[b][:].indirect(entries(list1, n * PAIR, PAIR)), results[:])
 
-        made = {}
-        for n in range(E // 2 + 1):
-            if n < E // 2:
-                da = round_da(n)
-            if n > 0:
-                results = empty(nc.vector.tensor_copy, n - 1, 0, made[n - 1][0])
-            if n < E // 2:
-                made[n] = first_layer_products(n, da)
-            if n > 0:
-                scatter_dx(nc.vector.tensor_copy, n - 1, 0, results)
-                scatter_dx(scalar_move, n - 1, 1, empty(nc.scalar.copy, n - 1, 1, made[n - 1][1]))
+        round_da(0, 0, PAIR)
+        made = [first_layer_products(0)]
+        round_da(1, 0, C)
+        round_da(1, C, PAIR)
+        round_da(2, 0, PAIR)
+        made.extend(first_layer_products(n) for n in range(1, E // 2))
+        for n in range(E // 2):
+            own = empty(nc.scalar.copy, n, 1, made[n][1])
+            scatter_dx(nc.vector.tensor_copy, n, 0, empty(nc.scalar.copy, n, 0, made[n][0]))
+            scatter_dx(scalar_move, n, 1, own)
 
         nc.sync.dma_start(out[0:P, :], dx[0][:])
         nc.scalar.dma_start(out[P : 2 * P, :], dx[1][:])

@@ -78,9 +78,8 @@ def tile_moe_seb_none_kernel(
             w2_raw[f, s] = raw
 
         piece = T // GATE2_ROWS
-        nc.sync.dma_start(list2[:], offs2)
         nc.sync.dma_start(dy_codes[0][:], dy_words[0].rearrange("p t d -> p (t d)").bitcast(I32))
-        nc.sync.dma_start(gate2_rows[0:GATE2_ROWS, 0:piece], gate2[0].rearrange("(r u) -> r u", u=piece))
+        nc.sync.dma_start(list2[:], offs2)
         for q in range(QUADRANTS):
             nc.sync.dma_start(
                 dy_plane[32 * q : 32 * q + 4 * PASSES, :].bitcast(I32),
@@ -90,6 +89,8 @@ def tile_moe_seb_none_kernel(
         for f in range(E):
             for s in range(PASSES):
                 load_w2(f, s)
+                if (f, s) == (0, 0):
+                    nc.sync.dma_start(gate2_rows[0:GATE2_ROWS, 0:piece], gate2[0].rearrange("(r u) -> r u", u=piece))
         nc.sync.dma_start(list1[:], offs)
         nc.sync.dma_start(gate1_all[:], gate1)
         nc.sync.dma_start(w1_codes[:].bitcast(I32), w1t_words[:, 0].rearrange("e p b -> p e b").bitcast(I32))
@@ -271,10 +272,14 @@ def tile_moe_seb_none_kernel(
         round_da(1, C, PAIR)
         round_da(2, 0, PAIR)
         made.extend(first_layer_products(n) for n in range(1, E // 2))
-        for n in range(E // 2):
-            own = empty(nc.scalar.copy, n, 1, made[n][1])
-            scatter_dx(nc.vector.tensor_copy, n, 0, empty(nc.scalar.copy, n, 0, made[n][0]))
-            scatter_dx(scalar_move, n, 1, own)
+        results = {}
+        for group in ((0,), (1, 2)):
+            for n in group:
+                results[n, 1] = empty(nc.scalar.copy, n, 1, made[n][1])
+                results[n, 0] = empty(nc.vector.tensor_copy if n == 2 else nc.scalar.copy, n, 0, made[n][0])
+            for n in group:
+                scatter_dx(nc.vector.tensor_copy, n, 0, results[n, 0])
+                scatter_dx(scalar_move, n, 1, results[n, 1])
 
-        nc.sync.dma_start(out[0:P, :], dx[0][:])
         nc.scalar.dma_start(out[P : 2 * P, :], dx[1][:])
+        nc.sync.dma_start(out[0:P, :], dx[0][:])

@@ -22,14 +22,20 @@ PACK = 4
 PASSES = N // (P * PACK)
 BLOCKS = H // P
 K_BLOCKS = K // P
+PAIR = 2 * C
+PAIRS = E // 2
 QUADRANTS = 4
 PER_COLUMN = 16
-HALF = H // 2
+BANKS = 8
 RUN = 4
 DMA_ALIGN = 256
+MX_ALIGN = 64
 GATE2_ROWS = 8
+RING_DEPTH = 2 * PASSES
 SPLIT = 64
-EARLY = 2
+
+LOW, HIGH, ALL_BLOCKS = slice(0, 2), slice(2, BLOCKS), slice(0, BLOCKS)
+FRONT, BACK, ALL_PLACES = slice(0, SPLIT), slice(SPLIT, P), slice(0, P)
 
 
 def entries(offsets, first, count):
@@ -42,14 +48,14 @@ def tile_moe_seb_none_kernel(
     nc = tc.nc
     with ExitStack() as ctx:
         keep = ctx.enter_context(tc.tile_pool(name="keep", bufs=1))
-        ring = ctx.enter_context(tc.tile_pool(name="ring", bufs=4))
-        psum = ctx.enter_context(tc.psum_pool(name="psum", bufs=1))
+        ring = ctx.enter_context(tc.tile_pool(name="ring", bufs=RING_DEPTH))
+        psum = ctx.enter_context(tc.psum_pool(name="psum", bufs=BANKS))
 
-        def wide_bank():
-            return psum.tile([P, BLOCKS, C], F32, name="wide_bank", bufs=6)
+        def next_bank():
+            return psum.tile([P, BLOCKS, C], F32, name="bank")
 
-        def row_bank():
-            return psum.tile([P, BLOCKS, C], F32, name="row_bank", bufs=2)
+        def scalar_move(target, source):
+            nc.scalar.activation(target, source, COPY)
 
         list1 = keep.tile([P, T // PER_COLUMN], U16, name="list1")
         list2 = keep.tile([P, T // PER_COLUMN], U16, name="list2")
@@ -57,7 +63,7 @@ def tile_moe_seb_none_kernel(
         w1_plane = keep.tile([P, E, K], U8, name="w1_plane", align_bytes=DMA_ALIGN)
         w1_codes = keep.tile([P, E, 2 * K], U8, name="w1_codes", align_bytes=DMA_ALIGN)
         gate1_all = keep.tile([P, T], F32, name="gate1_all", align_bytes=DMA_ALIGN)
-        gate2_rows = keep.tile([P, C], F32, name="gate2_rows")
+        gate2_rows = keep.tile([P, P], F32, name="gate2_rows")
         gate2_cols = keep.tile([P, GATE2_ROWS], F32, name="gate2_cols")
         identity = keep.tile([P, P], F32, name="identity")
         dy_codes = [keep.tile([P, T], I32, name="dy_codes%d" % s, align_bytes=DMA_ALIGN) for s in range(PASSES)]
@@ -69,26 +75,25 @@ def tile_moe_seb_none_kernel(
         make_identity(nc, identity[:])
         nc.gpsimd.memset(w1_plane[:].rearrange("p e k -> p (e k)").bitcast(I32), 0)
 
-        w2_raw = {}
+        def load_dy(s):
+            nc.sync.dma_start(dy_codes[s][:], dy_words[s].rearrange("p t d -> p (t d)").bitcast(I32))
 
-        def load_w2(f, s):
-            raw = keep.tile([P, PACK, H], F32, name="w2_raw%d_%d" % (f, s), align_bytes=DMA_ALIGN)
-            rows = w2t[f, s * P * PACK : (s + 1) * P * PACK, :]
-            nc.sync.dma_start(raw[:], rows.rearrange("(p j) i -> p j i", j=PACK))
-            w2_raw[f, s] = raw
-
-        piece = T // GATE2_ROWS
-        nc.sync.dma_start(dy_codes[0][:], dy_words[0].rearrange("p t d -> p (t d)").bitcast(I32))
+        load_dy(0)
         nc.sync.dma_start(list2[:], offs2)
         for q in range(QUADRANTS):
             nc.sync.dma_start(
                 dy_plane[32 * q : 32 * q + 4 * PASSES, :].bitcast(I32),
                 dy_scales[:, 4 * q : 4 * q + 4, :].bitcast(I32),
             )
-        nc.sync.dma_start(dy_codes[1][:], dy_words[1].rearrange("p t d -> p (t d)").bitcast(I32))
+        load_dy(1)
+        piece = T // GATE2_ROWS
+        w2_raw = {}
         for f in range(E):
             for s in range(PASSES):
-                load_w2(f, s)
+                raw = keep.tile([P, PACK, H], F32, name="w2_raw%d_%d" % (f, s), align_bytes=DMA_ALIGN)
+                rows = w2t[f, s * P * PACK : (s + 1) * P * PACK, :]
+                nc.sync.dma_start(raw[:], rows.rearrange("(p j) i -> p j i", j=PACK))
+                w2_raw[f, s] = raw
                 if (f, s) == (0, 0):
                     nc.sync.dma_start(gate2_rows[0:GATE2_ROWS, 0:piece], gate2[0].rearrange("(r u) -> r u", u=piece))
         nc.sync.dma_start(list1[:], offs)
@@ -100,186 +105,174 @@ def tile_moe_seb_none_kernel(
                 w1t_scales[:, 0, 4 * q : 4 * q + 4, :].rearrange("e r k -> r e k").bitcast(I32),
             )
 
-        def turn_gate(gate_rows, gate_cols, count):
-            bank = row_bank()
-            nc.tensor.transpose(bank[:, 0, :], gate_rows[:], identity[:])
-            nc.scalar.copy(gate_cols[:], bank[:, 0, 0:count])
-
-        turn_gate(gate2_rows, gate2_cols, GATE2_ROWS)
+        bank = next_bank()
+        nc.tensor.transpose(bank[:, 0, :], gate2_rows[:], identity[:])
+        nc.scalar.copy(gate2_cols[:], bank[:, 0, 0:GATE2_ROWS])
         gate2_banks = []
-        gate2_all = w2_raw[0, 1][:, 0:2, H - T // 2 : H]
         for first in range(0, GATE2_ROWS, BLOCKS):
-            bank = wide_bank()
+            bank = next_bank()
             for n in range(BLOCKS):
                 column = gate2_cols[:, first + n : first + n + 1]
                 nc.tensor.transpose(bank[:, n, :], column.to_broadcast([P, P]), identity[:])
             gate2_banks.append(bank)
 
-        g_codes, g_plane = {}, {}
+        def gather_dy(window, dtype, name):
+            parts = []
+            for first in (0, T // 2):
+                tile = keep.tile([P, T // 2], dtype, name="%s_%d" % (name, first), align_bytes=MX_ALIGN)
+                nc.vector.tensor_copy(tile[:], window.indirect(entries(list2, first, T // 2)))
+                parts.extend(tile[:, n * C : (n + 1) * C] for n in range(E // 2))
+            return parts
 
-        def gather_dy(window, dtype, name, first, end):
-            tile = keep.tile([P, (end - first) * C], dtype, name="%s_%d" % (name, first), align_bytes=64)
-            nc.vector.tensor_copy(tile[:], window.indirect(entries(list2, first * C, (end - first) * C)))
-            return {f: tile[:, (f - first) * C : (f - first + 1) * C] for f in range(first, end)}
+        g_codes = [gather_dy(dy_codes[0][:].bitcast(U32), U32, "g_codes0")]
+        g_plane = gather_dy(dy_plane[:], U8, "g_plane")
+        g_codes.append(gather_dy(dy_codes[1][:].bitcast(U32), U32, "g_codes1"))
 
-        def gather_words(s):
-            for first, end in ((0, EARLY), (EARLY, E)):
-                parts = gather_dy(dy_codes[s][:].bitcast(U32), U32, "g_codes%d" % s, first, end)
-                g_codes.update({(f, s): part for f, part in parts.items()})
-
-        gather_words(0)
-        for first, end in ((0, EARLY), (EARLY, E)):
-            g_plane.update(gather_dy(dy_plane[:], U8, "g_plane", first, end))
-        gather_words(1)
-
-        grouped, w2_codes, w2_plane, banks = {}, {}, {}, {}
-
-        def open_pass(f, s):
-            grouped[f, s] = ring.tile([P, H * PACK], BF16, name="grouped", align_bytes=64)
-            w2_codes[f, s] = ring.tile([P, H], U32, name="w2_codes", align_bytes=64)
-            w2_plane[f, s] = ring.tile([P, H], U8, name="w2_plane", align_bytes=64)
+        rounded, w2_codes, w2_plane = {}, {}, {}
 
         def round_w2(engine_copy, f, s, blocks, places):
             engine_copy(
-                grouped[f, s][:].rearrange("p (t m j) -> p m j t", t=BLOCKS, j=PACK)[:, places, :, blocks],
+                rounded[f, s][:].rearrange("p (t m j) -> p m j t", t=BLOCKS, j=PACK)[:, places, :, blocks],
                 w2_raw[f, s][:].rearrange("p j (m t) -> p m j t", t=BLOCKS)[:, places, :, blocks],
             )
 
-        def quantise_w2(f, s, c0, c1):
+        def quantise_w2(f, s, blocks):
+            cols = slice(blocks.start * P, blocks.stop * P)
             nc.vector.quantize_mx(
-                out=w2_codes[f, s][:, c0:c1].bitcast(FP8X4),
-                scales=w2_plane[f, s][:, c0:c1],
-                in_=grouped[f, s][:, c0 * PACK : c1 * PACK],
+                out=w2_codes[f, s][:, cols].bitcast(FP8X4),
+                scales=w2_plane[f, s][:, cols],
+                in_=rounded[f, s][:, cols.start * PACK : cols.stop * PACK],
             )
 
-        def second_layer_products(f, first, end):
-            bank = wide_bank()
+        def second_layer_products(f, blocks):
+            bank = next_bank()
             for s in range(PASSES):
-                for b in range(first, end):
+                for b in range(blocks.start, blocks.stop):
                     cols = slice(b * P, (b + 1) * P)
                     nc.tensor.matmul_mx(
                         out=bank[:, b, :],
                         lhsT=w2_codes[f, s][:, cols].bitcast(FP8X4),
                         lhsT_scale=w2_plane[f, s][:, cols],
-                        rhs=g_codes[f, s].bitcast(FP8X4),
+                        rhs=g_codes[s][f].bitcast(FP8X4),
                         rhs_scale=g_plane[f][4 * s : P, :],
-                        start=(s, b) == (0, first),
-                        stop=(s, b) == (PASSES - 1, end - 1),
+                        start=(s, b) == (0, blocks.start),
+                        stop=(s, b) == (PASSES - 1, blocks.stop - 1),
                     )
             return bank
 
-        def gate_sums(f, bank, sums, first, end):
-            row, place = divmod(f, E // 2)
-            gate = gate2_all[:, row, place * C : (place + 1) * C].unsqueeze(1).to_broadcast([P, end - first, C])
-            nc.vector.tensor_tensor(sums[:, first:end, :], bank[:, first:end, :], gate, MULT)
+        gate2_all = w2_raw[0, 1][:, 0:2, H - T // 2 : H]
 
-        def scalar_move(target, source):
-            nc.scalar.activation(target, source, COPY)
+        def gate_sums(f, sums_bank, gated, blocks):
+            row, n = divmod(f, E // 2)
+            gate = gate2_all[:, row, n * C : (n + 1) * C].unsqueeze(1).to_broadcast([P, blocks.stop - blocks.start, C])
+            nc.vector.tensor_tensor(gated[:, blocks, :], sums_bank[:, blocks, :], gate, MULT)
 
-        def scatter_dc(move, f, b, sums):
-            move(dc[b][:].indirect(entries(list2, f * C, C)), sums[:, b, :])
+        def scatter_dc(move, f, b, gated):
+            move(dc[b][:].indirect(entries(list2, f * C, C)), gated[:, b, :])
 
-        low, high, whole = slice(0, 2), slice(2, BLOCKS), slice(0, P)
+        sums_banks = {}
         for f in range(E):
             for s in range(PASSES):
-                open_pass(f, s)
+                rounded[f, s] = ring.tile([P, H * PACK], BF16, name="rounded", align_bytes=MX_ALIGN)
+                w2_codes[f, s] = ring.tile([P, H], U32, name="w2_codes", align_bytes=MX_ALIGN)
+                w2_plane[f, s] = ring.tile([P, H], U8, name="w2_plane", align_bytes=MX_ALIGN)
             if f == 0:
-                round_w2(nc.scalar.copy, f, 0, low, whole)
-                round_w2(nc.scalar.copy, f, 0, high, whole)
-                quantise_w2(f, 0, 0, HALF)
-                quantise_w2(f, 0, HALF, H)
-                round_w2(nc.scalar.copy, f, 1, low, whole)
-                round_w2(nc.scalar.copy, f, 1, high, slice(SPLIT, P))
-                round_w2(nc.vector.tensor_copy, f, 1, high, slice(0, SPLIT))
-                for n, gate2_bank in enumerate(gate2_banks):
-                    spread = gate2_all[:, n, :].rearrange("p (r u) -> p r u", u=piece)
+                for blocks in (LOW, HIGH):
+                    round_w2(nc.scalar.copy, f, 0, blocks, ALL_PLACES)
+                for blocks in (LOW, HIGH):
+                    quantise_w2(f, 0, blocks)
+                round_w2(nc.scalar.copy, f, 1, LOW, ALL_PLACES)
+                round_w2(nc.scalar.copy, f, 1, HIGH, BACK)
+                round_w2(nc.vector.tensor_copy, f, 1, HIGH, FRONT)
+                for row, gate2_bank in enumerate(gate2_banks):
+                    spread = gate2_all[:, row, :].rearrange("p (r u) -> p r u", u=piece)
                     nc.scalar.copy(spread, gate2_bank[:, :, 0:piece])
             else:
-                round_w2(nc.scalar.copy, f, 0, high, slice(SPLIT, P))
-                round_w2(nc.vector.tensor_copy, f, 0, slice(0, BLOCKS), slice(0, SPLIT))
-                round_w2(nc.vector.tensor_copy, f, 0, low, slice(SPLIT, P))
-                sums = w2_raw[f, 0][:, :, 0:C]
-                gate_sums(f - 1, banks[f - 1], sums, 0, BLOCKS)
+                round_w2(nc.scalar.copy, f, 0, HIGH, BACK)
+                round_w2(nc.vector.tensor_copy, f, 0, ALL_BLOCKS, FRONT)
+                round_w2(nc.vector.tensor_copy, f, 0, LOW, BACK)
+                gated = w2_raw[f, 0][:, :, 0:C]
+                gate_sums(f - 1, sums_banks[f - 1], gated, ALL_BLOCKS)
                 for b in range(BLOCKS):
-                    scatter_dc(scalar_move, f - 1, b, sums)
-                quantise_w2(f, 0, 0, H)
-                round_w2(nc.vector.tensor_copy, f, 1, low, whole)
-                round_w2(nc.vector.tensor_copy, f, 1, high, whole)
-            quantise_w2(f, 1, 0, HALF)
-            quantise_w2(f, 1, HALF, H)
+                    scatter_dc(scalar_move, f - 1, b, gated)
+                quantise_w2(f, 0, ALL_BLOCKS)
+                for blocks in (LOW, HIGH):
+                    round_w2(nc.vector.tensor_copy, f, 1, blocks, ALL_PLACES)
+            for blocks in (LOW, HIGH):
+                quantise_w2(f, 1, blocks)
             if f < E - 1:
-                banks[f] = second_layer_products(f, 0, BLOCKS)
-        last_sums = keep.tile([P, BLOCKS, C], F32, name="last_sums")
-        for first in (0, 2):
-            gate_sums(E - 1, second_layer_products(E - 1, first, first + 2), last_sums, first, first + 2)
-        for b in range(BLOCKS):
-            scatter_dc(nc.vector.tensor_copy if b % 2 else scalar_move, E - 1, b, last_sums)
+                sums_banks[f] = second_layer_products(f, ALL_BLOCKS)
 
-        PAIR = 2 * C
-        slots = [keep.tile([P, BLOCKS, PAIR], F32, name="slots%d" % n) for n in range(E // 2)]
+        gated = keep.tile([P, BLOCKS, C], F32, name="last_gated")
+        for blocks in (LOW, HIGH):
+            gate_sums(E - 1, second_layer_products(E - 1, blocks), gated, blocks)
+        for b in range(BLOCKS):
+            scatter_dc(nc.vector.tensor_copy if b % 2 else scalar_move, E - 1, b, gated)
+
+        room = BLOCKS * PAIR
+        shared_room = keep.tile([P, 2 * room - C], F32, name="shared_room")
+        last_room = keep.tile([P, room], F32, name="last_room")
+        rooms = (shared_room[:, room - C :], shared_room[:, 0:room], last_room[:])
+        slots = [part.rearrange("p (t u) -> p t u", t=BLOCKS) for part in rooms]
+        da = [keep.tile([P, PAIR * PACK], BF16, name="da%d" % n, align_bytes=MX_ALIGN) for n in range(PAIRS)]
 
         def gather_dc(move, n, b):
             move(slots[n][:, b, :], dc[b][:].indirect(entries(list1, n * PAIR, PAIR)))
 
-        for n, b in ((0, 1), (0, 3), (1, 1), (1, 3)):
-            gather_dc(nc.vector.tensor_copy, n, b)
-        for n, b in ((0, 0), (0, 2), (1, 0), (1, 2), (2, 0), (2, 1), (2, 2), (2, 3)):
-            gather_dc(scalar_move, n, b)
-
-        da = [keep.tile([P, PAIR * PACK], BF16, name="da%d" % n, align_bytes=64) for n in range(E // 2)]
-
-        def round_da(n, c0, c1):
-            gate = gate1_all[:, n * PAIR + c0 : n * PAIR + c1].rearrange("p (c i) -> p c i", i=RUN)
+        def round_da(n, u0, u1):
+            gate = gate1_all[:, n * PAIR + u0 : n * PAIR + u1].rearrange("p (c i) -> p c i", i=RUN)
             nc.vector.tensor_tensor(
-                da[n][:, c0 * PACK : c1 * PACK].rearrange("p (c i t) -> p c t i", i=RUN, t=PACK),
-                slots[n][:, :, c0:c1].rearrange("p t (c i) -> p c t i", i=RUN),
-                gate.unsqueeze(2).to_broadcast([P, (c1 - c0) // RUN, PACK, RUN]),
+                da[n][:, u0 * PACK : u1 * PACK].rearrange("p (c i t) -> p c t i", i=RUN, t=PACK),
+                slots[n][:, :, u0:u1].rearrange("p t (c i) -> p c t i", i=RUN),
+                gate.unsqueeze(2).to_broadcast([P, (u1 - u0) // RUN, PACK, RUN]),
                 MULT,
             )
 
         def first_layer_products(n):
-            da_codes = keep.tile([P, PAIR], U32, name="da_codes%d" % n, align_bytes=64)
-            da_plane = keep.tile([P, PAIR], U8, name="da_plane%d" % n, align_bytes=64)
+            da_codes = keep.tile([P, PAIR], U32, name="da_codes%d" % n, align_bytes=MX_ALIGN)
+            da_plane = keep.tile([P, PAIR], U8, name="da_plane%d" % n, align_bytes=MX_ALIGN)
             nc.vector.quantize_mx(out=da_codes[:].bitcast(FP8X4), scales=da_plane[:], in_=da[n][:])
-            pair_banks = []
+            result_banks = [next_bank() for b in range(K_BLOCKS)]
             for b in range(K_BLOCKS):
-                bank = wide_bank()
-                for m in range(2):
-                    e = 2 * n + m
+                for half in range(2):
+                    e = 2 * n + half
                     nc.tensor.matmul_mx(
-                        out=bank[:, m, :],
+                        out=result_banks[b][:, half, :],
                         lhsT=w1_codes[:, e, 2 * P * b : 2 * P * (b + 1)].bitcast(FP4X4),
                         lhsT_scale=w1_plane[:, e, P * b : P * (b + 1)],
-                        rhs=da_codes[:, m * C : (m + 1) * C].bitcast(FP8X4),
-                        rhs_scale=da_plane[:, m * C : (m + 1) * C],
+                        rhs=da_codes[:, half * C : (half + 1) * C].bitcast(FP8X4),
+                        rhs_scale=da_plane[:, half * C : (half + 1) * C],
                         start=True,
                         stop=True,
                     )
-                pair_banks.append(bank)
-            return pair_banks
+            return result_banks
 
-        def empty(copy, n, b, bank):
+        for n, b in ((0, 1), (0, 3), (1, 1)):
+            gather_dc(nc.vector.tensor_copy, n, b)
+        for n in range(PAIRS):
+            for b in range(0, BLOCKS, 2 if n < PAIRS - 1 else 1):
+                gather_dc(scalar_move, n, b)
+        round_da(0, 0, C)
+        round_da(0, C, PAIR)
+        gather_dc(nc.vector.tensor_copy, 1, 3)
+        made = [first_layer_products(0)]
+        for n in range(1, PAIRS):
+            round_da(n, 0, PAIR)
+        made.extend(first_layer_products(n) for n in range(1, PAIRS))
+
+        def empty_bank(engine_copy, n, b):
             results = keep.tile([P, PAIR], F32, name="results%d_%d" % (n, b))
-            copy(results[:], bank[:, 0:2, :].rearrange("p m u -> p (m u)"))
+            engine_copy(results[:], made[n][b][:, 0:2, :].rearrange("p half u -> p (half u)"))
             return results
 
-        def scatter_dx(move, n, b, results):
-            move(dx[b][:].indirect(entries(list1, n * PAIR, PAIR)), results[:])
-
-        round_da(0, 0, PAIR)
-        made = [first_layer_products(0)]
-        round_da(1, 0, C)
-        round_da(1, C, PAIR)
-        round_da(2, 0, PAIR)
-        made.extend(first_layer_products(n) for n in range(1, E // 2))
-        results = {}
-        for group in ((0,), (1, 2)):
-            for n in group:
-                results[n, 1] = empty(nc.scalar.copy, n, 1, made[n][1])
-                results[n, 0] = empty(nc.vector.tensor_copy if n == 2 else nc.scalar.copy, n, 0, made[n][0])
-            for n in group:
-                scatter_dx(nc.vector.tensor_copy, n, 0, results[n, 0])
-                scatter_dx(scalar_move, n, 1, results[n, 1])
+        for pairs in (range(0, 1), range(1, PAIRS)):
+            results = {}
+            for n in pairs:
+                results[n, 1] = empty_bank(nc.scalar.copy, n, 1)
+                results[n, 0] = empty_bank(nc.vector.tensor_copy if n == PAIRS - 1 else nc.scalar.copy, n, 0)
+            for n in pairs:
+                for b, move in enumerate((nc.vector.tensor_copy, scalar_move)):
+                    move(dx[b][:].indirect(entries(list1, n * PAIR, PAIR)), results[n, b][:])
 
         nc.scalar.dma_start(out[P : 2 * P, :], dx[1][:])
         nc.sync.dma_start(out[0:P, :], dx[0][:])

@@ -78,13 +78,14 @@ def tile_moe_seb_none_kernel(
         def load_dy(s):
             nc.sync.dma_start(dy_codes[s][:], dy_words[s].rearrange("p t d -> p (t d)").bitcast(I32))
 
+        def load_dy_scales(s):
+            for q in range(QUADRANTS):
+                rows = dy_plane[32 * q + 4 * s : 32 * q + 4 * s + 4, :]
+                nc.sync.dma_start(rows.bitcast(I32), dy_scales[s, 4 * q : 4 * q + 4, :].bitcast(I32))
+
         load_dy(0)
         nc.sync.dma_start(list2[:], offs2)
-        for q in range(QUADRANTS):
-            nc.sync.dma_start(
-                dy_plane[32 * q : 32 * q + 4 * PASSES, :].bitcast(I32),
-                dy_scales[:, 4 * q : 4 * q + 4, :].bitcast(I32),
-            )
+        load_dy_scales(0)
         load_dy(1)
         piece = T // GATE2_ROWS
         w2_raw = {}
@@ -95,6 +96,7 @@ def tile_moe_seb_none_kernel(
                 nc.sync.dma_start(raw[:], rows.rearrange("(p j) i -> p j i", j=PACK))
                 w2_raw[f, s] = raw
                 if (f, s) == (0, 0):
+                    load_dy_scales(1)
                     nc.sync.dma_start(gate2_rows[0:GATE2_ROWS, 0:piece], gate2[0].rearrange("(r u) -> r u", u=piece))
         nc.sync.dma_start(list1[:], offs)
         nc.sync.dma_start(gate1_all[:], gate1)
@@ -124,9 +126,8 @@ def tile_moe_seb_none_kernel(
                 parts.extend(tile[:, n * C : (n + 1) * C] for n in range(E // 2))
             return parts
 
-        g_codes = [gather_dy(dy_codes[0][:].bitcast(U32), U32, "g_codes0")]
+        g_codes = [gather_dy(dy_codes[s][:].bitcast(U32), U32, "g_codes%d" % s) for s in range(PASSES)]
         g_plane = gather_dy(dy_plane[:], U8, "g_plane")
-        g_codes.append(gather_dy(dy_codes[1][:].bitcast(U32), U32, "g_codes1"))
 
         rounded, w2_codes, w2_plane = {}, {}, {}
 

from contextlib import ExitStack

import concourse.mybir as mybir
from concourse.masks import make_identity

K, T, E, C, H, N = 256, 768, 6, 128, 512, 1024
FLOPS = 2 * T * H * (N + K)

F32 = mybir.dt.float32
BF16 = mybir.dt.bfloat16
I32 = mybir.dt.int32
U32 = mybir.dt.uint32
U16 = mybir.dt.uint16
U8 = mybir.dt.uint8
FP8X4 = mybir.dt.float8_e4m3fn_x4
FP4X4 = mybir.dt.float4_e2m1fn_x4
COPY = mybir.ActivationFunctionType.Copy
MULT = mybir.AluOpType.mult

P = 128
PACK = 4
PASSES = N // (P * PACK)
BLOCKS = H // P
K_BLOCKS = K // P
PAIR = 2 * C
PAIRS = E // 2
QUADRANTS = 4
PER_COLUMN = 16
BANKS = 8
RUN = 4
DMA_ALIGN = 256
MX_ALIGN = 64
GATE2_ROWS = 8
RING_DEPTH = 2 * PASSES
SPLIT = 64

LOW, HIGH, ALL_BLOCKS = slice(0, 2), slice(2, BLOCKS), slice(0, BLOCKS)
FRONT, BACK, ALL_PLACES = slice(0, SPLIT), slice(SPLIT, P), slice(0, P)


def entries(offsets, first, count):
    return offsets[:, first // PER_COLUMN : (first + count) // PER_COLUMN]


def tile_moe_seb_none_kernel(
    tc, dy_words, dy_scales, w2t, w1t_words, w1t_scales, gate1, gate2, offs, offs2, out
):
    nc = tc.nc
    with ExitStack() as ctx:
        keep = ctx.enter_context(tc.tile_pool(name="keep", bufs=1))
        ring = ctx.enter_context(tc.tile_pool(name="ring", bufs=RING_DEPTH))
        psum = ctx.enter_context(tc.psum_pool(name="psum", bufs=BANKS))

        def next_bank():
            return psum.tile([P, BLOCKS, C], F32, name="bank")

        def scalar_move(target, source):
            nc.scalar.activation(target, source, COPY)

        list1 = keep.tile([P, T // PER_COLUMN], U16, name="list1")
        list2 = keep.tile([P, T // PER_COLUMN], U16, name="list2")
        dy_plane = keep.tile([P, T], U8, name="dy_plane", align_bytes=DMA_ALIGN)
        w1_plane = keep.tile([P, E, K], U8, name="w1_plane", align_bytes=DMA_ALIGN)
        w1_codes = keep.tile([P, E, 2 * K], U8, name="w1_codes", align_bytes=DMA_ALIGN)
        gate1_all = keep.tile([P, T], F32, name="gate1_all", align_bytes=DMA_ALIGN)
        gate2_rows = keep.tile([P, P], F32, name="gate2_rows")
        gate2_cols = keep.tile([P, GATE2_ROWS], F32, name="gate2_cols")
        identity = keep.tile([P, P], F32, name="identity")
        dy_codes = [keep.tile([P, T], I32, name="dy_codes%d" % s, align_bytes=DMA_ALIGN) for s in range(PASSES)]
        dc = [keep.tile([P, T], F32, name="dc%d" % b) for b in range(BLOCKS)]
        dx = [keep.tile([P, T], F32, name="dx%d" % b, align_bytes=DMA_ALIGN) for b in range(K_BLOCKS)]

        nc.vector.memset(gate2_rows[:], 0.0)
        nc.vector.memset(dy_plane[:].bitcast(I32), 0)
        make_identity(nc, identity[:])
        nc.gpsimd.memset(w1_plane[:].rearrange("p e k -> p (e k)").bitcast(I32), 0)

        def load_dy(s):
            nc.sync.dma_start(dy_codes[s][:], dy_words[s].rearrange("p t d -> p (t d)").bitcast(I32))

        def load_dy_scales(s):
            for q in range(QUADRANTS):
                rows = dy_plane[32 * q + 4 * s : 32 * q + 4 * s + 4, :]
                nc.sync.dma_start(rows.bitcast(I32), dy_scales[s, 4 * q : 4 * q + 4, :].bitcast(I32))

        load_dy(0)
        nc.sync.dma_start(list2[:], offs2)
        load_dy_scales(0)
        load_dy(1)
        piece = T // GATE2_ROWS
        w2_raw = {}
        for f in range(E):
            for s in range(PASSES):
                raw = keep.tile([P, PACK, H], F32, name="w2_raw%d_%d" % (f, s), align_bytes=DMA_ALIGN)
                rows = w2t[f, s * P * PACK : (s + 1) * P * PACK, :]
                nc.sync.dma_start(raw[:], rows.rearrange("(p j) i -> p j i", j=PACK))
                w2_raw[f, s] = raw
                if (f, s) == (0, 0):
                    load_dy_scales(1)
                    nc.sync.dma_start(gate2_rows[0:GATE2_ROWS, 0:piece], gate2[0].rearrange("(r u) -> r u", u=piece))
        nc.sync.dma_start(list1[:], offs)
        nc.sync.dma_start(gate1_all[:], gate1)
        nc.sync.dma_start(w1_codes[:].bitcast(I32), w1t_words[:, 0].rearrange("e p b -> p e b").bitcast(I32))
        for q in range(QUADRANTS):
            nc.sync.dma_start(
                w1_plane[32 * q : 32 * q + 4, :, :].bitcast(I32),
                w1t_scales[:, 0, 4 * q : 4 * q + 4, :].rearrange("e r k -> r e k").bitcast(I32),
            )

        bank = next_bank()
        nc.tensor.transpose(bank[:, 0, :], gate2_rows[:], identity[:])
        nc.scalar.copy(gate2_cols[:], bank[:, 0, 0:GATE2_ROWS])
        gate2_banks = []
        for first in range(0, GATE2_ROWS, BLOCKS):
            bank = next_bank()
            for n in range(BLOCKS):
                column = gate2_cols[:, first + n : first + n + 1]
                nc.tensor.transpose(bank[:, n, :], column.to_broadcast([P, P]), identity[:])
            gate2_banks.append(bank)

        def gather_dy(window, dtype, name):
            parts = []
            for first in (0, T // 2):
                tile = keep.tile([P, T // 2], dtype, name="%s_%d" % (name, first), align_bytes=MX_ALIGN)
                nc.vector.tensor_copy(tile[:], window.indirect(entries(list2, first, T // 2)))
                parts.extend(tile[:, n * C : (n + 1) * C] for n in range(E // 2))
            return parts

        g_codes = [gather_dy(dy_codes[s][:].bitcast(U32), U32, "g_codes%d" % s) for s in range(PASSES)]
        g_plane = gather_dy(dy_plane[:], U8, "g_plane")

        rounded, w2_codes, w2_plane = {}, {}, {}

        def round_w2(engine_copy, f, s, blocks, places):
            engine_copy(
                rounded[f, s][:].rearrange("p (t m j) -> p m j t", t=BLOCKS, j=PACK)[:, places, :, blocks],
                w2_raw[f, s][:].rearrange("p j (m t) -> p m j t", t=BLOCKS)[:, places, :, blocks],
            )

        def quantise_w2(f, s, blocks):
            cols = slice(blocks.start * P, blocks.stop * P)
            nc.vector.quantize_mx(
                out=w2_codes[f, s][:, cols].bitcast(FP8X4),
                scales=w2_plane[f, s][:, cols],
                in_=rounded[f, s][:, cols.start * PACK : cols.stop * PACK],
            )

        def second_layer_products(f, blocks):
            bank = next_bank()
            for s in range(PASSES):
                for b in range(blocks.start, blocks.stop):
                    cols = slice(b * P, (b + 1) * P)
                    nc.tensor.matmul_mx(
                        out=bank[:, b, :],
                        lhsT=w2_codes[f, s][:, cols].bitcast(FP8X4),
                        lhsT_scale=w2_plane[f, s][:, cols],
                        rhs=g_codes[s][f].bitcast(FP8X4),
                        rhs_scale=g_plane[f][4 * s : P, :],
                        start=(s, b) == (0, blocks.start),
                        stop=(s, b) == (PASSES - 1, blocks.stop - 1),
                    )
            return bank

        gate2_all = w2_raw[0, 1][:, 0:2, H - T // 2 : H]

        def gate_sums(f, sums_bank, gated, blocks):
            row, n = divmod(f, E // 2)
            gate = gate2_all[:, row, n * C : (n + 1) * C].unsqueeze(1).to_broadcast([P, blocks.stop - blocks.start, C])
            nc.vector.tensor_tensor(gated[:, blocks, :], sums_bank[:, blocks, :], gate, MULT)

        def scatter_dc(move, f, b, gated):
            move(dc[b][:].indirect(entries(list2, f * C, C)), gated[:, b, :])

        sums_banks = {}
        for f in range(E):
            for s in range(PASSES):
                rounded[f, s] = ring.tile([P, H * PACK], BF16, name="rounded", align_bytes=MX_ALIGN)
                w2_codes[f, s] = ring.tile([P, H], U32, name="w2_codes", align_bytes=MX_ALIGN)
                w2_plane[f, s] = ring.tile([P, H], U8, name="w2_plane", align_bytes=MX_ALIGN)
            if f == 0:
                for blocks in (LOW, HIGH):
                    round_w2(nc.scalar.copy, f, 0, blocks, ALL_PLACES)
                for blocks in (LOW, HIGH):
                    quantise_w2(f, 0, blocks)
                round_w2(nc.scalar.copy, f, 1, LOW, ALL_PLACES)
                round_w2(nc.scalar.copy, f, 1, HIGH, BACK)
                round_w2(nc.vector.tensor_copy, f, 1, HIGH, FRONT)
                for row, gate2_bank in enumerate(gate2_banks):
                    spread = gate2_all[:, row, :].rearrange("p (r u) -> p r u", u=piece)
                    nc.scalar.copy(spread, gate2_bank[:, :, 0:piece])
            else:
                round_w2(nc.scalar.copy, f, 0, HIGH, BACK)
                round_w2(nc.vector.tensor_copy, f, 0, ALL_BLOCKS, FRONT)
                round_w2(nc.vector.tensor_copy, f, 0, LOW, BACK)
                gated = w2_raw[f, 0][:, :, 0:C]
                gate_sums(f - 1, sums_banks[f - 1], gated, ALL_BLOCKS)
                for b in range(BLOCKS):
                    scatter_dc(scalar_move, f - 1, b, gated)
                quantise_w2(f, 0, ALL_BLOCKS)
                for blocks in (LOW, HIGH):
                    round_w2(nc.vector.tensor_copy, f, 1, blocks, ALL_PLACES)
            for blocks in (LOW, HIGH):
                quantise_w2(f, 1, blocks)
            if f < E - 1:
                sums_banks[f] = second_layer_products(f, ALL_BLOCKS)

        gated = keep.tile([P, BLOCKS, C], F32, name="last_gated")
        for blocks in (LOW, HIGH):
            gate_sums(E - 1, second_layer_products(E - 1, blocks), gated, blocks)
        for b in range(BLOCKS):
            scatter_dc(nc.vector.tensor_copy if b % 2 else scalar_move, E - 1, b, gated)

        room = BLOCKS * PAIR
        shared_room = keep.tile([P, 2 * room - C], F32, name="shared_room")
        last_room = keep.tile([P, room], F32, name="last_room")
        rooms = (shared_room[:, room - C :], shared_room[:, 0:room], last_room[:])
        slots = [part.rearrange("p (t u) -> p t u", t=BLOCKS) for part in rooms]
        da = [keep.tile([P, PAIR * PACK], BF16, name="da%d" % n, align_bytes=MX_ALIGN) for n in range(PAIRS)]

        def gather_dc(move, n, b):
            move(slots[n][:, b, :], dc[b][:].indirect(entries(list1, n * PAIR, PAIR)))

        def round_da(n, u0, u1):
            gate = gate1_all[:, n * PAIR + u0 : n * PAIR + u1].rearrange("p (c i) -> p c i", i=RUN)
            nc.vector.tensor_tensor(
                da[n][:, u0 * PACK : u1 * PACK].rearrange("p (c i t) -> p c t i", i=RUN, t=PACK),
                slots[n][:, :, u0:u1].rearrange("p t (c i) -> p c t i", i=RUN),
                gate.unsqueeze(2).to_broadcast([P, (u1 - u0) // RUN, PACK, RUN]),
                MULT,
            )

        def first_layer_products(n):
            da_codes = keep.tile([P, PAIR], U32, name="da_codes%d" % n, align_bytes=MX_ALIGN)
            da_plane = keep.tile([P, PAIR], U8, name="da_plane%d" % n, align_bytes=MX_ALIGN)
            nc.vector.quantize_mx(out=da_codes[:].bitcast(FP8X4), scales=da_plane[:], in_=da[n][:])
            result_banks = [next_bank() for b in range(K_BLOCKS)]
            for b in range(K_BLOCKS):
                for half in range(2):
                    e = 2 * n + half
                    nc.tensor.matmul_mx(
                        out=result_banks[b][:, half, :],
                        lhsT=w1_codes[:, e, 2 * P * b : 2 * P * (b + 1)].bitcast(FP4X4),
                        lhsT_scale=w1_plane[:, e, P * b : P * (b + 1)],
                        rhs=da_codes[:, half * C : (half + 1) * C].bitcast(FP8X4),
                        rhs_scale=da_plane[:, half * C : (half + 1) * C],
                        start=True,
                        stop=True,
                    )
            return result_banks

        for n, b in ((0, 1), (0, 3), (1, 1)):
            gather_dc(nc.vector.tensor_copy, n, b)
        for n in range(PAIRS):
            for b in range(0, BLOCKS, 2 if n < PAIRS - 1 else 1):
                gather_dc(scalar_move, n, b)
        round_da(0, 0, C)
        round_da(0, C, PAIR)
        gather_dc(nc.vector.tensor_copy, 1, 3)
        made = [first_layer_products(0)]
        for n in range(1, PAIRS):
            round_da(n, 0, PAIR)
        made.extend(first_layer_products(n) for n in range(1, PAIRS))

        def empty_bank(engine_copy, n, b):
            results = keep.tile([P, PAIR], F32, name="results%d_%d" % (n, b))
            engine_copy(results[:], made[n][b][:, 0:2, :].rearrange("p half u -> p (half u)"))
            return results

        for pairs in (range(0, 1), range(1, PAIRS)):
            results = {}
            for n in pairs:
                results[n, 1] = empty_bank(nc.scalar.copy, n, 1)
                results[n, 0] = empty_bank(nc.vector.tensor_copy if n == PAIRS - 1 else nc.scalar.copy, n, 0)
            for n in pairs:
                for b, move in enumerate((nc.vector.tensor_copy, scalar_move)):
                    move(dx[b][:].indirect(entries(list1, n * PAIR, PAIR)), results[n, b][:])

        nc.scalar.dma_start(out[P : 2 * P, :], dx[1][:])
        nc.sync.dma_start(out[0:P, :], dx[0][:])
